import numpy as np, ml_dtypes
CORES = [9,25,41,57]
N = 4
BF = ml_dtypes.bfloat16
def gentries(a):
    return np.ascontiguousarray(a.reshape(8, 16, -1).transpose(0, 2, 1)).reshape(8, -1)
def gtable(e):
    e = np.asarray(e); return np.ascontiguousarray(e.reshape(8, -1, 16).transpose(0, 2, 1)).reshape(128, -1).astype(np.int32)
V, H, PP, RO, S = 4096, 16384, 256, 3, 1
TH = 6
def slot(y, w1, w2):
    u1 = np.sum(y * w1[..., None], axis=-2) & 4095; u2 = np.sum(y * w2[..., None], axis=-2) & 4095
    return (((u1 * u2) >> 5) + u2) & (H - 1)
def keys(y):
    return np.ascontiguousarray((y & 255).astype(np.uint8).T).view("S16").reshape(-1)
def index(y):
    k = keys(y); o = np.argsort(k); return k[o], o
def find(ix, q):
    ks, o = ix; kq = keys(q); pos = np.minimum(np.searchsorted(ks, kq), len(ks) - 1)
    return np.where(ks[pos] == kq, o[pos], -1)
def weights(rng):
    return rng.integers(0, 16, (N, 8, 16)), rng.integers(0, 16, (N, 8, 16))
def themes(rng):
    return rng.integers(-6, 7, (8, TH, 16)) * (rng.random((8, TH, 16)) < 0.6)
def choose(rng, w1, w2, cand, bare=False):
    c = np.concatenate([cand[:, np.all((cand >= 0) & (cand <= 127), axis=0)], rng.integers(0, 128, (16, 2 * H))], axis=1)
    h = slot(c, w1, w2)
    if bare: c, h = c[:, h > 0], h[h > 0]
    i = np.sort(np.unique(h, return_index=True)[1])[:V]
    return c[:, rng.permutation(i)]
def song(rng, w1, w2, D, top=None, first=None, alpha=None, off=None, bare=()):
    if top is None: top = np.full((8, 16, 1), 128)
    if first is None: first = np.zeros((8, 16, 0), np.int64)
    if off is None: off = np.zeros((8, 16, 1), np.int64)
    al = np.full(TH, 3.0) if alpha is None else np.asarray(alpha, float)
    y = np.zeros((N, 8, 16, V), np.int64)
    for g in range(8):
        p = np.append(0.7 * rng.dirichlet(al), 0.3); E = np.ascontiguousarray(D[g].T); M = off.shape[2]
        for k in range(N):
            r = k * S % N; img = np.zeros((16, 0), np.int64)
            if k > 0:
                s = rng.choice(TH + 1, V, p=p); m = np.flatnonzero(s < TH)
                img = y[(r - S) % N, g][:, m] + E[:, s[m]] + off[g][:, rng.integers(0, M, len(m))]
            if k == N - 1:
                s = rng.choice(TH + 1, V, p=p); m = np.flatnonzero(s < TH)
                img = np.concatenate([img, y[0, g][:, m] - E[:, s[m]] + off[g][:, rng.integers(0, M, len(m))]], axis=1)
                img = img[:, rng.permutation(img.shape[1])]
            y[r, g] = choose(rng, w1[r, g], w2[r, g], np.concatenate([first[g], img, rng.integers(0, top[g], (16, V))], axis=1), g in bare)
    return y, [[index(y[r, g]) for g in range(8)] for r in range(N)]
def hits(y, ix, r, g, d):
    b = find(ix[r][g], y[(r - S) % N, g] + d[:, None]); a = np.flatnonzero(b >= 0)
    return a, b[a]
def main(y, ix, D, g):
    return int(np.argmax([sum(len(hits(y, ix, r, g, D[g, k])[0]) for r in range(N)) for k in range(TH)]))
def pick(rng, y, ix, r, g, d, n):
    a, b = hits(y, ix, r, g, d)
    if len(a) == 0: return rng.integers(0, V, (2, n))
    i = rng.integers(0, len(a), n); return np.stack([a[i], b[i]])
def pairs(rng, y, ix, D):
    pr = np.zeros((N, 8, 2, PP), np.int64); n = PP // 16
    for r in range(N):
        for g in range(8):
            o = rng.permutation(TH)
            tail = np.concatenate([pick(rng, y, ix, r, g, D[g, k], n) for k in o[2:]] + [rng.integers(0, V, (2, 4 * n))], axis=1)
            pr[r, g] = np.concatenate([pick(rng, y, ix, r, g, D[g, o[0]], 4 * n), pick(rng, y, ix, r, g, D[g, o[1]], 4 * n), tail[:, rng.permutation(8 * n)]], axis=1)
    return pr
def race(rng, w1, w2, y, ix, g):
    E = rng.integers(-2, 3, (N, 16))
    for k in range(N):
        r = k * S % N; img = np.zeros((16, 0), np.int64)
        if k > 0:
            img = y[(r - S) % N, g][:, rng.permutation(V)] + E[r][:, None]; img = img[:, np.all((img >= 0) & (img <= 127), axis=0)]
            img = img[:, np.sort(np.unique(slot(img, w1[r, g], w2[r, g]), return_index=True)[1])[:V // 4 + int(r == N - 1)]]
        y[r, g] = choose(rng, w1[r, g], w2[r, g], img); ix[r][g] = index(y[r, g])
    return E
def pack(y, w1, w2, pr):
    return {"x": np.ascontiguousarray(y.reshape(N, 128, V)).astype(np.int32), "w1": w1.reshape(N, 128, 1).astype(np.int32), "w2": w2.reshape(N, 128, 1).astype(np.int32),
            "pa": np.stack([gtable(a[:, 0]) for a in pr]), "pb": np.stack([gtable(a[:, 1]) for a in pr])}
def setup_inputs(rng):
    w1, w2 = weights(rng); D = themes(rng); y, ix = song(rng, w1, w2, D); pr = pairs(rng, y, ix, D)
    g, h = rng.permutation(8)[:2]; m = main(y, ix, D, g)
    for r in range(N): pr[r, g] = pick(rng, y, ix, r, g, D[g, m], PP)
    q = int(rng.integers(0, N)); pr[q, h] = pick(rng, y, ix, q, h, D[h, main(y, ix, D, h)], PP)
    return pack(y, w1, w2, pr)
def setup_inputs_ties(rng):
    w1, w2 = weights(rng); D = themes(rng); y, ix = song(rng, w1, w2, D); E = race(rng, w1, w2, y, ix, 6); pr = pairs(rng, y, ix, D)
    one = np.repeat(np.array([[V - 1], [0]]), PP, axis=1)
    for g in range(8):
        m = main(y, ix, D, g)
        for r in range(N):
            if g % 4 == 0 or (g % 4 == 3 and r == 0): pr[r, g] = one
            elif g % 4 != 2: pr[r, g] = pick(rng, y, ix, r, g, D[g, m], PP)
    pr[0, 6] = rng.integers(0, V, (2, PP))
    for r in range(1, N): pr[r, 6] = pick(rng, y, ix, r, 6, E[r], PP)
    return pack(y, w1, w2, pr)
def setup_inputs_near(rng):
    w1, w2 = weights(rng); D = themes(rng); off = np.zeros((8, 16, 10), np.int64); c = np.arange(8) % 4
    for g in range(8):
        i, j, z = 2 * g, 2 * g + 1, min(2 * g, 12)
        w1[:, g, z:z + 4] = 0; w2[:, g, z:z + 4] = 0
        off[g, i, 4] = 1; off[g, j, 5] = -1; off[g, i, 6] = 1; off[g, j, 6] = -1; off[g, j, 7] = 2
        off[g, z:z + 4, 8] = np.array([1, -3, 3, -1]); off[g, z:z + 4, 9] = np.array([-1, 3, -3, 1])
    D[:, 0] = -(1 + c)[:, None]; D[4, 0] = 1
    first = np.tile(np.stack([c, 1 + c, 127 + 0 * c], axis=1)[:, None, :], (1, 16, 1))
    y, ix = song(rng, w1, w2, D, first=first, alpha=[9, 3, 3, 3, 3, 3], off=off, bare=(2, 6)); pr = pairs(rng, y, ix, D)
    for g in range(8):
        for r in range(N):
            if g % 2 == 0 or r == 0: pr[r, g, :, :PP // 2] = pick(rng, y, ix, r, g, D[g, 0], PP // 2)
    return pack(y, w1, w2, pr)
def setup_inputs_same(rng):
    w1, w2 = weights(rng); D = themes(rng); D[::2, 0] = 0; D[1, 0] = 0; D[:, 2] = -D[:, 1]
    w1[:, 1] = w1[0, 1].copy(); w2[:, 1] = w2[0, 1].copy()
    first = [rng.integers(0, 128, (16, 64)) for g in range(8)]; first[1] = choose(rng, w1[0, 1], w2[0, 1], first[1])[:, :7 * V // 8]
    y, ix = song(rng, w1, w2, D, first=first, alpha=[6, 3, 3, 3, 3, 3]); pr = pairs(rng, y, ix, D)
    for g in (0, 1, 2, 4, 6):
        for r in range(0, N, 2): pr[r, g, :, :PP // 4] = pick(rng, y, ix, r, g, D[g, 0], PP // 4)
    return pack(y, w1, w2, pr)
def setup_inputs_late(rng):
    w1, w2 = weights(rng); D = themes(rng); y, ix = song(rng, w1, w2, D); pr = np.zeros((N, 8, 2, PP), np.int64)
    for g in range(8):
        m = main(y, ix, D, g); dead = np.zeros((N, V), bool)
        for r in range(N):
            a, b = hits(y, ix, r, g, D[g, m]); dead[(r - S) % N, a] = True; dead[r, b] = True
        for r in range(N):
            c = (r - S) % N; fa = np.flatnonzero(~dead[c]); fb = np.flatnonzero(~dead[r])
            if len(fa) == 0: fa = np.array([0])
            if len(fb) == 0: fb = np.array([0])
            q = pick(rng, y, ix, r, g, D[g, m], PP - 1)
            if g % 2 == 1:
                z = rng.random(PP - 1) < 0.5; late = np.arange(PP - 1) > 0
                q = np.stack([np.where(z & late, rng.choice(fa, PP - 1), q[0]), np.where(~z & late, rng.choice(fb, PP - 1), q[1])])
            ca, cb = hits(y, ix, r, g, D[g, (m + 1 + (r + g) % (TH - 1)) % TH]); ok = ~dead[c, ca] & ~dead[r, cb]; ca, cb = ca[ok], cb[ok]
            if len(ca) == 0: ca, cb = fa[:1], fb[:1]
            j = int(rng.integers(0, len(ca)))
            pr[r, g] = np.concatenate([q, np.array([[ca[j]], [cb[j]]])], axis=1)
    return pack(y, w1, w2, pr)
def setup_inputs_spread(rng):
    ws = np.array([0, 1, 2, 7, 15]); w1 = rng.choice(ws, (N, 8, 16)); w2 = rng.choice(ws, (N, 8, 16))
    top = 2 ** rng.integers(1, 8, (8, 16, 1)); top[:, ::5] = 128
    D = rng.integers(-1, 2, (8, TH, 16)) * 2 ** rng.integers(0, 6, (8, TH, 16)) * (rng.random((8, TH, 16)) < 0.5)
    D = np.where(top.reshape(8, 1, 16) < 128, np.abs(D), D)
    e = int(rng.integers(0, 8)); top[e, 1] = 1; D[e, :, 1] = 0; D[e, 0] = 0; D[e, 0, 1] = 127; D[e, 1, 1] = -127
    y, ix = song(rng, w1, w2, D, top=top); pr = pairs(rng, y, ix, D)
    for r in range(N): pr[r, e, :, :PP // 2] = pick(rng, y, ix, r, e, D[e, 0], PP // 2)
    return pack(y, w1, w2, pr)
def check_inputs(d):
    bad = []
    for k, hi in (("x", 127), ("w1", 15), ("w2", 15), ("pa", V - 1), ("pb", V - 1)):
        if np.min(d[k]) < 0 or np.max(d[k]) > hi: bad.append("range of " + k)
    h = np.sort(slot(d["x"].astype(np.int64).reshape(N, 8, 16, V), d["w1"].astype(np.int64).reshape(N, 8, 16), d["w2"].astype(np.int64).reshape(N, 8, 16)), axis=-1)
    if np.any(h[..., 1:] == h[..., :-1]): bad.append("two notes of a rank and group have one slot number")
    return bad
def reference(x, w1, w2, pa, pb):
    y = x.astype(np.int64).reshape(N, 8, 16, V)
    la = np.stack([gentries(a) for a in pa]).astype(np.int64); lb = np.stack([gentries(a) for a in pb]).astype(np.int64)
    ix = [[index(y[r, g]) for g in range(8)] for r in range(N)]
    cov = np.zeros((N, 8, V), np.int64); win = np.zeros((8, 2 * RO), np.int64)
    for t in range(RO):
        new = cov + 0
        for g in range(8):
            best, top, won = -1, -1, []
            for d in range(N):
                c = (d - S) % N
                free = np.flatnonzero((cov[c, g][la[d, g]] == 0) & (cov[d, g][lb[d, g]] == 0))
                if len(free) == 0: continue
                k = int(free[0]); D = y[d, g][:, lb[d, g, k]] - y[c, g][:, la[d, g, k]]
                fit = []
                for r in range(N):
                    e = (r - S) % N; b = find(ix[r][g], y[e, g] + D[:, None])
                    p = np.flatnonzero((b >= 0) & (cov[e, g] == 0) & (cov[r, g][np.maximum(b, 0)] == 0))
                    fit.append((p, b[p]))
                n = sum(len(p) for p, b in fit)
                if n > top: best, top, won = d, n, fit
            win[g, t] = best; win[g, RO + t] = top
            for r in range(len(won)):
                p, b = won[r]; new[(r - S) % N, g, p] = t + 1; new[r, g, b] = t + 1
        cov = new
    return {"yc": cov.astype(np.float32), "yw": np.stack([win] * N).astype(np.float32)}

@@ -1,0 +1,566 @@
+from concourse.bass import DstId, RemoteDMATransfer
+from concourse.mybir import AluOpType as ALU, AxisListType as AX, ActivationFunctionType as AF
+
+V, H, RO = 4096, 16384, 3
+HT = H + V
+BIG = 32768.0
+ONE = 65793.0
+NONE = -512.0
+KB = 192.0 + 2.0 ** -13
+CELLS = [(c, b, max(6 * c - 16 * b, 0), min(6 * c + 6 - 16 * b, 16)) for b in range(3) for c in range(8)
+         if 6 * c < 16 * b + 16 and 6 * c + 6 > 16 * b]
+NC = len(CELLS)
+AT = ((0, 256, 512), (1024, 1280, 768))
+
+f32, bf, i32, u16, f16 = "float32", "bfloat16", "int32", "uint16", "float16"
+S_ = {
+    "tab": (HT + V, f32), "xi": (V, i32), "xb": (V, bf), "xp": (V, bf), "xq": (V, bf), "xf": (V, f32),
+    "ga0": (2048, bf), "ga1": (2048, bf), "gb0": (2048, bf), "gb1": (2048, bf),
+    "na0": (768, bf), "na1": (768, bf), "nb0": (768, bf), "nb1": (768, bf),
+    "pkp": (1024, f32), "pkq": (768, f32), "so": (8, u16), "up": (512, f16), "uq": (512, f16),
+    "kk": (2048, bf), "ndb": (1024, bf), "elv": (512, bf), "m4k": (128, bf), "cid": (128, bf), "idh": (128, f16),
+    "dmy": (256, f32), "kd": (256, f32), "km": (256, f32), "kl": (256, f32),
+    "ix": (1024, u16), "ixr": (256, u16), "ixo": (256, u16), "slp": (256, i32),
+    "wi": (8, i32), "wf": (8, f32), "pab": (32, i32), "pt": (32, i32), "po": (32, u16), "ph": (32, u16), "pl": (32, u16),
+    "ri": (144, f32), "rg": (128, f32), "i1": (4, i32), "j1": (8, i32), "cf": (8, f32), "cg": (8, f32), "ce": (8, f32),
+    "tci": (4, i32), "tcf": (4, f32),
+    "w1s": (144, bf), "w2s": (144, bf), "w1b": (128, bf), "w2b": (128, bf), "bon": (128, bf), "bow": (128, f32),
+    "idn": (128, bf), "fa": (128, bf), "fb": (128, bf), "fc": (128, bf), "fm": (128, bf), "gs": (432, bf),
+    "em": (16, bf), "mk": (512, bf), "kr": (256, bf), "i16": (16, f32), "tie": (4, f32),
+    "xbb": (256, bf), "dd": (272, bf), "pg": (1024, bf), "nm": (2, f32), "ko": (2, u16),
+    "ofl": (192, bf), "q": (512, f32), "qf": (24, f32), "qw": (16, f32), "ndf": (4, f32), "cl": (48, f32),
+    "mx": (4, f32), "wz": (24, i32), "wy": (8, i32), "fo": (16, u16),
+    "ft": (1024, bf), "fs": (1536, bf), "it": (768, bf), "il": (1536, bf), "pre": (512, bf), "ind": (1024, bf),
+    "ya": (256, f32), "yb": (256, f32), "yd": (256, f32), "yo": (256, f32), "yt": (16, f32), "yi": (8, i32), "yws": (8, f32),
+}
+ALIAS = {"ta": 0, "tb": 1024, "tm": 2048, "tn": 2560, "sp": 3072}
+SCRATCH = {k: ("sbuf", [128, v[0]], v[1]) for k, v in S_.items()}
+SCRATCH["f3"] = ("sbuf", [128, 8, 16], bf)
+SCRATCH["mm"] = ("sbuf", [128, 8 * (NC + 2), 16], bf)
+for k_, n_ in (("psA", 1536), ("psB", 1536), ("psS0", 512), ("psS1", 512)):
+    SCRATCH[k_] = ("psum", [128, n_], f32)
+
+SEMAPHORES = (["cv", "ca", "cp", "cg", "sent", "ldw", "ldp", "st", "xq", "xq3"] + ["ld%d" % c for c in range(4)]
+              + ["xp%d" % c for c in range(4)] + ["h%d" % c for c in range(3)]
+              + [s + str(t) for s in ("of", "cn", "ff", "fi") for t in range(RO)])
+
+
+def helper_of(c, T, topo):
+    n = len(T.cores)
+    r = T.rank_of(c)
+    return [h for h in topo.cores_of(c) if topo.die(h) != topo.die(c) and T.rank_of(h) is None
+            and topo.may_write(h, T.cores[(r + 1) % n]) and topo.may_write(h, T.cores[(r - 1) % n])][0]
+
+
+def count(mask):
+    return bin(mask).count("1")
+
+
+def dst(c, topo):
+    rid, pid, _ = topo.addr(c)
+    return DstId(rid=rid, pnc=pid)
+
+
+def helper_program(g, core, owner, T, topo):
+    n = len(T.cores)
+    r = T.rank_of(owner)
+    succ, pred = T.cores[(r + 1) % n], T.cores[(r - 1) % n]
+    k = count(topo.mask(owner, core) & ~topo.mask(owner, succ))
+    total = 0
+    for c in (0, 2):
+        g.wait_ge(T.sem["h%d" % c], k)
+        rid, pid, _ = topo.addr(succ)
+        m = topo.mask(core, succ)
+        g.remote_dma(T.xp[:, 1024 * c:1024 * c + 1024], T.xb[:, 1024 * c:1024 * c + 1024], T.sem["xp%d" % c],
+                     T.sem.sent, pid, rid, m)
+        total += count(m)
+    g.wait_ge(T.sem.h1, k)
+    rid, pid, _ = topo.addr(pred)
+    m = topo.mask(core, pred)
+    g.remote_dma(T.xq[:, 0:3072], T.xb[:, 0:3072], T.sem.xq, T.sem.sent, pid, rid, m)
+    g.wait_ge(T.sem.sent, total + count(m))
+
+
+def rank_program(g, core, T, topo):
+    rank = T.rank_of(core)
+    if rank is None:
+        for c in T.cores:
+            if helper_of(c, T, topo) == core:
+                helper_program(g, core, c, T, topo)
+        return
+    n = len(T.cores)
+    succ, pred, far = T.cores[(rank + 1) % n], T.cores[(rank - 1) % n], T.cores[(rank + 2) % n]
+    others = [T.cores[(rank + j) % n] for j in range(1, n)]
+    helper = helper_of(core, T, topo)
+    off = topo.mask(core, succ)
+    for c in others:
+        off &= topo.mask(core, c)
+    near = topo.mask(core, helper) & ~topo.mask(core, succ)
+
+    Q = {"v": g.vector, "a": g.scalar, "p": g.tensor, "g": g, "s": g.sync}
+    cnt = {"v": 0, "a": 0, "p": 0, "g": 0}
+    seen = {k: {} for k in Q}
+    log = {}
+    sent = [0]
+
+    def R(name, a=0, b=None, s=1):
+        if name in ALIAS:
+            name, a, b = "xi", ALIAS[name] + a, ALIAS[name] + b
+        t = T[name]
+        b = t.shape[1] if b is None else b
+        lo, hi = (a // 512 * 512, (b + 511) // 512 * 512) if name.startswith("ps") else (a, b)
+        return (t[:, a:b:s] if s != 1 else t[:, a:b], [(name, lo, hi)])
+
+    def C(name, a):
+        return R(name, a, a + 1)
+
+    def ind(win, offs):
+        return (win[0].indirect(offs[0]), win[1] + offs[1])
+
+    def wait(q, sem, val):
+        if seen[q].get(sem, 0) < val:
+            Q[q].wait_ge(T.sem[sem], val)
+            seen[q][sem] = val
+
+    def order(q, reads, writes):
+        need = {}
+        for regs, w in ((reads, False), (writes, True)):
+            for name, lo, hi in regs:
+                ps = name.startswith("ps")
+                for a, b, ew, tok in log.get(name, []):
+                    if a < hi and lo < b and (w or ew or (ps and tok[2] != q)) and not (q == "p" and tok[2] == "p"):
+                        need[tok[0]] = max(need.get(tok[0], 0), tok[1])
+        for sem, val in need.items():
+            wait(q, sem, val)
+
+    def note(reads, writes, tok):
+        for name, lo, hi in writes:
+            log[name] = [e for e in log.get(name, []) if not (lo <= e[0] and e[1] <= hi)] + [(lo, hi, True, tok)]
+        for name, lo, hi in reads:
+            log[name] = [e for e in log.get(name, []) if not (not e[2] and e[3][0] == tok[0] and lo <= e[0] and e[1] <= hi)]
+            log[name].append((lo, hi, False, tok))
+
+    def op(q, call, outs, ins):
+        reads = [r for x in ins if isinstance(x, tuple) for r in x[1]]
+        writes = [r for x in outs for r in x[1]]
+        order(q, reads, writes)
+        cnt[q] += 1
+        call().then_inc(T.sem["c" + q], 1)
+        note(reads, writes, ("c" + q, cnt[q], q))
+
+    def ap(x):
+        return x[0] if isinstance(x, tuple) else x
+
+    def cp(out, a):
+        op("v", lambda: g.vector.tensor_copy(out[0], a[0]), [out], [a])
+
+    def tt(out, a, b, o):
+        op("v", lambda: g.vector.tensor_tensor(out[0], a[0], b[0], o), [out], [a, b])
+
+    def ts(out, a, s1, o1, s2=None, o2=None):
+        if o2 is None:
+            op("v", lambda: g.vector.tensor_scalar(out[0], a[0], ap(s1), None, o1), [out], [a, s1])
+        else:
+            op("v", lambda: g.vector.tensor_scalar(out[0], a[0], ap(s1), ap(s2), o1, o2), [out], [a, s1, s2])
+
+    def ms(out, val):
+        op("v", lambda: g.vector.memset(out[0], val), [out], [])
+
+    def red(out, a, o, neg=False):
+        op("v", lambda: g.vector.tensor_reduce(out[0], a[0], AX.X, o, negate=neg), [out], [a])
+
+    def act(out, a, f, bias=0.0, scale=1.0, acc=None):
+        if acc is None:
+            op("a", lambda: g.scalar.activation(out[0], a[0], f, ap(bias), scale), [out], [a, bias])
+        else:
+            op("a", lambda: g.scalar.activation(out[0], a[0], f, ap(bias), scale, accum_out=acc[0]), [out, acc], [a, bias])
+
+    def scatter(win, offs, src):
+        op("a", lambda: g.scalar.activation(win[0].indirect(offs[0]), src[0], AF.Silu), [win], [offs, src])
+
+    def mm(out, l, r, start, stop):
+        op("p", lambda: g.tensor.matmul(out[0], l[0], r[0], start, stop), [out], [l, r])
+
+    def iota(out, pat, base, cm, loose=False):
+        if loose:
+            op("g", lambda: g.iota(out[0], pat, base, cm, allow_small_or_imprecise_dtypes=True), [out], [])
+        else:
+            op("g", lambda: g.iota(out[0], pat, base, cm), [out], [])
+
+    def load(q, out, src, sem, total):
+        Q[q].dma_start(out[0], src).then_inc(T.sem[sem], 16)
+        note([], out[1], (sem, total, "dma"))
+
+    def lands(reg, sem, total):
+        note([], reg[1], (sem, total, "far"))
+
+    def send(src, parts):
+        order("g", src[1], [])
+        g.remote_dma_fused([RemoteDMATransfer(dst_ids=[dst(c, topo) for c, _ in to], dma_engine_mask=m,
+                                              remote_sem=T.sem[sem], srcs=[src[0]], dsts=[d[0] for _, d in to])
+                            for m, sem, to in parts], local_sem=T.sem.sent)
+        sent[0] += sum(count(m) for m, _, _ in parts)
+
+    ke = count(off)
+    for c in range(4):
+        via = helper_of(pred, T, topo) if c in (0, 2) else pred
+        lands(R("xp", 1024 * c, 1024 * c + 1024), "xp%d" % c, count(topo.mask(via, core)))
+    lands(R("xq", 0, 3072), "xq", count(topo.mask(helper_of(succ, T, topo), core)))
+    lands(R("xq", 3072, V), "xq3", ke)
+
+    for c in range(4):
+        load("s", R("xi", 1024 * c, 1024 * c + 1024), T.x[:, 1024 * c:1024 * c + 1024], "ld%d" % c, 16)
+    load("a", R("wi", 0, 1), T.w1[:], "ldw", 32)
+    load("a", R("wi", 1, 2), T.w2[:], "ldw", 32)
+    load("a", R("pab", 0, 16), T.pb[:], "ldp", 32)
+    load("a", R("pab", 16, 32), T.pa[:], "ldp", 32)
+
+    ms(R("tab", 0, 512), 0.0)
+    ms(R("tab", 512, 2048), 0.0)
+    iota(R("ri"), [[1, 144]], 0, 0, True)
+    iota(R("i1", 0, 3), [[-11, 3]], 33, 11)
+    iota(R("i1", 3, 4), [[0, 1]], 0, 1)
+    iota(R("rg"), [[16, 8], [0, 16]], 0, 0, True)
+    fill = [2048]
+
+    def zero(q, w):
+        a = fill[0]
+        fill[0] += w
+        if q == "g":
+            iota(R("tab", a, a + w), [[0, w]], 0, 0, True)
+        elif q == "v":
+            ms(R("tab", a, a + w), 0.0)
+        else:
+            act(R("tab", a, a + w), R("tab", 0, w), AF.Identity)
+
+    zero("g", 2048)
+    for w in (512, 512, 512, 2048, 2048, 2048, 2048):
+        zero("a", w)
+    ts(R("j1", 0, 4), R("i1"), 15, ALU.bitwise_and)
+    ts(R("j1", 4, 5), R("i1", 3, 4), 112, ALU.bitwise_and)
+    cp(R("cf", 0, 5), R("j1", 0, 5))
+    pm, g16, me = C("cf", 3), C("cf", 4), C("cg", 3)
+    ts(C("ce", 0), g16, 15.0, ALU.add)
+    zero("v", 2048)
+    cp(R("wf", 0, 2), R("wi", 0, 2))
+    for u, w in ((0, "w1s"), (1, "w2s")):
+        ts(R(w), R("ri"), C("ce", 0), ALU.is_equal, C("wf", u), ALU.mult)
+
+    def slide(u, k):
+        return R(("w1s", "w2s")[u], 15 - k, 143 - k)
+
+    for c in range(4):
+        part = R("xb", 1024 * c, 1024 * c + 1024)
+        cp(part, R("xi", 1024 * c, 1024 * c + 1024))
+        parts = [(near, "h%d" % c, [(helper, part)])] if c < 3 else []
+        if c in (1, 3):
+            parts.append((off, "xp%d" % c, [(succ, R("xp", 1024 * c, 1024 * c + 1024))]))
+        send(part, parts)
+        zero("v", 1024 if c < 3 else 512)
+        for k in range(4 * c, 4 * c + 4):
+            for u in range(2):
+                mm(R("psS%d" % u, 0, 256), slide(u, k), R("xb", 256 * k, 256 * k + 256), k == 0, k == 15)
+    send(R("xb", 3072, V), [(off, "xq3", [(pred, R("xq", 3072, V))])])
+    zero("g", HT - fill[0])
+    iota(R("kr"), [[-1, 256]], 256, 0, True)
+    for k in range(16):
+        act((T.xf[:, k:V:16], [("xf", 256 * k, 256 * k + 256)]), R("xb", 256 * k, 256 * k + 256), AF.Identity, 128.0)
+
+    def places(out, w):
+        ts(R("tb", 0, 2 * w), R("ta", 0, 2 * w), 4095, ALU.bitwise_and)
+        tt(R("tm", 0, w), R("tb", 0, w), R("tb", w, 2 * w), ALU.mult)
+        ts(R("tn", 0, w), R("tm", 0, w), 5, ALU.arith_shift_right, H - 1, ALU.bitwise_and)
+        tt(out, R("tn", 0, w), R("tb", w, 2 * w), ALU.add)
+
+    cp(R("ta", 0, 256), R("psS0", 0, 256))
+    cp(R("ta", 256, 512), R("psS1", 0, 256))
+    places(R("slp"), 256)
+    cp(R("ixo"), R("slp"))
+    scatter(R("tab", 0, HT), R("ixo"), R("xf"))
+
+    def cell(j, k=1):
+        return (T.mm[:, 8 * j:8 * (j + k), :], [("mm", j, j + k)])
+
+    def pack(ps, src, cells=range(NC), odd=0, minus=None):
+        for j, (c, b, lo, hi) in enumerate(CELLS):
+            if j in cells:
+                out = R(ps, AT[odd][b], AT[odd][b] + 256)
+                if minus is not None and j >= NC - 2:
+                    mm(out, cell(j + 2), R(minus, 2048 + 256 * c, 2304 + 256 * c), False, False)
+                mm(out, cell(j), R(src, 256 * c, 256 * c + 256), lo == 0, hi == 16)
+
+    def sums(ps, o, src, a, b):
+        for u in range(2):
+            for k in range(16):
+                mm(R(ps, o + 256 * u + a // 16, o + 256 * u + b // 16), slide(u, k), R(src, a + k, b, 16), k == 0, k == 15)
+
+    def centred(out, ps):
+        cp(R("ta", 0, 512), ps)
+        ts(R("tb", 0, 512), R("ta", 0, 512), 4095, ALU.bitwise_and)
+        ts(R(out), R("tb", 0, 512), -2048.0, ALU.add)
+
+    sums("psA", 1024, "xp", 0, 2048)
+    sums("psA", 1024, "xp", 2048, 3072)
+    sums("psA", 1024, "xp", 3072, V)
+
+    ts(R("cg", 0, 4), R("cf", 0, 4), g16, ALU.add)
+    cp(R("po"), R("pab"))
+    for r, nm_ in enumerate(("fa", "fb", "fc")):
+        ts(R(nm_), R("ri", 0, 128), C("cg", r), ALU.is_equal, float(256 ** r), ALU.mult)
+    cp(R("xbb"), ind(R("xb"), R("po", 0, 16)))
+    ms(cell(0, NC), 0.0)
+    tt(R("idn"), R("fa"), R("fb"), ALU.add)
+    ms(R("dd", 256, 272), NONE)
+    tt(R("fm"), R("idn"), R("fc"), ALU.add)
+    for u, w in ((0, "w1b"), (1, "w2b")):
+        ts(R(w), R("rg"), g16, ALU.is_equal, C("wf", u), ALU.mult)
+    f3 = [("f3", 0, 1)]
+    cp((T.f3[:], f3), R("fm"))
+    ms(R("elv"), 11.0)
+    ts(R("idh"), R("ri", 0, 128), me, ALU.is_equal)
+    ts(R("m4k"), R("ri", 0, 128), me, ALU.is_equal, -4096.0, ALU.mult)
+    ts(R("cid"), R("ri", 0, 128), me, ALU.is_equal, 35.0 * 2048, ALU.mult)
+    for j, (c, b, lo, hi) in enumerate(CELLS):
+        cp((T.mm[:, 8 * j:8 * j + 8, lo:hi], [("mm", j, j + 1)]), (T.f3[:, :, lo:hi], f3))
+    pack("psB", "xp")
+
+    def for_totals():
+        ts(C("ce", 1), pm, -2.5, ALU.add)
+        ms(R("q"), 0.0)
+        ts(R("tci", 0, 3), R("ri", 0, 48, 16), C("ce", 1), ALU.add, 1.0 / 6, ALU.mult)
+        ts(R("idn"), R("ri", 0, 128), me, ALU.is_equal)
+        ts(R("tcf", 0, 3), R("tci", 0, 3), g16, ALU.add, 8.0, ALU.add)
+        ts(R("pkp", 256, 1024), R("psB", 0, 768), ONE, ALU.add)
+        ts(R("pkp", 0, 256), R("psB", 512, 768), ONE, ALU.add)
+        for b in range(3):
+            ts(R("gs", 144 * b, 144 * b + 136), R("ri", 0, 136), C("tcf", b), ALU.is_equal)
+
+    def for_winner():
+        ts(R("bow"), R("rg"), g16, ALU.is_equal, 512.0, ALU.mult)
+        ts(R("tie"), R("ri", 0, 4), 1.0 / 64, ALU.mult)
+        ts(R("q", 4, 512, 128), R("ri", 0, 4), 256.0, ALU.mult)
+        ts(R("i16"), R("ri", 0, 16), 16.0, ALU.mult, pm, ALU.add)
+        ts(cell(NC, 2), cell(NC - 2, 2), -1.0, ALU.mult)
+
+    def for_pairs():
+        ts(R("pt"), R("pab"), 8, ALU.arith_shift_right)
+        ts(R("em"), R("ri", 0, 16), pm, ALU.is_equal)
+        cp(R("ph"), R("pt"))
+        ts(C("ce", 3), pm, 256.0, ALU.mult, HT - 1.0, ALU.add)
+        ts(R("pt"), R("pab"), 255, ALU.bitwise_and)
+        cp(R("mk"), ind(R("em"), R("ph")))
+        ts(R("dmy"), R("kr"), C("ce", 3), ALU.add)
+        cp(R("pl", 0, 16), R("pt", 0, 16))
+        ts(R("pl", 16, 32), R("pt", 16, 32), 256.0, ALU.add)
+        ts(R("bon"), R("rg"), g16, ALU.is_equal, -1.0, ALU.mult)
+
+    tab = R("tab", 0, HT)
+
+    def shifted(ps, us, kb, sign, ds, w, k0):
+        for e, d in enumerate(ds):
+            a = k0 // 2 + w * e
+            ts(R("ndb", a, a + w), R("elv", 0, w), 0.0, ALU.mult, C("ndf", d), sign)
+        for u in range(2):
+            for e, d in enumerate(ds):
+                a = k0 + 512 * u + w * e
+                ts(R("kk", a, a + w), R(us, 256 * u, 256 * u + w), 2.0 ** -12, ALU.mult, C("qf", kb + 4 * u + d), ALU.add)
+            mm(R(ps, 512 * u, 512 * u + 512), R("cid"), R("elv"), True, False)
+            for e in range(len(ds)):
+                mm(R(ps, 512 * u + w * e, 512 * u + w * e + w), R("idh"), R(us, 256 * u, 256 * u + w), False, False)
+            mm(R(ps, 512 * u, 512 * u + 512), R(("w1b", "w2b")[u]), R("ndb", k0 // 2, k0 // 2 + 512), False, False)
+            mm(R(ps, 512 * u, 512 * u + 512), R("m4k"), R("kk", k0 + 512 * u, k0 + 512 * u + 512), False, True)
+
+    def placed(out, ps):
+        cp(R("tb", 0, 512), R(ps, 0, 512))
+        tt(R("tm", 0, 512), R("tb", 0, 512), R(ps, 512, 1024), ALU.mult)
+        ts(R("tn", 0, 512), R("tm", 0, 512), 5, ALU.arith_shift_right, H - 1, ALU.bitwise_and)
+        tt(out, R("tn", 0, 512), R(ps, 512, 1024), ALU.add)
+
+    def gather_a(buf, offs, o, bias, lo, hi):
+        act(R(buf, lo, hi), ind(tab, R(offs, o + lo // 16, o + hi // 16)), AF.Identity, bias)
+
+    def gather_b(buf, offs, o, notes, lo, hi):
+        tt(R(buf, lo, hi), ind(tab, R(offs, o + 128 + lo // 16, o + 128 + hi // 16)), R(notes, 2048 + lo, 2048 + hi), ALU.subtract)
+
+    def total(ps, j, cov):
+        at = [a % 768 for a in AT[j]]
+        steps = [(R("gs", 144 * b + 8, 144 * b + 136), R("na%d" % j, at[b], at[b] + 256)) for b in range(3)]
+        steps += [(R("gs", 144 * b, 144 * b + 128), R("nb%d" % j, at[b], at[b] + 256)) for b in range(3)]
+        steps = [steps[i] for i in (0, 1, 3, 4, 2, 5)]
+        if cov is not None:
+            steps = [(R("idn"), cov)] + steps
+        for i, (l, r) in enumerate(steps):
+            mm(R(ps, 0, 256), l, r, i == 0, i == len(steps) - 1)
+
+    for t in range(RO):
+        last = t == RO - 1
+        o0 = 64 * t
+        mine = o0 + 16 * (n - 1 - rank)
+        if t == 0:
+            tt(R("dd", 0, 256), ind(R("xp"), R("po", 16, 32)), R("xbb"), ALU.subtract)
+            cp(R("ofl", mine, mine + 2), R("dd", 0, 2))
+            cov = None
+        else:
+            s0 = 512 * (t - 1)
+            tt(R("kl"), R("kd"), R("il", s0, s0 + 256), ALU.subtract)
+            tt(R("km"), R("kl"), R("slp"), ALU.max)
+            cp(R("ixo"), R("km"))
+            scatter(R("tab"), R("ixo"), R("xf"))
+            tt(R("pg", 512, 1024), ind(R("il", s0, s0 + 512), R("pl")), R("mk"), ALU.mult)
+            mm(R("psS0", 0, 256), R("idn"), R("kr"), True, False)
+            for j in range(4):
+                mm(R("psS0", 0, 256), R("bon"), R("pg", 256 * j, 256 * j + 256), False, j == 3)
+            red(C("nm", 0), R("psS0", 0, 256), ALU.max, True)
+            ts(C("ko", 0), C("nm", 0), 0.0, ALU.min, 256.0, ALU.add)
+            cp(R("ofl", mine, mine + 16), ind(R("dd"), C("ko", 0)))
+        slot = R("ofl", mine, mine + 2)
+        send(slot, [(off, "of%d" % t, [(c, slot) for c in others])])
+        for j in range(n):
+            if 16 * j + o0 != mine:
+                lands(R("ofl", o0 + 16 * j, o0 + 16 * j + 2), "of%d" % t, ke * (n - 1))
+        if t == 0:
+            centred("up", R("psA", 1024, 1536))
+            for_totals()
+        else:
+            cov = R("ind", s0 + 256, s0 + 512)
+            tt(R("ind", s0, s0 + 512), R("pre"), R("il", s0, s0 + 512), ALU.max)
+        nd = R("ofl", o0, o0 + 64, 16)
+        for j, l in enumerate(("w1b", "w2b", "fm")):
+            mm(R("psS1", 256 + 4 * j, 260 + 4 * j), R(l), nd, True, True)
+        cp(R("ndf"), nd)
+        ts(R("qf", 0, 8), R("psS1", 256, 264), -2.0 ** -12, ALU.mult, KB, ALU.add)
+        shifted("psA", "up", 0, ALU.subtract, (0, 1), 256, 0)
+        ts(R("qf", 8, 12), nd, -127.0, ALU.add)
+        shifted("psB", "up", 0, ALU.subtract, (2, 3), 256, 1024)
+        ts(R("q", 3, 512, 128), R("psS1", 264, 268), -1.0, ALU.mult, -128 * ONE, ALU.add)
+        ts(R("q", 0, 512, 128), nd, -1.0, ALU.mult, -127.0, ALU.add)
+        ts(R("q", 1, 512, 128), R("psS1", 256, 260), 2048.0, ALU.add)
+        ts(R("q", 2, 512, 128), R("psS1", 260, 264), 2048.0, ALU.add)
+        ts(R("qf", 12, 16), R("psS1", 264, 268), -128 * ONE, ALU.add)
+        ts(R("qf", 16, 24), R("psS1", 256, 264), 2.0 ** -12, ALU.mult, KB, ALU.add)
+        if t == 0:
+            sums("psS1", 0, "xq", 0, V)
+        for h, ps in enumerate(("psA", "psB")):
+            placed(R("tm", 0, 512), ps)
+            cp(R("ix", 512 * h, 512 * h + 512), R("tm", 0, 512))
+        if t == 0:
+            iota(R("xf"), [[0, V]], 0, 0, True)
+
+        def pk(d, cells):
+            pack("psA", "ga%d" % (d % 2), cells, d % 2)
+            pack("psB", "gb%d" % (d % 2), cells, d % 2)
+
+        def look(d, lo, hi, cells):
+            gather_a("ga%d" % (d % 2), "ix", 256 * d, C("qf", 8 + d), lo, hi)
+            gather_b("gb%d" % (d % 2), "ix", 256 * d, "xp", lo, hi)
+            pk(d, cells)
+
+        def chk(d, lo=0, hi=768):
+            j = d % 2
+            tt(R("na%d" % j, lo, hi), R("psA", 768 * j + lo, 768 * j + hi), R("pkp", 256 - 256 * j + lo, 256 - 256 * j + hi), ALU.not_equal)
+            act(R("nb%d" % j, lo, hi), R("psB", 768 * j + lo, 768 * j + hi), AF.Abs, C("qf", 12 + d))
+
+        def tot(d):
+            total("psS%d" % (d % 2), d % 2, cov)
+
+        def fin(d):
+            act(R("ft", 256 * d, 256 * d + 256), R("psS%d" % (d % 2), 0, 256), AF.Relu, 1.0, -2.0, C("cl", 16 * t + 4 * rank + d))
+
+        for d in range(n):
+            look(d, 0, 1536, range(7))
+            if d > 1:
+                fin(d - 2)
+            if d > 0:
+                chk(d - 1)
+            if t == 0 and d == 1:
+                centred("uq", R("psS1"))
+            pk(d, (7,))
+            if d > 0:
+                tot(d - 1)
+            look(d, 1536, 2048, (8, 9))
+            if t == 0 and d == 2:
+                for_winner()
+        chk(3, 256, 768); chk(3, 0, 256); fin(2); tot(3); fin(3)
+        c0 = 16 * t
+        own = R("cl", c0 + 4 * rank, c0 + 4 * rank + 4)
+        send(own, [(off, "cn%d" % t, [(c, own) for c in others])])
+        for j in range(n):
+            if j != rank:
+                lands(R("cl", c0 + 4 * j, c0 + 4 * j + 4), "cn%d" % t, ke * (n - 1))
+        shifted("psB", "uq", 16, ALU.add, range(n), 128, 0)
+        if t == 0:
+            pack("psA", "xq")
+            act(R("pkq"), R("psA", 0, 768), AF.Identity, ONE)
+        placed(R("sp", 0, 512), "psB")
+        mm(R("psS0", 0, 4), R("bow"), R("tie"), True, False)
+        for i, j in enumerate([rank] + [j for j in range(n) if j != rank]):
+            mm(R("psS0", 0, 4), R("bow"), R("cl", c0 + 4 * j, c0 + 4 * j + 4), False, i == n - 1)
+        red(C("mx", t), R("psS0", 0, 4), ALU.max)
+        ts(R("wz", 8 * t, 8 * t + 8), R("i16", 0, 8), C("mx", t), ALU.add)
+        ts(R("wy"), R("wz", 8 * t, 8 * t + 8), 511, ALU.bitwise_and)
+        cp(R("so"), R("wy"))
+        cp(R("ixr", 0, 128), ind(R("sp", 0, 512), R("so")))
+        cp(R("qw"), ind(R("q"), C("so", 0)))
+        s0 = 512 * t
+        mark = 3.0 if last else BIG
+        fit = R("fs", s0 + 256, s0 + 512)
+        for u in range(2):
+            a = 256 * u + 128
+            ts(R("ta", 128 * u, 128 * u + 128), R("uq", a, a + 128), C("qw", 1 + u), ALU.add)
+        ts(R("fo"), R("i16"), C("qw", 4), ALU.add)
+        places(R("tm", 0, 128), 128)
+        cp(R("ixr", 128, 256), R("tm", 0, 128))
+        gather_a("ga0", "ixr", 0, C("qw", 0), 0, 1024)
+        pack("psA", "ga0", range(5))
+        act(fit, ind(R("ft"), R("fo")), AF.Identity, 0.0, mark)
+        send(fit, [(off, "ff%d" % t, [(pred, R("fs", s0, s0 + 256))])])
+        lands(R("fs", s0, s0 + 256), "ff%d" % t, ke)
+        gather_a("ga0", "ixr", 0, C("qw", 0), 1024, 2048)
+        pack("psA", "ga0", range(5, NC))
+        gather_a("gb0", "ixr", 128, 0.0, 1536, 2048)
+        gather_b("gb0", "ixr", 0, "xq", 0, 1024)
+        pack("psB", "gb0", range(5))
+        gather_b("gb0", "ixr", 0, "xq", 1024, 1536)
+        pack("psB", "gb0", range(5, NC), 0, "xq")
+        tt(R("na0"), R("psA", 0, 768), R("pkq"), ALU.not_equal)
+        act(R("nb0", 0, 512), R("psB", 0, 512), AF.Abs, C("qw", 3))
+        act(R("nb0", 512, 768), R("psB", 512, 768), AF.Abs, C("qw", 3))
+        total("psS1", 0, None)
+        img = R("it", 256 * t, 256 * t + 256)
+        act(img, R("psS1", 0, 256), AF.Relu, mark, -2.0 * mark)
+        to = [(succ, R("il", s0, s0 + 256))] + ([] if last else [(far, R("il", s0 + 256, s0 + 512))])
+        send(img, [(off, "fi%d" % t, to)])
+        lands(R("il", s0, s0 + 256 * len(to)), "fi%d" % t, ke * len(to))
+        if t == 0:
+            for_pairs()
+            cp(R("pre"), R("fs", 0, 512))
+        elif not last:
+            tt(R("pre"), R("ind", s0 - 512, s0), R("fs", s0, s0 + 512), ALU.max)
+        if not last:
+            tt(R("kd"), R("dmy"), R("pre", 0, 256), ALU.subtract)
+            tt(R("pg", 0, 512), ind(R("pre"), R("pl")), R("mk"), ALU.mult)
+
+    s0 = 512 * (RO - 1)
+    tt(R("ya"), R("ind", 0, 256), R("ind", 512, 768), ALU.add)
+    ts(R("yd"), R("ind", 512, 768), 3.0 / BIG, ALU.mult, -3.0, ALU.add)
+    ts(R("yb"), R("ya"), -1.0 / BIG, ALU.mult, 3.0, ALU.add)
+    ts(R("yi", 0, 3), R("wz", 0, 24, 8), 9, ALU.arith_shift_right)
+    tt(R("ya"), R("yb"), R("yd"), ALU.add)
+    ts(R("yi", 4, 7), R("wz", 0, 24, 8), 7, ALU.arith_shift_right, 3, ALU.bitwise_and)
+    ts(R("yt", 3, 6), R("yi", 0, 3), 1.0, ALU.add)
+    tt(R("yd"), R("ya"), R("fs", s0, s0 + 256), ALU.add)
+    ts(R("yt", 0, 3), R("yi", 4, 7), -1.0, ALU.mult, 4.0, ALU.add)
+    ts(R("yt", 8, 11), R("yi", 0, 3), 0.0, ALU.is_gt)
+    ts(R("yt", 11, 14), R("yi", 0, 3), 0.0, ALU.is_gt)
+    tt(R("yt", 0, 6), R("yt", 0, 6), R("yt", 8, 14), ALU.mult)
+    ts(R("yws", 0, 6), R("yt", 0, 6), -1.0, ALU.add)
+    order("s", R("yws")[1], [])
+    g.sync.dma_start(T.yw[:], T.yws[0:128:16, 0:6]).then_inc(T.sem.st, 16)
+    tt(R("ya"), R("yd"), R("il", s0, s0 + 256), ALU.max)
+    tt(R("yo"), R("ya"), R("yb"), ALU.min)
+    order("s", R("yo")[1], [])
+    g.sync.dma_start(T.yc[:], T.yo[:]).then_inc(T.sem.st, 16)
+    for q in cnt:
+        wait("s", "c" + q, cnt[q])
+    g.sync.wait_ge(T.sem.sent, sent[0])
+    g.sync.wait_ge(T.sem.st, 32)

@@ -7,49 +7,53 @@ BIG = 32768.0
 ONE = 65793.0
 NONE = -512.0
 KB = 192.0 + 2.0 ** -13
-CELLS = [(c, b, max(6 * c - 16 * b, 0), min(6 * c + 6 - 16 * b, 16)) for b in range(3) for c in range(8)
-         if 6 * c < 16 * b + 16 and 6 * c + 6 > 16 * b]
-NC = len(CELLS)
-AT = ((0, 256, 512), (1024, 1280, 768))
+CHUNKS = ((0, 768), (768, 2048), (2048, 3072), (3072, 4096))
+HALVES = ((0, 128), (128, 256))
+CAST = (0, 1, 2, 3)
+DEPTH = 2
+SLOW = 7
+STAGE = "a"
+CLEAR = [(512, "g")] * 6 + [(1024, "a")] * 14 + [(512, "v")] * 6
+FORTH = "avav" "aava" "avaa" "vava"
+WHO = "avaa"
+SINGLY = ((0, 0),)
+RESTS = ((0, 128), (128, 256))
+PB = (0, 4)
+PASSES = 4
+NG, NN = 8, 3
+GATHER, SCATTER, PE, WAKE, ISSUE, FLIGHT, LOCAL = 1.56, 3.8, 0.5, 120, 700, 3000, 2600
 
 f32, bf, i32, u16, f16 = "float32", "bfloat16", "int32", "uint16", "float16"
 S_ = {
-    "tab": (HT + V, f32), "xi": (V, i32), "xb": (V, bf), "xp": (V, bf), "xq": (V, bf), "xf": (V, f32),
-    "ga0": (2048, bf), "ga1": (2048, bf), "gb0": (2048, bf), "gb1": (2048, bf),
-    "na0": (768, bf), "na1": (768, bf), "nb0": (768, bf), "nb1": (768, bf),
-    "pkp": (1024, f32), "pkq": (768, f32), "so": (8, u16), "up": (512, f16), "uq": (512, f16),
-    "kk": (2048, bf), "ndb": (1024, bf), "elv": (512, bf), "m4k": (128, bf), "cid": (128, bf), "idh": (128, f16),
-    "dmy": (256, f32), "kd": (256, f32), "km": (256, f32), "kl": (256, f32),
-    "ix": (1024, u16), "ixr": (256, u16), "ixo": (256, u16), "slp": (256, i32),
-    "wi": (8, i32), "wf": (8, f32), "pab": (32, i32), "pt": (32, i32), "po": (32, u16), "ph": (32, u16), "pl": (32, u16),
-    "ri": (144, f32), "rg": (128, f32), "i1": (4, i32), "j1": (8, i32), "cf": (8, f32), "cg": (8, f32), "ce": (8, f32),
-    "tci": (4, i32), "tcf": (4, f32),
-    "w1s": (144, bf), "w2s": (144, bf), "w1b": (128, bf), "w2b": (128, bf), "bon": (128, bf), "bow": (128, f32),
-    "idn": (128, bf), "fa": (128, bf), "fb": (128, bf), "fc": (128, bf), "fm": (128, bf), "gs": (432, bf),
-    "em": (16, bf), "mk": (512, bf), "kr": (256, bf), "i16": (16, f32), "tie": (4, f32),
-    "xbb": (256, bf), "dd": (272, bf), "pg": (1024, bf), "nm": (2, f32), "ko": (2, u16),
-    "ofl": (192, bf), "q": (512, f32), "qf": (24, f32), "qw": (16, f32), "ndf": (4, f32), "cl": (48, f32),
-    "mx": (4, f32), "wz": (24, i32), "wy": (8, i32), "fo": (16, u16),
-    "ft": (1024, bf), "fs": (1536, bf), "it": (768, bf), "il": (1536, bf), "pre": (512, bf), "ind": (1024, bf),
-    "ya": (256, f32), "yb": (256, f32), "yd": (256, f32), "yo": (256, f32), "yt": (16, f32), "yi": (8, i32), "yws": (8, f32),
+    "tab": (HT + V, f32), "xi": (V, i32), "xs": (V, bf), "xb": (V, bf), "xf": (V, f32), "zr": (2048, f32),
+    "ga": (NG * 1024, bf), "kk": (2048, bf), "ndb": (1024, bf), "elv": (512, bf), "m4k": (128, bf), "cid": (128, bf),
+    "idh": (128, f16), "idf": (128, f32), "hn": (128, bf), "idw": (224, bf), "sel": (224, f16), "fsl": (64, bf),
+    "pw": (144, bf), "big": (128, bf), "neg": (128, bf), "ut": (1536, f32), "xo": (256, f32), "km": (256, f32), "slp": (256, f32),
+    "pa1": (1024, f32), "ix": (1024, u16), "ixr": (256, u16), "ixo": (256, u16), "so": (16, u16),
+    "wi": (40, i32), "pay": (160, f16), "wf": (8, f32), "pt": (96, i32), "po": (32, u16), "ph": (32, u16), "pl": (32, u16),
+    "ri": (256, f32), "rm": (384, bf), "rg": (128, bf), "r32": (128, bf), "rb": (128, bf),
+    "i1": (4, i32), "j1": (8, i32), "cf": (8, f32), "cg": (16, f32), "ce": (24, f32), "tci": (8, i32),
+    "wm": (48, bf), "wb": (256, bf), "we": (256, bf), "eq": (128, bf), "bon": (256, bf), "bow": (128, f32),
+    "em": (16, bf), "mk": (512, bf), "kr": (256, bf), "i16": (16, f32), "tie": (4, f32), "m4": (4, bf),
+    "xab": (576, bf), "dd": (272, bf), "pg": (512, bf), "nm": (2, f32), "ko": (2, u16), "dg": (16, f32), "dm": (4, bf), "dmf": (4, f32),
+    "q": (1024, f32), "qf": (16, f32), "qw": (16, f32), "cl": (12, f32), "mx": (8, f32),
+    "ft": (1024, bf), "fw": (256, bf), "cov": (512, bf), "zf": (256, f32), "yo": (256, f32), "yl": (256, f32),
+    "yt": (4, f32), "yws": (32, f32),
 }
-ALIAS = {"ta": 0, "tb": 1024, "tm": 2048, "tn": 2560, "sp": 3072}
 SCRATCH = {k: ("sbuf", [128, v[0]], v[1]) for k, v in S_.items()}
-SCRATCH["f3"] = ("sbuf", [128, 8, 16], bf)
-SCRATCH["mm"] = ("sbuf", [128, 8 * (NC + 2), 16], bf)
-for k_, n_ in (("psA", 1536), ("psB", 1536), ("psS0", 512), ("psS1", 512)):
-    SCRATCH[k_] = ("psum", [128, n_], f32)
+SCRATCH["us"] = ("sbuf", [128, 4, 256], f16)
+SCRATCH["pk"] = ("sbuf", [128, 96, 16], f32)
+SCRATCH["na"] = ("sbuf", [128, 48 * NN, 16], bf)
+for k_ in ("y1", "y2", "y3"):
+    SCRATCH[k_] = ("sbuf", [128, 2, 256], bf)
+for k_, (a_, b_) in enumerate(CHUNKS):
+    SCRATCH["st%d" % k_] = ("dram", [4, 128, (b_ - a_) // 4], bf)
+    SCRATCH["dl%d" % k_] = ("dram", [4, 128, (b_ - a_) // 4], bf)
+SCRATCH["psA"] = ("psum", [128, 2048], f32)
+SCRATCH["psB"] = ("psum", [128, 2048], f32)
 
-SEMAPHORES = (["cv", "ca", "cp", "cg", "sent", "ldw", "ldp", "st", "xq", "xq3"] + ["ld%d" % c for c in range(4)]
-              + ["xp%d" % c for c in range(4)] + ["h%d" % c for c in range(3)]
-              + [s + str(t) for s in ("of", "cn", "ff", "fi") for t in range(RO)])
-
-
-def helper_of(c, T, topo):
-    n = len(T.cores)
-    r = T.rank_of(c)
-    return [h for h in topo.cores_of(c) if topo.die(h) != topo.die(c) and T.rank_of(h) is None
-            and topo.may_write(h, T.cores[(r + 1) % n]) and topo.may_write(h, T.cores[(r - 1) % n])][0]
+SEMAPHORES = (["cv", "ca", "cp", "cg", "sent", "ldw", "st", "pay", "yw"]
+              + [s + str(k) for s in ("sg", "ld", "la", "ow", "re", "cf", "yc") for k in range(4)])
 
 
 def count(mask):
@@ -61,506 +65,574 @@ def dst(c, topo):
     return DstId(rid=rid, pnc=pid)
 
 
-def helper_program(g, core, owner, T, topo):
-    n = len(T.cores)
-    r = T.rank_of(owner)
-    succ, pred = T.cores[(r + 1) % n], T.cores[(r - 1) % n]
-    k = count(topo.mask(owner, core) & ~topo.mask(owner, succ))
-    total = 0
-    for c in (0, 2):
-        g.wait_ge(T.sem["h%d" % c], k)
-        rid, pid, _ = topo.addr(succ)
-        m = topo.mask(core, succ)
-        g.remote_dma(T.xp[:, 1024 * c:1024 * c + 1024], T.xb[:, 1024 * c:1024 * c + 1024], T.sem["xp%d" % c],
-                     T.sem.sent, pid, rid, m)
-        total += count(m)
-    g.wait_ge(T.sem.h1, k)
-    rid, pid, _ = topo.addr(pred)
-    m = topo.mask(core, pred)
-    g.remote_dma(T.xq[:, 0:3072], T.xb[:, 0:3072], T.sem.xq, T.sem.sent, pid, rid, m)
-    g.wait_ge(T.sem.sent, total + count(m))
+def shares(core, to, topo):
+    eng = [e for e in topo.engines(core, to[0]) if all(e in topo.engines(core, c) for c in to)]
+    h = len(eng) // 4
+    return sum(1 << e for e in eng), [sum(1 << e for e in part) for part in (eng[:2 * h], eng[2 * h:3 * h], eng[3 * h:])]
+
+
+def meets(log, reads, writes, engine):
+    return [tok for regs, w in ((reads, False), (writes, True)) for name, lo, hi in regs for a, b, ew, tok, q in log.get(name, [])
+            if a < hi and lo < b and (w or ew or (name.startswith("ps") and q != engine))]
+
+
+def enter(log, reads, writes, tok, engine):
+    for name, lo, hi in writes:
+        log[name] = [e for e in log.get(name, []) if not (lo <= e[0] and e[1] <= hi)] + [(lo, hi, True, tok, engine)]
+    for name, lo, hi in reads:
+        log.setdefault(name, []).append((lo, hi, False, tok, engine))
+
+
+def arrange(calls):
+    log, deps = {}, []
+    for i, c in enumerate(calls):
+        key = "".join(c["cost"])
+        deps.append(set(meets(log, c["reads"], c["writes"], key if len(key) == 1 else i)) | set(c["after"]))
+        enter(log, c["reads"], c["writes"], i, key if len(key) == 1 else i)
+    way = [0.0] * len(calls)
+    users = [[] for _ in calls]
+    for i in reversed(range(len(calls))):
+        way[i] = min(calls[i]["cost"].values()) + calls[i]["late"] + WAKE + max([way[j] for j in users[i]] + [0.0])
+        for d in deps[i]:
+            users[d].append(i)
+
+    def lay(before, after, rank, back):
+        busy = {q: [] for q in "vapgsx"}
+        left = [len(d) for d in before]
+        since = [calls[i]["late"] if back else 0.0 for i in range(len(calls))]
+        ready = {i for i in range(len(calls)) if not left[i]}
+        at = [None] * len(calls)
+        while ready:
+            i = max(ready, key=lambda x: (rank[x], x if back else -x))
+            ready.remove(i)
+            best = None
+            for q, cost in calls[i]["cost"].items():
+                t, k = since[i], 0
+                for k, (a, b) in enumerate(busy[q] + [(1e18, 1e18)]):
+                    if t + cost <= a:
+                        break
+                    t = max(t, b)
+                if best is None or t + cost < best[0]:
+                    best = (t + cost, t, q, k)
+            end, t, q, k = best
+            if q != "x":
+                busy[q].insert(k, (t, end))
+            at[i] = (t, i, q, end)
+            for j in after[i]:
+                lag = calls[j if back else i]["late"] + (0 if q == "p" and "p" in calls[j]["cost"] else WAKE)
+                since[j] = max(since[j], end + lag)
+                left[j] -= 1
+                if not left[j]:
+                    ready.add(j)
+        return at
+
+    plan = None
+    for _ in range(PASSES):
+        at = lay(deps, users, [1e9 - i if c["lead"] else way[i] for i, c in enumerate(calls)], False)
+        span = max(x[3] + calls[x[1]]["late"] for x in at)
+        if plan is None or span < plan[0]:
+            plan = (span, at)
+        way = [x[3] for x in lay(users, deps, [x[3] + calls[x[1]]["late"] for x in at], True)]
+    return [(i, q) for _, i, q, _ in sorted(plan[1])]
 
 
 def rank_program(g, core, T, topo):
     rank = T.rank_of(core)
     if rank is None:
-        for c in T.cores:
-            if helper_of(c, T, topo) == core:
-                helper_program(g, core, c, T, topo)
         return
     n = len(T.cores)
-    succ, pred, far = T.cores[(rank + 1) % n], T.cores[(rank - 1) % n], T.cores[(rank + 2) % n]
-    others = [T.cores[(rank + j) % n] for j in range(1, n)]
-    helper = helper_of(core, T, topo)
-    off = topo.mask(core, succ)
-    for c in others:
-        off &= topo.mask(core, c)
-    near = topo.mask(core, helper) & ~topo.mask(core, succ)
-
+    others = [(rank + j) % n for j in range(1, n)]
+    off, thirds = shares(core, [T.cores[r] for r in others], topo)
+    ke = count(off)
     Q = {"v": g.vector, "a": g.scalar, "p": g.tensor, "g": g, "s": g.sync}
-    cnt = {"v": 0, "a": 0, "p": 0, "g": 0}
-    seen = {k: {} for k in Q}
-    log = {}
+    calls = []
     sent = [0]
+    lead = [True]
 
-    def R(name, a=0, b=None, s=1):
-        if name in ALIAS:
-            name, a, b = "xi", ALIAS[name] + a, ALIAS[name] + b
+    def R(name, a=0, b=None, s=1, m=128):
+        name = "xi" if name == "wk" else name
         t = T[name]
         b = t.shape[1] if b is None else b
         lo, hi = (a // 512 * 512, (b + 511) // 512 * 512) if name.startswith("ps") else (a, b)
-        return (t[:, a:b:s] if s != 1 else t[:, a:b], [(name, lo, hi)])
+        return (t[0:m, a:b:s] if s != 1 else t[0:m, a:b], [(name, lo, hi)], (b - a + s - 1) // s, SCRATCH[name][2], False)
 
     def C(name, a):
         return R(name, a, a + 1)
 
+    def B(bank, a=0, b=512, s=1, m=128):
+        return R("ps" + "AB"[bank // 4], 512 * (bank % 4) + a, 512 * (bank % 4) + b, s, m)
+
+    def X(name, a, b, view, m):
+        return (view, [(name, a, b)], m, SCRATCH[name][2], False)
+
+    def D(k, r=None, name="dl"):
+        t = T[name + str(k)]
+        return (t[:], [(t.name, 0, n)], 0, bf, False) if r is None else (t[r], [(t.name, r, r + 1)], 0, bf, False)
+
+    def hbm(view, behind=()):
+        return (view, list(behind), 0, i32, False)
+
     def ind(win, offs):
-        return (win[0].indirect(offs[0]), win[1] + offs[1])
+        return (win[0].indirect(offs[0]), win[1] + offs[1], 16 * offs[2], win[3], True)
+
+    def call(cost, make, outs, ins, late=0, after=(), sem=None):
+        calls.append({"lead": lead[0], "cost": cost, "make": make, "late": late, "after": after, "sem": sem,
+                      "reads": sorted({r for x in ins if isinstance(x, tuple) for r in x[1]}),
+                      "writes": sorted({r for x in outs for r in x[1]})})
+        return len(calls) - 1
+
+    def ap(x):
+        return x[0] if isinstance(x, tuple) else x
+
+    def cyc(out, a, k=1.0):
+        if a[4]:
+            return 60 + GATHER * a[2]
+        return 60 + max(64, a[2] * (0.5 if out[3] in (bf, f16, u16) and a[3] in (bf, f16, u16) and k == 1.0 else k))
+
+    def cp(out, a):
+        call({"v": cyc(out, a)}, lambda q: g.vector.tensor_copy(out[0], a[0]), [out], [a])
+
+    def tt(out, a, b, o):
+        two = not (a[1][0][0].startswith("ps") or b[1][0][0].startswith("ps"))
+        call({"v": cyc(out, a, 2.0 if two else 1.001)}, lambda q: g.vector.tensor_tensor(out[0], a[0], b[0], o), [out], [a, b])
+
+    def ts(out, a, s1, o1, s2=None, o2=None):
+        if o2 is None:
+            call({"v": cyc(out, a)}, lambda q: g.vector.tensor_scalar(out[0], a[0], ap(s1), None, o1), [out], [a, s1])
+        else:
+            call({"v": cyc(out, a)}, lambda q: g.vector.tensor_scalar(out[0], a[0], ap(s1), ap(s2), o1, o2), [out], [a, s1, s2])
+
+    def lin(out, a, scale=1.0, bias=0.0, qs="va"):
+        def make(q):
+            if q == "a":
+                return g.scalar.activation(out[0], a[0], AF.Identity, ap(bias), ap(scale))
+            return g.vector.tensor_scalar(out[0], a[0], ap(scale), ap(bias), ALU.mult, ALU.add)
+        cost = {"v": cyc(out, a), "a": 80 + (GATHER if a[4] else 1) * a[2]}
+        call({q: cost[q] for q in qs}, make, [out], [a, scale, bias])
+
+    def relu(out, a, scale, bias, acc=None):
+        def make(q):
+            if acc is None:
+                return g.scalar.activation(out[0], a[0], AF.Relu, bias, scale)
+            return g.scalar.activation(out[0], a[0], AF.Relu, bias, scale, accum_out=acc[0])
+        call({"a": 100 + a[2]}, make, [out] + ([] if acc is None else [acc]), [a])
+
+    def ms(out, val):
+        call({"v": cyc(out, out)}, lambda q: g.vector.memset(out[0], val), [out], [])
+
+    def red(out, a, o, neg=False):
+        call({"v": cyc(out, a)}, lambda q: g.vector.tensor_reduce(out[0], a[0], AX.X, o, negate=neg), [out], [a])
+
+    def scatter(win, offs, src, first=0):
+        call({"a": 80 + SCATTER * src[2] + first}, lambda q: g.scalar.activation(win[0].indirect(offs[0]), src[0], AF.Silu), [win], [offs, src])
+
+    def group(steps, apart=False):
+        def make(q):
+            for i, (out, l, r) in enumerate(steps):
+                last = g.tensor.matmul(out[0], l[0], r[0], apart or i == 0, apart or i == len(steps) - 1)
+            return last
+        call({"p": sum(12 + PE * max(64, r[2]) * (4 if r[3] == f32 else 1) for _, _, r in steps)}, make,
+             [s[0] for s in steps], [x for s in steps for x in s[1:]])
+
+    def iota(out, pat, base, cm):
+        def make(q):
+            if out[3] == i32:
+                return g.iota(out[0], pat, base, cm)
+            return g.iota(out[0], pat, base, cm, allow_small_or_imprecise_dtypes=True)
+        call({"g": 160 + 2 * out[2]}, make, [out], [])
+
+    def dma(q, out, src, sem, total, late=LOCAL, hold=120):
+        return call({q: hold}, lambda q: Q[q].dma_start(out[0], src[0]), [out], [src], late, (), (sem, total))
+
+    def send(parts, late=0):
+        def make(q):
+            g.remote_dma_fused([RemoteDMATransfer(dst_ids=[dst(c, topo) for c, _ in to], dma_engine_mask=m,
+                                                  remote_sem=T.sem[sem], srcs=[src[0]], dsts=[d[0] for _, d in to])
+                                for src, m, sem, to in parts], local_sem=T.sem.sent)
+        sent[0] += sum(count(p[1]) for p in parts)
+        return call({"g": ISSUE}, make, [], [p[0] for p in parts], FLIGHT + late, (), "far")
+
+    def lands(regs, sem, total, twin):
+        call({"x": 1}, None, regs, [], -WAKE, (twin,), (sem, total))
+
+    for a, b, src in ((0, 16, T.pa), (16, 17, T.w1), (17, 18, T.w2), (18, 34, T.pb)):
+        dma("a", R("wi", a, b), hbm(src[:]), "ldw", 64)
+    for k, (a, b) in enumerate(CHUNKS):
+        dma("s", R("xi", a, b), hbm(T.x[:, a:b], R("xi", *CHUNKS[k - DEPTH])[1] if k >= DEPTH else []), "ld%d" % k, 16, LOCAL, 2 * (b - a))
+
+    lead[0] = False
+    ms(R("zr", 0, 512), 0.0)
+    lin(R("zr", 512, 1024), R("zr", 0, 512))
+    iota(R("zr", 1024, 2048), [[0, 1024]], 0, 0)
+    a = 0
+    for w, qs in CLEAR:
+        def clear(q, out=R("tab", a, a + w), w=w):
+            if q == "v":
+                return g.vector.memset(out[0], 0.0)
+            if q == "a":
+                return g.scalar.activation(out[0], T.zr[:, 0:w], AF.Identity, 0.0, 1.0)
+            return g.iota(out[0], [[0, w]], 0, 0, allow_small_or_imprecise_dtypes=True)
+        cost = {"v": 60 + w, "a": 80 + w, "g": 160 + 2 * w}
+        call({q: cost[q] for q in qs}, clear, [R("tab", a, a + w)], [R("zr", 0, w)] if "a" in qs else [])
+        a += w
+
+    iota(R("i1"), [[32, 4]], 0, 1)
+    iota(R("ri"), [[1, 256]], 0, 0)
+    iota(R("rm"), [[0, 3], [1, 128]], 0, 0)
+    iota(R("rg"), [[16, 8], [0, 16]], 0, 0)
+    iota(R("r32"), [[0, 4], [1, 32]], 0, 0)
+    iota(R("rb"), [[0, 4], [1, 2], [0, 16]], 0, 0)
+    iota(R("kr"), [[-1, 256]], 256, 0)
+    ts(R("j1", 0, 4), R("i1"), 112, ALU.bitwise_and)
+    ts(C("j1", 4), C("i1", 0), 15, ALU.bitwise_and)
+    ts(C("j1", 5), C("i1", 0), 31, ALU.bitwise_and)
+    ts(C("j1", 6), C("i1", 0), 96, ALU.bitwise_and)
+    ts(C("j1", 7), C("i1", 0), 4, ALU.arith_shift_right, 1, ALU.bitwise_and)
+    cp(R("cf"), R("j1"))
+    g16, gup, pm, p31, r32, gp = C("cf", 0), C("cf", 1), C("cf", 4), C("cf", 5), C("cf", 6), C("cf", 7)
+    me = C("cg", 4)
+    ts(me, g16, pm, ALU.add)
+    ts(C("ce", 0), p31, 96.0, ALU.add)
+    ts(C("ce", 1), r32, 32.0 * rank, ALU.is_equal)
+    ts(R("sel"), R("ri", 0, 224), C("ce", 0), ALU.is_equal, C("ce", 1), ALU.mult)
+    ts(R("idf"), R("rm", 0, 128), me, ALU.is_equal)
+    ms(R("neg"), -128.0)
+
+    mine = 40 * rank
+    ts(R("pay", mine, mine + 34), R("wi", 0, 34), -2048.0, ALU.add)
+    cp(R("pay", mine + 16, mine + 18), R("wi", 16, 18))
+    slot = R("pay", mine, mine + 34)
+    lands([R("pay", 40 * r, 40 * r + 34) for r in others], "pay", ke * (n - 1),
+          send([(slot, off, "pay", [(T.cores[r], slot) for r in others])], 1500))
+    for lo, a, b, step in ((20, 16, 34, 0), (0, 0, 18, 1), (18, 16, 18, -1)):
+        group([(B(7, lo, lo + b - a), R("sel", 96 - 32 * r, 224 - 32 * r), R("pay", 40 * ((r + step) % n) + a, 40 * ((r + step) % n) + b))
+               for r in range(n)])
+    cp(R("wf", 0, 6), B(7, 16, 22))
+    ts(R("pt", 0, 16), B(7, 22, 38), 2048.0, ALU.add)
+    ts(R("pt", 16, 32), B(7, 0, 16), 2048.0, ALU.add)
+    for u in range(2):
+        ts(R("wb", 128 * u, 128 * u + 128), R("rg"), g16, ALU.is_equal, C("wf", 4 + u), ALU.mult)
+        for kind, (to, w) in enumerate(((0, 4), (1, 0), (3, 2))):
+            a = 16 * kind + 8 * u
+            ts(R("wm", a, a + 8), R("rm", 0, 128, 16), C("cf", to), ALU.is_equal, C("wf", w + u), ALU.mult)
+    ts(R("eq"), R("r32"), p31, ALU.is_equal)
+    group([(B(7, 0, 256), R("eq"), R("wb"))])
+    lin(R("we"), B(7, 0, 256))
+
+    for k, (a, b) in enumerate(CHUNKS):
+        w = (b - a) // 4
+        lead[0] = True
+        ts(R("xs", a, b), R("xi", a, b), 128.0, ALU.add)
+        dma(STAGE, D(k, None, "st"), R("xs", a, b), "sg%d" % k, 16, LOCAL + w)
+        dma(STAGE, D(k, rank), (T.xs[32 * rank:32 * rank + 32, a:b],) + R("xs", a, b)[1:], "ow%d" % k, 16)
+        lands([D(k, r) for r in others], "la%d" % k, ke,
+              send([(D(k, r, "st"), thirds[(j + k) % 3], "la%d" % k, [(T.cores[r], D(k, rank))]) for j, r in enumerate(others)], SLOW * w))
+        dma("s", R("xb", a, b), D(k), "re%d" % k, 16, LOCAL + 3 * w)
+        if k in CAST:
+            dma("g", R("xf", a, b), D(k), "cf%d" % k, 16, LOCAL + 6 * w, ISSUE)
+        lead[0] = False
+        if k not in CAST:
+            lin(R("xf", a, b), R("xb", a, b))
+
+    def sums(bank, o, a, b, c0, m, out):
+        w = 16 * (b - a)
+        group([(B(bank, k, w, 16, m), R("xb", 16 * c0 + k, 16 * (c0 + m), 16), R("wm", a, b)) for k in range(16)], True)
+        lin(R("ut", o, o + w, 1, m), B(bank, 0, w, 1, m))
+        turned(o, m, out, range(2))
+
+    def turned(o, m, out, js):
+        for j in js:
+            group([(out(j), R("wb", 128 * (j % 2), 128 * (j % 2) + 128), R("neg", 0, m)),
+                   (out(j), R("ut", o + 128 * j, o + 128 * j + 128, 1, m), R("idf", 0, m, 1, m))])
+
+    def places(out, o, w):
+        ts(R("wk", o + 2 * w, o + 4 * w), R("wk", o, o + 2 * w), 4095, ALU.bitwise_and)
+        tt(R("wk", o, o + w), R("wk", o + 2 * w, o + 3 * w), R("wk", o + 3 * w, o + 4 * w), ALU.mult)
+        ts(R("wk", o + w, o + 2 * w), R("wk", o, o + w), 5, ALU.arith_shift_right, H - 1, ALU.bitwise_and)
+        tt(out, R("wk", o + w, o + 2 * w), R("wk", o + 3 * w, o + 4 * w), ALU.add)
+
+    for k, (a, b) in enumerate(CHUNKS):
+        a, w = a // 16, (b - a) // 16
+        sums(6 + k % 2, 256 * (k % 2), 0, 16, a, w, lambda u: B(4 + k % 2, w * u, w * u + w))
+        cp(R("wk", 4 * a, 4 * a + 2 * w), B(4 + k % 2, 0, 2 * w))
+        places(R("slp", a, a + w), 4 * a, w)
+        cp(R("ixo", a, a + w), R("slp", a, a + w))
+        scatter(R("tab", 0, HT), R("ixo", a, a + w), R("xf", 16 * a, 16 * (a + w)), 0 if k else 1570)
+
+    def centred(j, a, b, src):
+        w = b - a
+        o = 1024 + 8 * a + 4 * w * j
+        cp(R("wk", o, o + 2 * w), src)
+        ts(R("wk", o + 2 * w, o + 4 * w), R("wk", o, o + 2 * w), 4095, ALU.bitwise_and)
+        ts(X("us", 256 * j + a, 256 * j + b, T.us[:, 2 * j:2 * j + 2, a:b], 2 * w), R("wk", o + 2 * w, o + 4 * w), -2048.0, ALU.add)
+
+    for h, (a, b) in enumerate(HALVES):
+        w = b - a
+        sums(2 + h, 512 + 512 * h, 16, 48, a, w, lambda j: B(h, w * j, w * j + w))
+        centred(0, a, b, B(h, 0, 2 * w))
+
+    def U(j, a, b):
+        return X("us", 256 * (j // 2) + a, 256 * (j // 2) + b, T.us[:, j, a:b], b - a)
+
+    ts(R("idw"), R("rm", 0, 224), me, ALU.is_equal)
+    idn, up2 = R("idw", 0, 128), R("idw", 96, 224)
+    cp(R("po"), R("pt", 0, 32))
+    ts(R("xab", 512, 544), ind(R("xb"), R("po", 0, 2)), -1.0, ALU.mult)
+    cp(R("xab", 544, 576), ind(R("xb"), R("po", 16, 18)))
+    group([(B(4, 0, 1), idn, C("xab", 512)), (B(4, 0, 1), up2, C("xab", 544))])
+    cp(C("dg", 0), B(4, 0, 1))
+    lin(R("xab", 0, 256), ind(R("xb"), R("po", 0, 16)), -1.0)
+    lin(R("xab", 256, 512), ind(R("xb"), R("po", 16, 32)))
+    group([(B(6, 0, 256), idn, R("xab", 0, 256)), (B(6, 0, 256), up2, R("xab", 256, 512))])
+    lin(R("dd", 0, 256), B(6, 0, 256))
+    ms(R("dd", 256, 272), NONE)
+    ts(C("ce", 6), r32, -1.0 / 32, ALU.mult, 3.0, ALU.add)
+    ts(R("m4"), R("rm", 0, 4), C("ce", 6), ALU.is_equal)
+    ms(R("elv"), 11.0)
+    ts(R("idh"), R("rm", 0, 128), me, ALU.is_equal)
+    ts(R("m4k"), R("rm", 0, 128), me, ALU.is_equal, -4096.0, ALU.mult)
+    ts(R("cid"), R("rm", 0, 128), me, ALU.is_equal, 35.0 * 2048, ALU.mult)
+
+    ts(C("tci", 4), pm, -1.0, ALU.add, 1.0 / 3, ALU.mult)
+    cp(C("ce", 2), C("tci", 4))
+    ts(C("ce", 3), C("ce", 2), -3.0, ALU.mult, pm, ALU.add)
+    ts(C("ce", 4), C("ce", 3), 32512.5, ALU.mult, -32257.5, ALU.add)
+    ts(C("ce", 8), C("ce", 4), C("ce", 3), ALU.mult, 1.0, ALU.add)
+    ts(C("ce", 5), C("ce", 2), 8.0, ALU.mult)
+    ts(R("ce", 9, 13), R("cf", 0, 4), 1.0 / 16, ALU.mult, C("ce", 5), ALU.add)
+    for j, to in enumerate((9, 12, 10)):
+        ts(R("pw", 48 * j, 48 * j + 48), R("rm", 0, 48), C("ce", to), ALU.is_equal, C("ce", 8), ALU.mult)
+    ts(R("big"), R("rm", 0, 128), me, ALU.is_equal, BIG, ALU.mult)
+
+    def pack(banks, src, a, j):
+        for h in range(2):
+            group([(B(banks[h], k, 384, 8), R(src, a + 8 * h + k, a + 2048, 16), R("pw", 48 * j, 48 * j + 48)) for k in range(8)], True)
+
+    def words(name, j, h, a=0, b=48):
+        return X(name, 2 * j + h, 2 * j + h + 1, T[name][:, 48 * j + a:48 * j + b, 8 * h:8 * h + 8], 8 * (b - a))
+
+    for j in range(2):
+        pack((2, 3), "xb", 2048 * j, 0)
+        for h in range(2):
+            lin(words("pk", j, h, 0, 40), B(2 + h, 0, 320), 1.0, -127 * ONE)
+            lin(words("pk", j, h, 40, 48), B(2 + h, 320, 384), 1.0, -127.0)
+
+    for e in range(n):
+        ms(R("q", 256 * e, 256 * e + 16), 0.0)
+    ts(R("bow"), R("rb"), gp, ALU.is_equal, 1024.0, ALU.mult)
+    ts(R("tie"), R("ri", 0, 4), 1.0 / 256, ALU.mult)
+    ts(R("i16"), R("ri", 0, 16), 16.0, ALU.mult, pm, ALU.add)
+    ts(C("ce", 18), pm, 256.0, ALU.mult, float(HT), ALU.add)
+    lin(R("xo"), R("ri"), 1.0, C("ce", 18))
+    ts(R("pt", 32, 64), R("pt", 0, 32), 15, ALU.bitwise_and)
+    ts(R("pt", 64, 96), R("pt", 0, 32), 4, ALU.arith_shift_right)
+    ts(R("em"), R("rm", 0, 16), pm, ALU.is_equal)
+    cp(R("ph"), R("pt", 32, 64))
+    cp(R("pl"), R("pt", 64, 96))
+    ts(R("bon", 0, 128), R("rg"), g16, ALU.is_equal, -512.0, ALU.mult)
+    ts(R("bon", 128, 256), R("rg"), gup, ALU.is_equal, -512.0, ALU.mult)
+    lin(R("mk"), ind(R("em"), R("ph")))
+    ts(C("ce", 19), r32, 0.5, ALU.mult, pm, ALU.add)
+    ts(R("ce", 13, 15), R("ri", 0, 2), gp, ALU.is_equal)
+    ts(R("cg", 8, 10), R("ri", 0, 2), gp, ALU.is_equal, 3.0, ALU.mult)
+    ts(R("fsl"), R("rm", 0, 64), C("ce", 19), ALU.is_equal)
+    ts(R("hn"), R("rm", 0, 128), me, ALU.is_equal, -32.0 * BIG, ALU.mult)
+
+    def turn(bank, names):
+        for r in range(n):
+            for j in range(4):
+                a = 64 * r + 16 * j
+                group([(B(bank, a, a + 16), X(nm, 0, 4, T[nm][:, :, j:256:4], 128), R("fsl", 16 * r, 16 * r + 16)) for nm in names])
+
+    tab = R("tab", 0, HT)
+
+    def shifted(bank, ds, k0):
+        for e, d in enumerate(ds):
+            a = k0 // 2 + 256 * e
+            lin(R("ndb", a, a + 256), R("elv", 0, 256), 0.0, C("dmf", d))
+        for u in range(2):
+            for e, d in enumerate(ds):
+                a = k0 + 512 * u + 256 * e
+                ts(R("kk", a, a + 256), U(u, 0, 256), 2.0 ** -12, ALU.mult, C("qf", 4 * u + d), ALU.add)
+            group([(B(bank + u), R("cid"), R("elv"))]
+                  + [(B(bank + u, 256 * e, 256 * e + 256), R("idh"), U(u, 0, 256)) for e in range(2)]
+                  + [(B(bank + u), R("we", 128 * u, 128 * u + 128), R("ndb", k0 // 2, k0 // 2 + 512)),
+                     (B(bank + u), R("m4k"), R("kk", k0 + 512 * u, k0 + 512 * u + 512))])
+
+    def placed(bank, a, w, o, out="ix", qs="va"):
+        lin(R("pa1", o, o + w), B(bank, a, a + w), 1.0, 0.0, qs)
+        tt(R("wk", 2 * o, 2 * o + w), R("pa1", o, o + w), B(bank + 1, a, a + w), ALU.mult)
+        ts(R("wk", 2 * o + w, 2 * o + 2 * w), R("wk", 2 * o, 2 * o + w), 5, ALU.arith_shift_right, H - 1, ALU.bitwise_and)
+        tt(R("wk", 2 * o, 2 * o + w), R("wk", 2 * o + w, 2 * o + 2 * w), B(bank + 1, a, a + w), ALU.add)
+        cp(R(out, o, o + w), R("wk", 2 * o, 2 * o + w))
+
+    ring = {"ga": 0, "ps": 0, "na": 0}
+
+    def take(name, size):
+        a = ring[name] % size
+        ring[name] = a + 1
+        return a
+
+    def look(offs, c0, bias, shift, lo, bank, first, banks, who, at=0):
+        a, o = 2048 * take("ga", NG // 2), take("na", NN)
+        js = (take("ps", banks), take("ps", banks))
+        for i in range(2):
+            q = who[(c0 + lo) // 64 + i]
+            by = R(offs, c0 + lo + 64 * i, c0 + lo + 64 * i + 64)
+            if offs == "ixr" and q == "v":
+                by = (by[0], R(offs)[1]) + by[2:]
+            lin(R("ga", a + 1024 * i, a + 1024 * i + 1024), ind(tab, by), 1.0, bias, q)
+        pack(js, "ga", a, shift)
+        for h in range(2):
+            tt(words("na", o, h), B(js[h], 0, 384), words("pk", lo // 128, h), ALU.not_equal)
+        out = B(bank, at + lo, at + lo + 128)
+        group([(out, l, R(nm, c + lo, c + lo + 128)) for l, nm, c in first]
+              + [(out, X("na", 2 * o, 2 * o + 2, T.na[:, 48 * o + 8 * w:48 * o + 8 * w + 8, :], 128), R("big")) for w in range(6)])
+
+    for t in range(RO):
+        last = t == RO - 1
+        if t == 0:
+            first = []
+        else:
+            c0 = 256 * (t - 1)
+            ts(R("cov", c0, c0 + 256), R("ixo"), float(HT), ALU.is_lt)
+            first = [(idn, "cov", c0)]
+            tt(R("pg"), ind(R("cov", c0, c0 + 256), R("pl")), R("mk"), ALU.mult)
+            group([(B(6, 0, 256), idn, R("kr")), (B(6, 0, 256), R("bon", 0, 128), R("pg", 0, 256)),
+                   (B(6, 0, 256), R("bon", 128, 256), R("pg", 256, 512))])
+            red(C("nm", 0), B(6, 0, 256), ALU.max, True)
+            ts(C("ko", 0), C("nm", 0), 0.0, ALU.min, 256.0, ALU.add)
+            cp(R("dg"), ind(R("dd"), C("ko", 0)))
+        ts(R("dm"), R("m4"), C("dg", 0), ALU.mult)
+        ts(R("dmf"), R("m4"), C("dg", 0), ALU.mult, -1.0, ALU.mult)
+        for j, l in enumerate((R("we", 0, 128), R("we", 128, 256), R("eq"))):
+            group([(B(7, 4 * j, 4 * j + 4), l, R("dm"))])
+        ts(R("qf", 0, 8), B(7, 0, 8), -2.0 ** -12, ALU.mult, KB, ALU.add)
+        ts(R("qf", 8, 12), B(7, 8, 12), -127.0, ALU.add)
+        ts(R("q", 0, 1024, 256), B(7, 8, 12), -1.0, ALU.mult, -127.0, ALU.add)
+        ts(R("q", 1, 1024, 256), B(7, 0, 4), 2.0 ** -12, ALU.mult, KB, ALU.add)
+        ts(R("q", 2, 1024, 256), B(7, 4, 8), 2.0 ** -12, ALU.mult, KB, ALU.add)
+        cp(R("q", 3, 1024, 256), R("dm"))
+        for hh in range(2):
+            shifted(PB[hh], (2 * hh, 2 * hh + 1), 1024 * hh)
+        for hh in range(2):
+            for a, w in (((0, 256), (256, 256)) if (t, hh) in SINGLY else ((0, 512),)):
+                placed(PB[hh], a, w, 512 * hh + a)
+        if t > 0:
+            for j in range(2):
+                lin(X("y%d" % t, j, j + 1, T["y%d" % t][:, j, :], 256), R("cov", c0, c0 + 256), C("ce", 13 + j))
+        if last:
+            turn(6, ("y1", "y2"))
+            lin(R("zf"), B(6, 0, 256))
+        ring["ps"] = 0
+        if t == 0:
+            for h in range(2):
+                turned(512 + 512 * h, 128, lambda j: B(7, 256 * j + 128 * h - 512, 256 * j + 128 * h - 384), (2, 3))
+            centred(1, 0, 256, B(7))
+
+        def fit(d):
+            relu(R("ft", 256 * d, 256 * d + 256), B(6 + d // 2, 256 * (d % 2), 256 * (d % 2) + 256), -2.0, 1.0, C("cl", 4 * t + d))
+
+        for d in range(n):
+            for lo in (0, 128):
+                if (d, lo) == (3, 128):
+                    fit(2)
+                look("ix", 256 * d, C("qf", 8 + d), 1, lo, 6 + d // 2, first, 6, FORTH, 256 * (d % 2))
+            if d == 1:
+                fit(0)
+            if d % 2:
+                fit(d)
+        cl = R("cl", 4 * t, 4 * t + 4)
+        top, base = C("mx", t), C("mx", 4 + t)
+        group([(B(6, 0, 4), R("bow"), R("tie")), (B(6, 0, 4), R("bow"), cl)])
+        group([(B(6, 4, 8), R("bow"), cl)])
+        red(top, B(6, 0, 4), ALU.max)
+        red(base, B(6, 4, 8), ALU.max)
+        ts(R("so"), R("i16"), base, ALU.subtract, top, ALU.add)
+        cp(R("qw"), ind(R("q"), C("so", 0)))
+        relu(C("yt", 0), base, -1.0, 1.0)
+        lin(C("yt", 1), base, 1.0 / 1024, 0.0, "a")
+        lin(C("yt", 2), base, 1.0 / 256, 3.0, "a")
+        lin(C("yt", 3), top, -1.0 / 256, C("yt", 2), "a")
+        lin(C("yws", 8 * rank + t), C("yt", 0), -1.0, C("yt", 3), "a")
+        lin(C("yws", 8 * rank + t + 3), C("yt", 0), -1.0, C("yt", 1), "a")
+        for a, b in RESTS:
+            w, bank = b - a, 2 * (a // 128)
+            lin(R("ndb", a, b), R("elv", 0, w), 0.0, C("qw", 3), "a")
+            for u in range(2):
+                ts(R("kk", 256 * u + a, 256 * u + b), U(2 + u, a, b), 2.0 ** -12, ALU.mult, C("qw", 1 + u), ALU.add)
+                group([(B(bank + u, 0, w), R("cid"), R("elv", 0, w)), (B(bank + u, 0, w), R("idh"), U(2 + u, a, b)),
+                       (B(bank + u, 0, w), R("we", 128 * u, 128 * u + 128), R("ndb", a, b)),
+                       (B(bank + u, 0, w), R("m4k"), R("kk", 256 * u + a, 256 * u + b))])
+            placed(bank, 0, w, a, "ixr", "a")
+        if last:
+            lin(R("fw"), ind(R("ft"), R("so")))
+            first = [(R("hn"), "fw", 0), (R("hn"), "cov", c0)]
+            wins = R("yws", 8 * rank, 8 * rank + 6)
+            lands([R("yws", 8 * r, 8 * r + 6) for r in others], "yw", ke * (n - 1),
+                  send([(wins, off, "yw", [(T.cores[r], wins) for r in others])]))
+        else:
+            lin(R("fw"), ind(R("ft"), R("so")), -BIG, BIG)
+            first = [(R("idf"), "slp", 0)]
+            group([(B(7, 0, 256), R("idf"), R("slp")), (B(7, 0, 256), idn, R("fw"))])
+            tt(R("km"), B(7, 0, 256), R("xo"), ALU.min)
+        ring["ps"] = 0
+        for lo in (0, 128):
+            look("ixr", 0, C("qw", 0), 2, lo, 4 + lo // 128, first, 4, WHO)
+        if not last:
+            for a in (0, 128):
+                tt(R("xo", a, a + 128), B(4 + a // 128, a, a + 128), R("km", a, a + 128), ALU.min)
+                cp(R("ixo", a, a + 128), R("xo", a, a + 128))
+                scatter(R("tab"), R("ixo", a, a + 128), R("zr"))
+
+    for hh in range(2):
+        for j in range(2):
+            a = 128 * hh
+            ts(X("y3", 2 * hh + j, 2 * hh + j + 1, T.y3[:, j, a:a + 128], 128), B(4 + hh, a, a + 128), 0.5, ALU.is_lt, C("cg", 8 + j), ALU.mult)
+    turn(6, ("y3",))
+    tt(R("yo"), B(6, 0, 256), R("zf"), ALU.subtract)
+    halves = [thirds[0], thirds[1] | thirds[2], off]
+    for js in ((0, 1), (2,)):
+        back = send([(R("yo", 64 * others[j], 64 * others[j] + 64), halves[j], "yc%d" % rank,
+                      [(T.cores[others[j]], R("yl", 64 * rank, 64 * rank + 64))]) for j in js])
+    for r in range(n):
+        dma("s", hbm(T.yw[2 * r:2 * r + 2, :]), X("yws", 8 * r, 8 * r + 6, T.yws[0:32:16, 8 * r:8 * r + 6], 6), "st", 128)
+    dma("s", hbm(T.yc[2 * rank:2 * rank + 2, :]), R("yo", 64 * rank, 64 * rank + 64), "st", 128)
+    for j, r in enumerate(others):
+        lands([R("yl", 64 * r, 64 * r + 64)], "yc%d" % r, count(halves[2 - j]), back)
+        dma("sa"[j % 2], hbm(T.yc[2 * r:2 * r + 2, :]), R("yl", 64 * r, 64 * r + 64), "st", 128)
+
+    cnt = {"v": 0, "a": 0, "p": 0, "g": 0}
+    seen = {k: {} for k in Q}
+    log = {}
 
     def wait(q, sem, val):
         if seen[q].get(sem, 0) < val:
             Q[q].wait_ge(T.sem[sem], val)
             seen[q][sem] = val
 
-    def order(q, reads, writes):
-        need = {}
-        for regs, w in ((reads, False), (writes, True)):
-            for name, lo, hi in regs:
-                ps = name.startswith("ps")
-                for a, b, ew, tok in log.get(name, []):
-                    if a < hi and lo < b and (w or ew or (ps and tok[2] != q)) and not (q == "p" and tok[2] == "p"):
-                        need[tok[0]] = max(need.get(tok[0], 0), tok[1])
-        for sem, val in need.items():
-            wait(q, sem, val)
-
-    def note(reads, writes, tok):
-        for name, lo, hi in writes:
-            log[name] = [e for e in log.get(name, []) if not (lo <= e[0] and e[1] <= hi)] + [(lo, hi, True, tok)]
-        for name, lo, hi in reads:
-            log[name] = [e for e in log.get(name, []) if not (not e[2] and e[3][0] == tok[0] and lo <= e[0] and e[1] <= hi)]
-            log[name].append((lo, hi, False, tok))
-
-    def op(q, call, outs, ins):
-        reads = [r for x in ins if isinstance(x, tuple) for r in x[1]]
-        writes = [r for x in outs for r in x[1]]
-        order(q, reads, writes)
-        cnt[q] += 1
-        call().then_inc(T.sem["c" + q], 1)
-        note(reads, writes, ("c" + q, cnt[q], q))
-
-    def ap(x):
-        return x[0] if isinstance(x, tuple) else x
-
-    def cp(out, a):
-        op("v", lambda: g.vector.tensor_copy(out[0], a[0]), [out], [a])
-
-    def tt(out, a, b, o):
-        op("v", lambda: g.vector.tensor_tensor(out[0], a[0], b[0], o), [out], [a, b])
-
-    def ts(out, a, s1, o1, s2=None, o2=None):
-        if o2 is None:
-            op("v", lambda: g.vector.tensor_scalar(out[0], a[0], ap(s1), None, o1), [out], [a, s1])
+    for i, q in arrange(calls):
+        c = calls[i]
+        if q != "x":
+            need = {}
+            for sem, val in meets(log, c["reads"], c["writes"], q):
+                if not (q == "p" and sem == "cp"):
+                    need[sem] = max(need.get(sem, 0), val)
+            for sem, val in need.items():
+                wait(q, sem, val)
+            made = c["make"](q)
+        if c["sem"] == "far":
+            continue
+        if c["sem"] is None:
+            cnt[q] += 1
+            tok = ("c" + q, cnt[q])
+            made.then_inc(T.sem[tok[0]], 1)
         else:
-            op("v", lambda: g.vector.tensor_scalar(out[0], a[0], ap(s1), ap(s2), o1, o2), [out], [a, s1, s2])
-
-    def ms(out, val):
-        op("v", lambda: g.vector.memset(out[0], val), [out], [])
-
-    def red(out, a, o, neg=False):
-        op("v", lambda: g.vector.tensor_reduce(out[0], a[0], AX.X, o, negate=neg), [out], [a])
-
-    def act(out, a, f, bias=0.0, scale=1.0, acc=None):
-        if acc is None:
-            op("a", lambda: g.scalar.activation(out[0], a[0], f, ap(bias), scale), [out], [a, bias])
-        else:
-            op("a", lambda: g.scalar.activation(out[0], a[0], f, ap(bias), scale, accum_out=acc[0]), [out, acc], [a, bias])
-
-    def scatter(win, offs, src):
-        op("a", lambda: g.scalar.activation(win[0].indirect(offs[0]), src[0], AF.Silu), [win], [offs, src])
-
-    def mm(out, l, r, start, stop):
-        op("p", lambda: g.tensor.matmul(out[0], l[0], r[0], start, stop), [out], [l, r])
-
-    def iota(out, pat, base, cm, loose=False):
-        if loose:
-            op("g", lambda: g.iota(out[0], pat, base, cm, allow_small_or_imprecise_dtypes=True), [out], [])
-        else:
-            op("g", lambda: g.iota(out[0], pat, base, cm), [out], [])
-
-    def load(q, out, src, sem, total):
-        Q[q].dma_start(out[0], src).then_inc(T.sem[sem], 16)
-        note([], out[1], (sem, total, "dma"))
-
-    def lands(reg, sem, total):
-        note([], reg[1], (sem, total, "far"))
-
-    def send(src, parts):
-        order("g", src[1], [])
-        g.remote_dma_fused([RemoteDMATransfer(dst_ids=[dst(c, topo) for c, _ in to], dma_engine_mask=m,
-                                              remote_sem=T.sem[sem], srcs=[src[0]], dsts=[d[0] for _, d in to])
-                            for m, sem, to in parts], local_sem=T.sem.sent)
-        sent[0] += sum(count(m) for m, _, _ in parts)
-
-    ke = count(off)
-    for c in range(4):
-        via = helper_of(pred, T, topo) if c in (0, 2) else pred
-        lands(R("xp", 1024 * c, 1024 * c + 1024), "xp%d" % c, count(topo.mask(via, core)))
-    lands(R("xq", 0, 3072), "xq", count(topo.mask(helper_of(succ, T, topo), core)))
-    lands(R("xq", 3072, V), "xq3", ke)
-
-    for c in range(4):
-        load("s", R("xi", 1024 * c, 1024 * c + 1024), T.x[:, 1024 * c:1024 * c + 1024], "ld%d" % c, 16)
-    load("a", R("wi", 0, 1), T.w1[:], "ldw", 32)
-    load("a", R("wi", 1, 2), T.w2[:], "ldw", 32)
-    load("a", R("pab", 0, 16), T.pb[:], "ldp", 32)
-    load("a", R("pab", 16, 32), T.pa[:], "ldp", 32)
-
-    ms(R("tab", 0, 512), 0.0)
-    ms(R("tab", 512, 2048), 0.0)
-    iota(R("ri"), [[1, 144]], 0, 0, True)
-    iota(R("i1", 0, 3), [[-11, 3]], 33, 11)
-    iota(R("i1", 3, 4), [[0, 1]], 0, 1)
-    iota(R("rg"), [[16, 8], [0, 16]], 0, 0, True)
-    fill = [2048]
-
-    def zero(q, w):
-        a = fill[0]
-        fill[0] += w
-        if q == "g":
-            iota(R("tab", a, a + w), [[0, w]], 0, 0, True)
-        elif q == "v":
-            ms(R("tab", a, a + w), 0.0)
-        else:
-            act(R("tab", a, a + w), R("tab", 0, w), AF.Identity)
-
-    zero("g", 2048)
-    for w in (512, 512, 512, 2048, 2048, 2048, 2048):
-        zero("a", w)
-    ts(R("j1", 0, 4), R("i1"), 15, ALU.bitwise_and)
-    ts(R("j1", 4, 5), R("i1", 3, 4), 112, ALU.bitwise_and)
-    cp(R("cf", 0, 5), R("j1", 0, 5))
-    pm, g16, me = C("cf", 3), C("cf", 4), C("cg", 3)
-    ts(C("ce", 0), g16, 15.0, ALU.add)
-    zero("v", 2048)
-    cp(R("wf", 0, 2), R("wi", 0, 2))
-    for u, w in ((0, "w1s"), (1, "w2s")):
-        ts(R(w), R("ri"), C("ce", 0), ALU.is_equal, C("wf", u), ALU.mult)
-
-    def slide(u, k):
-        return R(("w1s", "w2s")[u], 15 - k, 143 - k)
-
-    for c in range(4):
-        part = R("xb", 1024 * c, 1024 * c + 1024)
-        cp(part, R("xi", 1024 * c, 1024 * c + 1024))
-        parts = [(near, "h%d" % c, [(helper, part)])] if c < 3 else []
-        if c in (1, 3):
-            parts.append((off, "xp%d" % c, [(succ, R("xp", 1024 * c, 1024 * c + 1024))]))
-        send(part, parts)
-        zero("v", 1024 if c < 3 else 512)
-        for k in range(4 * c, 4 * c + 4):
-            for u in range(2):
-                mm(R("psS%d" % u, 0, 256), slide(u, k), R("xb", 256 * k, 256 * k + 256), k == 0, k == 15)
-    send(R("xb", 3072, V), [(off, "xq3", [(pred, R("xq", 3072, V))])])
-    zero("g", HT - fill[0])
-    iota(R("kr"), [[-1, 256]], 256, 0, True)
-    for k in range(16):
-        act((T.xf[:, k:V:16], [("xf", 256 * k, 256 * k + 256)]), R("xb", 256 * k, 256 * k + 256), AF.Identity, 128.0)
-
-    def places(out, w):
-        ts(R("tb", 0, 2 * w), R("ta", 0, 2 * w), 4095, ALU.bitwise_and)
-        tt(R("tm", 0, w), R("tb", 0, w), R("tb", w, 2 * w), ALU.mult)
-        ts(R("tn", 0, w), R("tm", 0, w), 5, ALU.arith_shift_right, H - 1, ALU.bitwise_and)
-        tt(out, R("tn", 0, w), R("tb", w, 2 * w), ALU.add)
-
-    cp(R("ta", 0, 256), R("psS0", 0, 256))
-    cp(R("ta", 256, 512), R("psS1", 0, 256))
-    places(R("slp"), 256)
-    cp(R("ixo"), R("slp"))
-    scatter(R("tab", 0, HT), R("ixo"), R("xf"))
-
-    def cell(j, k=1):
-        return (T.mm[:, 8 * j:8 * (j + k), :], [("mm", j, j + k)])
-
-    def pack(ps, src, cells=range(NC), odd=0, minus=None):
-        for j, (c, b, lo, hi) in enumerate(CELLS):
-            if j in cells:
-                out = R(ps, AT[odd][b], AT[odd][b] + 256)
-                if minus is not None and j >= NC - 2:
-                    mm(out, cell(j + 2), R(minus, 2048 + 256 * c, 2304 + 256 * c), False, False)
-                mm(out, cell(j), R(src, 256 * c, 256 * c + 256), lo == 0, hi == 16)
-
-    def sums(ps, o, src, a, b):
-        for u in range(2):
-            for k in range(16):
-                mm(R(ps, o + 256 * u + a // 16, o + 256 * u + b // 16), slide(u, k), R(src, a + k, b, 16), k == 0, k == 15)
-
-    def centred(out, ps):
-        cp(R("ta", 0, 512), ps)
-        ts(R("tb", 0, 512), R("ta", 0, 512), 4095, ALU.bitwise_and)
-        ts(R(out), R("tb", 0, 512), -2048.0, ALU.add)
-
-    sums("psA", 1024, "xp", 0, 2048)
-    sums("psA", 1024, "xp", 2048, 3072)
-    sums("psA", 1024, "xp", 3072, V)
-
-    ts(R("cg", 0, 4), R("cf", 0, 4), g16, ALU.add)
-    cp(R("po"), R("pab"))
-    for r, nm_ in enumerate(("fa", "fb", "fc")):
-        ts(R(nm_), R("ri", 0, 128), C("cg", r), ALU.is_equal, float(256 ** r), ALU.mult)
-    cp(R("xbb"), ind(R("xb"), R("po", 0, 16)))
-    ms(cell(0, NC), 0.0)
-    tt(R("idn"), R("fa"), R("fb"), ALU.add)
-    ms(R("dd", 256, 272), NONE)
-    tt(R("fm"), R("idn"), R("fc"), ALU.add)
-    for u, w in ((0, "w1b"), (1, "w2b")):
-        ts(R(w), R("rg"), g16, ALU.is_equal, C("wf", u), ALU.mult)
-    f3 = [("f3", 0, 1)]
-    cp((T.f3[:], f3), R("fm"))
-    ms(R("elv"), 11.0)
-    ts(R("idh"), R("ri", 0, 128), me, ALU.is_equal)
-    ts(R("m4k"), R("ri", 0, 128), me, ALU.is_equal, -4096.0, ALU.mult)
-    ts(R("cid"), R("ri", 0, 128), me, ALU.is_equal, 35.0 * 2048, ALU.mult)
-    for j, (c, b, lo, hi) in enumerate(CELLS):
-        cp((T.mm[:, 8 * j:8 * j + 8, lo:hi], [("mm", j, j + 1)]), (T.f3[:, :, lo:hi], f3))
-    pack("psB", "xp")
-
-    def for_totals():
-        ts(C("ce", 1), pm, -2.5, ALU.add)
-        ms(R("q"), 0.0)
-        ts(R("tci", 0, 3), R("ri", 0, 48, 16), C("ce", 1), ALU.add, 1.0 / 6, ALU.mult)
-        ts(R("idn"), R("ri", 0, 128), me, ALU.is_equal)
-        ts(R("tcf", 0, 3), R("tci", 0, 3), g16, ALU.add, 8.0, ALU.add)
-        ts(R("pkp", 256, 1024), R("psB", 0, 768), ONE, ALU.add)
-        ts(R("pkp", 0, 256), R("psB", 512, 768), ONE, ALU.add)
-        for b in range(3):
-            ts(R("gs", 144 * b, 144 * b + 136), R("ri", 0, 136), C("tcf", b), ALU.is_equal)
-
-    def for_winner():
-        ts(R("bow"), R("rg"), g16, ALU.is_equal, 512.0, ALU.mult)
-        ts(R("tie"), R("ri", 0, 4), 1.0 / 64, ALU.mult)
-        ts(R("q", 4, 512, 128), R("ri", 0, 4), 256.0, ALU.mult)
-        ts(R("i16"), R("ri", 0, 16), 16.0, ALU.mult, pm, ALU.add)
-        ts(cell(NC, 2), cell(NC - 2, 2), -1.0, ALU.mult)
-
-    def for_pairs():
-        ts(R("pt"), R("pab"), 8, ALU.arith_shift_right)
-        ts(R("em"), R("ri", 0, 16), pm, ALU.is_equal)
-        cp(R("ph"), R("pt"))
-        ts(C("ce", 3), pm, 256.0, ALU.mult, HT - 1.0, ALU.add)
-        ts(R("pt"), R("pab"), 255, ALU.bitwise_and)
-        cp(R("mk"), ind(R("em"), R("ph")))
-        ts(R("dmy"), R("kr"), C("ce", 3), ALU.add)
-        cp(R("pl", 0, 16), R("pt", 0, 16))
-        ts(R("pl", 16, 32), R("pt", 16, 32), 256.0, ALU.add)
-        ts(R("bon"), R("rg"), g16, ALU.is_equal, -1.0, ALU.mult)
-
-    tab = R("tab", 0, HT)
-
-    def shifted(ps, us, kb, sign, ds, w, k0):
-        for e, d in enumerate(ds):
-            a = k0 // 2 + w * e
-            ts(R("ndb", a, a + w), R("elv", 0, w), 0.0, ALU.mult, C("ndf", d), sign)
-        for u in range(2):
-            for e, d in enumerate(ds):
-                a = k0 + 512 * u + w * e
-                ts(R("kk", a, a + w), R(us, 256 * u, 256 * u + w), 2.0 ** -12, ALU.mult, C("qf", kb + 4 * u + d), ALU.add)
-            mm(R(ps, 512 * u, 512 * u + 512), R("cid"), R("elv"), True, False)
-            for e in range(len(ds)):
-                mm(R(ps, 512 * u + w * e, 512 * u + w * e + w), R("idh"), R(us, 256 * u, 256 * u + w), False, False)
-            mm(R(ps, 512 * u, 512 * u + 512), R(("w1b", "w2b")[u]), R("ndb", k0 // 2, k0 // 2 + 512), False, False)
-            mm(R(ps, 512 * u, 512 * u + 512), R("m4k"), R("kk", k0 + 512 * u, k0 + 512 * u + 512), False, True)
-
-    def placed(out, ps):
-        cp(R("tb", 0, 512), R(ps, 0, 512))
-        tt(R("tm", 0, 512), R("tb", 0, 512), R(ps, 512, 1024), ALU.mult)
-        ts(R("tn", 0, 512), R("tm", 0, 512), 5, ALU.arith_shift_right, H - 1, ALU.bitwise_and)
-        tt(out, R("tn", 0, 512), R(ps, 512, 1024), ALU.add)
-
-    def gather_a(buf, offs, o, bias, lo, hi):
-        act(R(buf, lo, hi), ind(tab, R(offs, o + lo // 16, o + hi // 16)), AF.Identity, bias)
-
-    def gather_b(buf, offs, o, notes, lo, hi):
-        tt(R(buf, lo, hi), ind(tab, R(offs, o + 128 + lo // 16, o + 128 + hi // 16)), R(notes, 2048 + lo, 2048 + hi), ALU.subtract)
-
-    def total(ps, j, cov):
-        at = [a % 768 for a in AT[j]]
-        steps = [(R("gs", 144 * b + 8, 144 * b + 136), R("na%d" % j, at[b], at[b] + 256)) for b in range(3)]
-        steps += [(R("gs", 144 * b, 144 * b + 128), R("nb%d" % j, at[b], at[b] + 256)) for b in range(3)]
-        steps = [steps[i] for i in (0, 1, 3, 4, 2, 5)]
-        if cov is not None:
-            steps = [(R("idn"), cov)] + steps
-        for i, (l, r) in enumerate(steps):
-            mm(R(ps, 0, 256), l, r, i == 0, i == len(steps) - 1)
-
-    for t in range(RO):
-        last = t == RO - 1
-        o0 = 64 * t
-        mine = o0 + 16 * (n - 1 - rank)
-        if t == 0:
-            tt(R("dd", 0, 256), ind(R("xp"), R("po", 16, 32)), R("xbb"), ALU.subtract)
-            cp(R("ofl", mine, mine + 2), R("dd", 0, 2))
-            cov = None
-        else:
-            s0 = 512 * (t - 1)
-            tt(R("kl"), R("kd"), R("il", s0, s0 + 256), ALU.subtract)
-            tt(R("km"), R("kl"), R("slp"), ALU.max)
-            cp(R("ixo"), R("km"))
-            scatter(R("tab"), R("ixo"), R("xf"))
-            tt(R("pg", 512, 1024), ind(R("il", s0, s0 + 512), R("pl")), R("mk"), ALU.mult)
-            mm(R("psS0", 0, 256), R("idn"), R("kr"), True, False)
-            for j in range(4):
-                mm(R("psS0", 0, 256), R("bon"), R("pg", 256 * j, 256 * j + 256), False, j == 3)
-            red(C("nm", 0), R("psS0", 0, 256), ALU.max, True)
-            ts(C("ko", 0), C("nm", 0), 0.0, ALU.min, 256.0, ALU.add)
-            cp(R("ofl", mine, mine + 16), ind(R("dd"), C("ko", 0)))
-        slot = R("ofl", mine, mine + 2)
-        send(slot, [(off, "of%d" % t, [(c, slot) for c in others])])
-        for j in range(n):
-            if 16 * j + o0 != mine:
-                lands(R("ofl", o0 + 16 * j, o0 + 16 * j + 2), "of%d" % t, ke * (n - 1))
-        if t == 0:
-            centred("up", R("psA", 1024, 1536))
-            for_totals()
-        else:
-            cov = R("ind", s0 + 256, s0 + 512)
-            tt(R("ind", s0, s0 + 512), R("pre"), R("il", s0, s0 + 512), ALU.max)
-        nd = R("ofl", o0, o0 + 64, 16)
-        for j, l in enumerate(("w1b", "w2b", "fm")):
-            mm(R("psS1", 256 + 4 * j, 260 + 4 * j), R(l), nd, True, True)
-        cp(R("ndf"), nd)
-        ts(R("qf", 0, 8), R("psS1", 256, 264), -2.0 ** -12, ALU.mult, KB, ALU.add)
-        shifted("psA", "up", 0, ALU.subtract, (0, 1), 256, 0)
-        ts(R("qf", 8, 12), nd, -127.0, ALU.add)
-        shifted("psB", "up", 0, ALU.subtract, (2, 3), 256, 1024)
-        ts(R("q", 3, 512, 128), R("psS1", 264, 268), -1.0, ALU.mult, -128 * ONE, ALU.add)
-        ts(R("q", 0, 512, 128), nd, -1.0, ALU.mult, -127.0, ALU.add)
-        ts(R("q", 1, 512, 128), R("psS1", 256, 260), 2048.0, ALU.add)
-        ts(R("q", 2, 512, 128), R("psS1", 260, 264), 2048.0, ALU.add)
-        ts(R("qf", 12, 16), R("psS1", 264, 268), -128 * ONE, ALU.add)
-        ts(R("qf", 16, 24), R("psS1", 256, 264), 2.0 ** -12, ALU.mult, KB, ALU.add)
-        if t == 0:
-            sums("psS1", 0, "xq", 0, V)
-        for h, ps in enumerate(("psA", "psB")):
-            placed(R("tm", 0, 512), ps)
-            cp(R("ix", 512 * h, 512 * h + 512), R("tm", 0, 512))
-        if t == 0:
-            iota(R("xf"), [[0, V]], 0, 0, True)
-
-        def pk(d, cells):
-            pack("psA", "ga%d" % (d % 2), cells, d % 2)
-            pack("psB", "gb%d" % (d % 2), cells, d % 2)
-
-        def look(d, lo, hi, cells):
-            gather_a("ga%d" % (d % 2), "ix", 256 * d, C("qf", 8 + d), lo, hi)
-            gather_b("gb%d" % (d % 2), "ix", 256 * d, "xp", lo, hi)
-            pk(d, cells)
-
-        def chk(d, lo=0, hi=768):
-            j = d % 2
-            tt(R("na%d" % j, lo, hi), R("psA", 768 * j + lo, 768 * j + hi), R("pkp", 256 - 256 * j + lo, 256 - 256 * j + hi), ALU.not_equal)
-            act(R("nb%d" % j, lo, hi), R("psB", 768 * j + lo, 768 * j + hi), AF.Abs, C("qf", 12 + d))
-
-        def tot(d):
-            total("psS%d" % (d % 2), d % 2, cov)
-
-        def fin(d):
-            act(R("ft", 256 * d, 256 * d + 256), R("psS%d" % (d % 2), 0, 256), AF.Relu, 1.0, -2.0, C("cl", 16 * t + 4 * rank + d))
-
-        for d in range(n):
-            look(d, 0, 1536, range(7))
-            if d > 1:
-                fin(d - 2)
-            if d > 0:
-                chk(d - 1)
-            if t == 0 and d == 1:
-                centred("uq", R("psS1"))
-            pk(d, (7,))
-            if d > 0:
-                tot(d - 1)
-            look(d, 1536, 2048, (8, 9))
-            if t == 0 and d == 2:
-                for_winner()
-        chk(3, 256, 768); chk(3, 0, 256); fin(2); tot(3); fin(3)
-        c0 = 16 * t
-        own = R("cl", c0 + 4 * rank, c0 + 4 * rank + 4)
-        send(own, [(off, "cn%d" % t, [(c, own) for c in others])])
-        for j in range(n):
-            if j != rank:
-                lands(R("cl", c0 + 4 * j, c0 + 4 * j + 4), "cn%d" % t, ke * (n - 1))
-        shifted("psB", "uq", 16, ALU.add, range(n), 128, 0)
-        if t == 0:
-            pack("psA", "xq")
-            act(R("pkq"), R("psA", 0, 768), AF.Identity, ONE)
-        placed(R("sp", 0, 512), "psB")
-        mm(R("psS0", 0, 4), R("bow"), R("tie"), True, False)
-        for i, j in enumerate([rank] + [j for j in range(n) if j != rank]):
-            mm(R("psS0", 0, 4), R("bow"), R("cl", c0 + 4 * j, c0 + 4 * j + 4), False, i == n - 1)
-        red(C("mx", t), R("psS0", 0, 4), ALU.max)
-        ts(R("wz", 8 * t, 8 * t + 8), R("i16", 0, 8), C("mx", t), ALU.add)
-        ts(R("wy"), R("wz", 8 * t, 8 * t + 8), 511, ALU.bitwise_and)
-        cp(R("so"), R("wy"))
-        cp(R("ixr", 0, 128), ind(R("sp", 0, 512), R("so")))
-        cp(R("qw"), ind(R("q"), C("so", 0)))
-        s0 = 512 * t
-        mark = 3.0 if last else BIG
-        fit = R("fs", s0 + 256, s0 + 512)
-        for u in range(2):
-            a = 256 * u + 128
-            ts(R("ta", 128 * u, 128 * u + 128), R("uq", a, a + 128), C("qw", 1 + u), ALU.add)
-        ts(R("fo"), R("i16"), C("qw", 4), ALU.add)
-        places(R("tm", 0, 128), 128)
-        cp(R("ixr", 128, 256), R("tm", 0, 128))
-        gather_a("ga0", "ixr", 0, C("qw", 0), 0, 1024)
-        pack("psA", "ga0", range(5))
-        act(fit, ind(R("ft"), R("fo")), AF.Identity, 0.0, mark)
-        send(fit, [(off, "ff%d" % t, [(pred, R("fs", s0, s0 + 256))])])
-        lands(R("fs", s0, s0 + 256), "ff%d" % t, ke)
-        gather_a("ga0", "ixr", 0, C("qw", 0), 1024, 2048)
-        pack("psA", "ga0", range(5, NC))
-        gather_a("gb0", "ixr", 128, 0.0, 1536, 2048)
-        gather_b("gb0", "ixr", 0, "xq", 0, 1024)
-        pack("psB", "gb0", range(5))
-        gather_b("gb0", "ixr", 0, "xq", 1024, 1536)
-        pack("psB", "gb0", range(5, NC), 0, "xq")
-        tt(R("na0"), R("psA", 0, 768), R("pkq"), ALU.not_equal)
-        act(R("nb0", 0, 512), R("psB", 0, 512), AF.Abs, C("qw", 3))
-        act(R("nb0", 512, 768), R("psB", 512, 768), AF.Abs, C("qw", 3))
-        total("psS1", 0, None)
-        img = R("it", 256 * t, 256 * t + 256)
-        act(img, R("psS1", 0, 256), AF.Relu, mark, -2.0 * mark)
-        to = [(succ, R("il", s0, s0 + 256))] + ([] if last else [(far, R("il", s0 + 256, s0 + 512))])
-        send(img, [(off, "fi%d" % t, to)])
-        lands(R("il", s0, s0 + 256 * len(to)), "fi%d" % t, ke * len(to))
-        if t == 0:
-            for_pairs()
-            cp(R("pre"), R("fs", 0, 512))
-        elif not last:
-            tt(R("pre"), R("ind", s0 - 512, s0), R("fs", s0, s0 + 512), ALU.max)
-        if not last:
-            tt(R("kd"), R("dmy"), R("pre", 0, 256), ALU.subtract)
-            tt(R("pg", 0, 512), ind(R("pre"), R("pl")), R("mk"), ALU.mult)
-
-    s0 = 512 * (RO - 1)
-    tt(R("ya"), R("ind", 0, 256), R("ind", 512, 768), ALU.add)
-    ts(R("yd"), R("ind", 512, 768), 3.0 / BIG, ALU.mult, -3.0, ALU.add)
-    ts(R("yb"), R("ya"), -1.0 / BIG, ALU.mult, 3.0, ALU.add)
-    ts(R("yi", 0, 3), R("wz", 0, 24, 8), 9, ALU.arith_shift_right)
-    tt(R("ya"), R("yb"), R("yd"), ALU.add)
-    ts(R("yi", 4, 7), R("wz", 0, 24, 8), 7, ALU.arith_shift_right, 3, ALU.bitwise_and)
-    ts(R("yt", 3, 6), R("yi", 0, 3), 1.0, ALU.add)
-    tt(R("yd"), R("ya"), R("fs", s0, s0 + 256), ALU.add)
-    ts(R("yt", 0, 3), R("yi", 4, 7), -1.0, ALU.mult, 4.0, ALU.add)
-    ts(R("yt", 8, 11), R("yi", 0, 3), 0.0, ALU.is_gt)
-    ts(R("yt", 11, 14), R("yi", 0, 3), 0.0, ALU.is_gt)
-    tt(R("yt", 0, 6), R("yt", 0, 6), R("yt", 8, 14), ALU.mult)
-    ts(R("yws", 0, 6), R("yt", 0, 6), -1.0, ALU.add)
-    order("s", R("yws")[1], [])
-    g.sync.dma_start(T.yw[:], T.yws[0:128:16, 0:6]).then_inc(T.sem.st, 16)
-    tt(R("ya"), R("yd"), R("il", s0, s0 + 256), ALU.max)
-    tt(R("yo"), R("ya"), R("yb"), ALU.min)
-    order("s", R("yo")[1], [])
-    g.sync.dma_start(T.yc[:], T.yo[:]).then_inc(T.sem.st, 16)
+            tok = c["sem"]
+            if q != "x":
+                made.then_inc(T.sem[tok[0]], 16)
+        enter(log, c["reads"], c["writes"], tok, q)
     for q in cnt:
         wait("s", "c" + q, cnt[q])
     g.sync.wait_ge(T.sem.sent, sent[0])
-    g.sync.wait_ge(T.sem.st, 32)
+    g.sync.wait_ge(T.sem.st, 128)

@@ -6,37 +6,46 @@ HT = H + V
 BIG = 32768.0
 ONE = 65793.0
 NONE = -512.0
-KB = 192.0 + 2.0 ** -13
-CHUNKS = ((0, 768), (768, 2048), (2048, 3072), (3072, 4096))
+KB = 191.5 + 2.0 ** -13
+ROUND = 1.5 * 2.0 ** 33
+CHUNKS = ((0, 1024), (1024, 2560), (2560, 4096))
+DIRECT = 1
+SEQ = (1, 0, 2)
+PARTS = ((0, 32), (32, 64), (64, 128), (128, 256))
 HALVES = ((0, 128), (128, 256))
-CAST = (0, 1, 2, 3)
-DEPTH = 2
-SLOW = 7
-STAGE = "a"
-CLEAR = [(512, "g")] * 6 + [(1024, "a")] * 14 + [(512, "v")] * 6
-FORTH = "avav" "aava" "avaa" "vava"
-WHO = "avaa"
-SINGLY = ((0, 0),)
-RESTS = ((0, 128), (128, 256))
+SLOW = 4
+CA = (512, 1024, 2048, 2048, 2048, 2048, 2048)
+CG = (1, 2, 1)
+EV = ("va", "v", "v")
+CB = 1024
+EVEN = [80, 80, 80, 80, 84, 84, 92]
+FORTH = [[96, 96] + EVEN[1:], [64] + EVEN, [64] + EVEN]
+WHO = [[64, 96], [64, 96], [64, 64]]
+CHECK = "v" * 16
+CHECKR = ("vvvv", "vvvv", "avav")
+LAG = 2
+RING = (0, 1, 4, 5, 2, 3)
+SINGLY = ((0, 0), (1, 0), (2, 0))
 PB = (0, 4)
 PASSES = 4
 NG, NN = 8, 3
-GATHER, SCATTER, PE, WAKE, ISSUE, FLIGHT, LOCAL = 1.56, 3.8, 0.5, 120, 700, 3000, 2600
+GATHER, SCATTER, PE, WAKE, ISSUE, FLIGHT, LOCAL = 1.56, 3.8, 0.5, 150, 600, 2400, 2200
 
 f32, bf, i32, u16, f16 = "float32", "bfloat16", "int32", "uint16", "float16"
 S_ = {
-    "tab": (HT + V, f32), "xi": (V, i32), "xs": (V, bf), "xb": (V, bf), "xf": (V, f32), "zr": (2048, f32),
-    "ga": (NG * 1024, bf), "kk": (2048, bf), "ndb": (1024, bf), "elv": (512, bf), "m4k": (128, bf), "cid": (128, bf),
-    "idh": (128, f16), "idf": (128, f32), "hn": (128, bf), "idw": (224, bf), "sel": (224, f16), "fsl": (64, bf),
+    "tab": (HT + V + 112, f32), "xi": (V, i32), "xs": (V, bf), "xb": (V, bf), "xf": (V, f32), "zr": (2048, f32),
+    "ga": (NG * 1024, bf), "kk": (2048, bf), "ndb": (512, bf), "elv": (512, bf), "m4k": (128, bf), "cid": (128, bf),
+    "idh": (128, f16), "idf": (128, f32), "nid": (128, f32), "hn": (128, bf), "idw": (224, bf), "sel": (224, f16),
+    "fsl": (512, bf), "y3": (256, bf), "rd": (1024, bf), "mo": (128, bf),
     "pw": (144, bf), "big": (128, bf), "neg": (128, bf), "ut": (1536, f32), "xo": (256, f32), "km": (256, f32), "slp": (256, f32),
     "pa1": (1024, f32), "ix": (1024, u16), "ixr": (256, u16), "ixo": (256, u16), "so": (16, u16),
     "wi": (40, i32), "pay": (160, f16), "wf": (8, f32), "pt": (96, i32), "po": (32, u16), "ph": (32, u16), "pl": (32, u16),
     "ri": (256, f32), "rm": (384, bf), "rg": (128, bf), "r32": (128, bf), "rb": (128, bf),
     "i1": (4, i32), "j1": (8, i32), "cf": (8, f32), "cg": (16, f32), "ce": (24, f32), "tci": (8, i32),
-    "wm": (48, bf), "wb": (256, bf), "we": (256, bf), "eq": (128, bf), "bon": (256, bf), "bow": (128, f32),
-    "em": (16, bf), "mk": (512, bf), "kr": (256, bf), "i16": (16, f32), "tie": (4, f32), "m4": (4, bf),
-    "xab": (576, bf), "dd": (272, bf), "pg": (512, bf), "nm": (2, f32), "ko": (2, u16), "dg": (16, f32), "dm": (4, bf), "dmf": (4, f32),
-    "q": (1024, f32), "qf": (16, f32), "qw": (16, f32), "cl": (12, f32), "mx": (8, f32),
+    "wm": (32, bf), "wb": (256, bf), "we": (256, bf), "lay": (896, bf), "eq": (128, bf), "bon": (256, bf), "bow": (128, f32),
+    "em": (16, bf), "mk": (512, bf), "kr": (256, bf), "i16": (16, f32), "tie": (4, f32), "m4": (16, bf), "kc": (12, f32),
+    "xab": (576, bf), "dd": (272, bf), "pg": (512, bf), "nm": (2, f32), "ko": (2, u16), "dm": (16, bf),
+    "qf": (16, f32), "qw": (16, f32), "cl": (12, f32), "mx": (8, f32),
     "ft": (1024, bf), "fw": (256, bf), "cov": (512, bf), "zf": (256, f32), "yo": (256, f32), "yl": (256, f32),
     "yt": (4, f32), "yws": (32, f32),
 }
@@ -44,16 +53,14 @@ SCRATCH = {k: ("sbuf", [128, v[0]], v[1]) for k, v in S_.items()}
 SCRATCH["us"] = ("sbuf", [128, 4, 256], f16)
 SCRATCH["pk"] = ("sbuf", [128, 96, 16], f32)
 SCRATCH["na"] = ("sbuf", [128, 48 * NN, 16], bf)
-for k_ in ("y1", "y2", "y3"):
-    SCRATCH[k_] = ("sbuf", [128, 2, 256], bf)
-for k_, (a_, b_) in enumerate(CHUNKS):
+for k_, (a_, b_) in list(enumerate(CHUNKS))[DIRECT:]:
     SCRATCH["st%d" % k_] = ("dram", [4, 128, (b_ - a_) // 4], bf)
     SCRATCH["dl%d" % k_] = ("dram", [4, 128, (b_ - a_) // 4], bf)
 SCRATCH["psA"] = ("psum", [128, 2048], f32)
 SCRATCH["psB"] = ("psum", [128, 2048], f32)
 
 SEMAPHORES = (["cv", "ca", "cp", "cg", "sent", "ldw", "st", "pay", "yw"]
-              + [s + str(k) for s in ("sg", "ld", "la", "ow", "re", "cf", "yc") for k in range(4)])
+              + [s + str(k) for s in ("sg", "ld", "la", "ow", "re", "yc") for k in range(4)])
 
 
 def count(mask):
@@ -143,10 +150,12 @@ def rank_program(g, core, T, topo):
     n = len(T.cores)
     others = [(rank + j) % n for j in range(1, n)]
     off, thirds = shares(core, [T.cores[r] for r in others], topo)
+    masks = [thirds[0], thirds[1] | thirds[2], off]
     ke = count(off)
     Q = {"v": g.vector, "a": g.scalar, "p": g.tensor, "g": g, "s": g.sync}
     calls = []
     sent = [0]
+    line, behind = [], []
     lead = [True]
 
     def R(name, a=0, b=None, s=1, m=128):
@@ -169,13 +178,17 @@ def rank_program(g, core, T, topo):
         t = T[name + str(k)]
         return (t[:], [(t.name, 0, n)], 0, bf, False) if r is None else (t[r], [(t.name, r, r + 1)], 0, bf, False)
 
-    def hbm(view, behind=()):
-        return (view, list(behind), 0, i32, False)
+    def hbm(view):
+        return (view, [], 0, i32, False)
 
     def ind(win, offs):
         return (win[0].indirect(offs[0]), win[1] + offs[1], 16 * offs[2], win[3], True)
 
     def call(cost, make, outs, ins, late=0, after=(), sem=None):
+        if lead[0] and "g" in cost:
+            after = tuple(after) + tuple(line)
+            line[:] = [len(calls)]
+        after = tuple(after) + tuple(behind)
         calls.append({"lead": lead[0], "cost": cost, "make": make, "late": late, "after": after, "sem": sem,
                       "reads": sorted({r for x in ins if isinstance(x, tuple) for r in x[1]}),
                       "writes": sorted({r for x in outs for r in x[1]})})
@@ -194,7 +207,7 @@ def rank_program(g, core, T, topo):
 
     def tt(out, a, b, o):
         two = not (a[1][0][0].startswith("ps") or b[1][0][0].startswith("ps"))
-        call({"v": cyc(out, a, 2.0 if two else 1.001)}, lambda q: g.vector.tensor_tensor(out[0], a[0], b[0], o), [out], [a, b])
+        return call({"v": cyc(out, a, 2.0 if two else 1.001)}, lambda q: g.vector.tensor_tensor(out[0], a[0], b[0], o), [out], [a, b])
 
     def ts(out, a, s1, o1, s2=None, o2=None):
         if o2 is None:
@@ -202,13 +215,13 @@ def rank_program(g, core, T, topo):
         else:
             call({"v": cyc(out, a)}, lambda q: g.vector.tensor_scalar(out[0], a[0], ap(s1), ap(s2), o1, o2), [out], [a, s1, s2])
 
-    def lin(out, a, scale=1.0, bias=0.0, qs="va"):
+    def lin(out, a, scale=1.0, bias=0.0, qs="va", after=()):
         def make(q):
             if q == "a":
                 return g.scalar.activation(out[0], a[0], AF.Identity, ap(bias), ap(scale))
             return g.vector.tensor_scalar(out[0], a[0], ap(scale), ap(bias), ALU.mult, ALU.add)
         cost = {"v": cyc(out, a), "a": 80 + (GATHER if a[4] else 1) * a[2]}
-        call({q: cost[q] for q in qs}, make, [out], [a, scale, bias])
+        call({q: cost[q] for q in qs}, make, [out], [a, scale, bias], 0, after)
 
     def relu(out, a, scale, bias, acc=None):
         def make(q):
@@ -217,29 +230,35 @@ def rank_program(g, core, T, topo):
             return g.scalar.activation(out[0], a[0], AF.Relu, bias, scale, accum_out=acc[0])
         call({"a": 100 + a[2]}, make, [out] + ([] if acc is None else [acc]), [a])
 
+    def size(out, a):
+        return call({"a": 80 + a[2]}, lambda q: g.scalar.activation(out[0], a[0], AF.Abs, 0.0, 1.0), [out], [a])
+
     def ms(out, val):
         call({"v": cyc(out, out)}, lambda q: g.vector.memset(out[0], val), [out], [])
 
     def red(out, a, o, neg=False):
         call({"v": cyc(out, a)}, lambda q: g.vector.tensor_reduce(out[0], a[0], AX.X, o, negate=neg), [out], [a])
 
-    def scatter(win, offs, src, first=0):
-        call({"a": 80 + SCATTER * src[2] + first}, lambda q: g.scalar.activation(win[0].indirect(offs[0]), src[0], AF.Silu), [win], [offs, src])
+    def scatter(win, offs, src):
+        call({"a": 80 + SCATTER * src[2]}, lambda q: g.scalar.activation(win[0].indirect(offs[0]), src[0], AF.Silu), [win], [offs, src])
 
-    def group(steps, apart=False):
+    def group(steps, apart=False, start=True, stop=True, after=()):
         def make(q):
             for i, (out, l, r) in enumerate(steps):
-                last = g.tensor.matmul(out[0], l[0], r[0], apart or i == 0, apart or i == len(steps) - 1)
+                last = g.tensor.matmul(out[0], l[0], r[0], apart or (start and i == 0), apart or (stop and i == len(steps) - 1))
             return last
-        call({"p": sum(12 + PE * max(64, r[2]) * (4 if r[3] == f32 else 1) for _, _, r in steps)}, make,
-             [s[0] for s in steps], [x for s in steps for x in s[1:]])
+        return call({"p": sum(12 + PE * max(64, r[2]) * (4 if r[3] == f32 else 1) for _, _, r in steps)}, make,
+                    [s[0] for s in steps], [x for s in steps for x in s[1:]], 0, after)
 
-    def iota(out, pat, base, cm):
+    def iota(out, pat, base, cm, once=()):
         def make(q):
             if out[3] == i32:
                 return g.iota(out[0], pat, base, cm)
             return g.iota(out[0], pat, base, cm, allow_small_or_imprecise_dtypes=True)
-        call({"g": 160 + 2 * out[2]}, make, [out], [])
+        call({"g": 160 + 2 * out[2]}, make, [out], list(once))
+
+    def widen(out, a):
+        call({"g": 200 + 2 * a[2]}, lambda q: g.affine_select(out[0], a[0], [[0, a[2]]], ALU.is_ge, 0.0, 0, 0), [out], [a])
 
     def dma(q, out, src, sem, total, late=LOCAL, hold=120):
         return call({q: hold}, lambda q: Q[q].dma_start(out[0], src[0]), [out], [src], late, (), (sem, total))
@@ -250,39 +269,54 @@ def rank_program(g, core, T, topo):
                                                   remote_sem=T.sem[sem], srcs=[src[0]], dsts=[d[0] for _, d in to])
                                 for src, m, sem, to in parts], local_sem=T.sem.sent)
         sent[0] += sum(count(p[1]) for p in parts)
-        return call({"g": ISSUE}, make, [], [p[0] for p in parts], FLIGHT + late, (), "far")
+        i = call({"g": ISSUE}, make, [], [p[0] for p in parts], 0, (), "far")
+        return call({"x": FLIGHT + late}, None, [], [], 0, (i,), "far")
 
     def lands(regs, sem, total, twin):
         call({"x": 1}, None, regs, [], -WAKE, (twin,), (sem, total))
 
     for a, b, src in ((0, 16, T.pa), (16, 17, T.w1), (17, 18, T.w2), (18, 34, T.pb)):
-        dma("a", R("wi", a, b), hbm(src[:]), "ldw", 64)
-    for k, (a, b) in enumerate(CHUNKS):
-        dma("s", R("xi", a, b), hbm(T.x[:, a:b], R("xi", *CHUNKS[k - DEPTH])[1] if k >= DEPTH else []), "ld%d" % k, 16, LOCAL, 2 * (b - a))
+        dma("s", R("wi", a, b), hbm(src[:]), "ldw", 64)
+    for k in SEQ:
+        a, b = CHUNKS[k]
+        w = (b - a) // 4
+        if k >= DIRECT:
+            dma("s", R("xi", a, b), hbm(T.x[:, a:b]), "ld%d" % k, 16, LOCAL, 2 * w)
+            continue
+        for j, r in enumerate(others + [rank]):
+            dma("s", R("xi", a + w * j, a + w * j + w), hbm(T.x[32 * r:32 * r + 32, a:b]), "ld%d" % k, 64, LOCAL, w // 2)
 
-    lead[0] = False
-    ms(R("zr", 0, 512), 0.0)
-    lin(R("zr", 512, 1024), R("zr", 0, 512))
-    iota(R("zr", 1024, 2048), [[0, 1024]], 0, 0)
-    a = 0
-    for w, qs in CLEAR:
-        def clear(q, out=R("tab", a, a + w), w=w):
-            if q == "v":
-                return g.vector.memset(out[0], 0.0)
-            if q == "a":
-                return g.scalar.activation(out[0], T.zr[:, 0:w], AF.Identity, 0.0, 1.0)
-            return g.iota(out[0], [[0, w]], 0, 0, allow_small_or_imprecise_dtypes=True)
-        cost = {"v": 60 + w, "a": 80 + w, "g": 160 + 2 * w}
-        call({q: cost[q] for q in qs}, clear, [R("tab", a, a + w)], [R("zr", 0, w)] if "a" in qs else [])
-        a += w
+    cleared = [0]
 
+    def clear(q, w):
+        out = R("tab", cleared[0], cleared[0] + w)
+        cleared[0] += w
+        if q == "v":
+            ms(out, 0.0)
+        elif q == "a":
+            call({"a": 80 + w + (1570 if cleared[0] == 512 + w else 0)},
+                 lambda q: g.scalar.activation(out[0], T.tab[:, 0:w], AF.Silu), [out], [R("tab", 0, w)])
+        else:
+            iota(out, [[0, w]], 0, 0)
+
+    clear("v", 512)
+    for w in CA:
+        clear("a", w)
+
+    mine = 40 * rank
+    ts(R("pay", mine, mine + 34), R("wi", 0, 34), -2048.0, ALU.add)
+    cp(R("pay", mine + 16, mine + 18), R("wi", 16, 18))
+    slot = R("pay", mine, mine + 34)
     iota(R("i1"), [[32, 4]], 0, 1)
     iota(R("ri"), [[1, 256]], 0, 0)
+    iota(R("kr"), [[-1, 256]], 256, 0)
     iota(R("rm"), [[0, 3], [1, 128]], 0, 0)
     iota(R("rg"), [[16, 8], [0, 16]], 0, 0)
     iota(R("r32"), [[0, 4], [1, 32]], 0, 0)
     iota(R("rb"), [[0, 4], [1, 2], [0, 16]], 0, 0)
-    iota(R("kr"), [[-1, 256]], 256, 0)
+    lands([R("pay", 40 * r, 40 * r + 34) for r in others], "pay", ke * (n - 1),
+          send([(slot, off, "pay", [(T.cores[r], slot) for r in others])], 1500))
+
     ts(R("j1", 0, 4), R("i1"), 112, ALU.bitwise_and)
     ts(C("j1", 4), C("i1", 0), 15, ALU.bitwise_and)
     ts(C("j1", 5), C("i1", 0), 31, ALU.bitwise_and)
@@ -298,12 +332,6 @@ def rank_program(g, core, T, topo):
     ts(R("idf"), R("rm", 0, 128), me, ALU.is_equal)
     ms(R("neg"), -128.0)
 
-    mine = 40 * rank
-    ts(R("pay", mine, mine + 34), R("wi", 0, 34), -2048.0, ALU.add)
-    cp(R("pay", mine + 16, mine + 18), R("wi", 16, 18))
-    slot = R("pay", mine, mine + 34)
-    lands([R("pay", 40 * r, 40 * r + 34) for r in others], "pay", ke * (n - 1),
-          send([(slot, off, "pay", [(T.cores[r], slot) for r in others])], 1500))
     for lo, a, b, step in ((20, 16, 34, 0), (0, 0, 18, 1), (18, 16, 18, -1)):
         group([(B(7, lo, lo + b - a), R("sel", 96 - 32 * r, 224 - 32 * r), R("pay", 40 * ((r + step) % n) + a, 40 * ((r + step) % n) + b))
                for r in range(n)])
@@ -312,31 +340,64 @@ def rank_program(g, core, T, topo):
     ts(R("pt", 16, 32), B(7, 0, 16), 2048.0, ALU.add)
     for u in range(2):
         ts(R("wb", 128 * u, 128 * u + 128), R("rg"), g16, ALU.is_equal, C("wf", 4 + u), ALU.mult)
-        for kind, (to, w) in enumerate(((0, 4), (1, 0), (3, 2))):
+    lead[0] = False
+    for u in range(2):
+        for kind, (to, w) in enumerate(((1, 0), (3, 2))):
             a = 16 * kind + 8 * u
             ts(R("wm", a, a + 8), R("rm", 0, 128, 16), C("cf", to), ALU.is_equal, C("wf", w + u), ALU.mult)
     ts(R("eq"), R("r32"), p31, ALU.is_equal)
     group([(B(7, 0, 256), R("eq"), R("wb"))])
-    lin(R("we"), B(7, 0, 256))
+    lin(R("we"), B(7, 0, 256), -2.0 ** -12)
 
+    lead[0] = True
+    for k in SEQ:
+        a, b = CHUNKS[k]
+        ts(R("xs", a, b), R("xi", a, b), 128.0, ALU.add)
+        if k >= DIRECT:
+            dma("s", D(k, None, "st"), R("xs", a, b), "sg%d" % k, 16, LOCAL + (b - a) // 4)
+            dma("s", D(k, rank), (T.xs[32 * rank:32 * rank + 32, a:b],) + R("xs", a, b)[1:], "ow%d" % k, 16)
     for k, (a, b) in enumerate(CHUNKS):
         w = (b - a) // 4
-        lead[0] = True
-        ts(R("xs", a, b), R("xi", a, b), 128.0, ALU.add)
-        dma(STAGE, D(k, None, "st"), R("xs", a, b), "sg%d" % k, 16, LOCAL + w)
-        dma(STAGE, D(k, rank), (T.xs[32 * rank:32 * rank + 32, a:b],) + R("xs", a, b)[1:], "ow%d" % k, 16)
-        lands([D(k, r) for r in others], "la%d" % k, ke,
-              send([(D(k, r, "st"), thirds[(j + k) % 3], "la%d" % k, [(T.cores[r], D(k, rank))]) for j, r in enumerate(others)], SLOW * w))
-        dma("s", R("xb", a, b), D(k), "re%d" % k, 16, LOCAL + 3 * w)
-        if k in CAST:
-            dma("g", R("xf", a, b), D(k), "cf%d" % k, 16, LOCAL + 6 * w, ISSUE)
-        lead[0] = False
-        if k not in CAST:
-            lin(R("xf", a, b), R("xb", a, b))
+        if k < DIRECT:
+            for js in ((0, 1), (2,)):
+                twin = send([(R("xs", a + w * j, a + w * j + w), masks[j], "la%d" % k,
+                              [(T.cores[others[j]], R("ga", a + w * rank, a + w * rank + w))]) for j in js], SLOW * w)
+            lands([R("ga", a + w * r, a + w * r + w) for r in others], "la%d" % k, 2 * ke, twin)
+        else:
+            lands([D(k, r) for r in others], "la%d" % k, ke,
+                  send([(D(k, r, "st"), thirds[(j + k) % 3], "la%d" % k, [(T.cores[r], D(k, rank))]) for j, r in enumerate(others)], SLOW * w))
+            dma("s", R("xb", a, b), D(k), "re%d" % k, 16, LOCAL + 2 * w)
+        for _ in range(CG[k]):
+            clear("g", 512)
 
-    def sums(bank, o, a, b, c0, m, out):
-        w = 16 * (b - a)
-        group([(B(bank, k, w, 16, m), R("xb", 16 * c0 + k, 16 * (c0 + m), 16), R("wm", a, b)) for k in range(16)], True)
+    ts(C("tci", 5), C("i1", 0), 3, ALU.bitwise_and)
+    cp(C("ce", 20), C("tci", 5))
+    ts(C("ce", 21), C("ce", 20), me, ALU.subtract, 0.25, ALU.mult)
+    ts(C("ce", 22), C("ce", 21), 160.0, ALU.add)
+    ts(R("cg", 10, 14), R("ri", 0, 4), C("ce", 20), ALU.is_equal)
+    for j in range(4):
+        ts(R("lay", 224 * j, 224 * j + 224), R("kr", 0, 224), C("ce", 22), ALU.is_equal, C("cg", 10 + j), ALU.mult)
+    for _ in range((HT - sum(CA) - CB) // 512 - 1 - sum(CG)):
+        clear("v", 512)
+
+    def unfold(k):
+        a, b = CHUNKS[k]
+        w = (b - a) // 4
+        step = 512 // w * w if k < DIRECT else 512
+        for lo in range(a, b, step):
+            hi = min(b, lo + step)
+            if k < DIRECT:
+                bank = lo // step % 2
+                for c in range(lo, hi, w):
+                    j = (c - a) // w
+                    group([(B(bank, c - lo, c - lo + w), R("lay", 224 * j + 96 - 32 * r, 224 * j + 224 - 32 * r),
+                            R("xs", b - w, b) if r == rank else R("ga", a + w * r, a + w * r + w)) for r in [rank] + others])
+                lin(R("xb", lo, hi), B(bank, 0, hi - lo), 1.0, 0.0, "a")
+            widen(R("xf", lo, hi), R("xb", lo, hi))
+
+    def sums(bank, o, by, c0, m, out):
+        w = 16 * by[2]
+        group([(B(bank, k, w, 16, m), R("xb", 16 * c0 + k, 16 * (c0 + m), 16), by) for k in range(16)], True)
         lin(R("ut", o, o + w, 1, m), B(bank, 0, w, 1, m))
         turned(o, m, out, range(2))
 
@@ -351,25 +412,32 @@ def rank_program(g, core, T, topo):
         ts(R("wk", o + w, o + 2 * w), R("wk", o, o + w), 5, ALU.arith_shift_right, H - 1, ALU.bitwise_and)
         tt(out, R("wk", o + w, o + 2 * w), R("wk", o + 3 * w, o + 4 * w), ALU.add)
 
-    for k, (a, b) in enumerate(CHUNKS):
-        a, w = a // 16, (b - a) // 16
-        sums(6 + k % 2, 256 * (k % 2), 0, 16, a, w, lambda u: B(4 + k % 2, w * u, w * u + w))
+    for k in range(len(CHUNKS)):
+        lead[0] = k == 0
+        unfold(k)
+        if k == 0:
+            behind[:] = [len(calls) - 2]
+            clear("a", CB)
+            behind[:] = []
+    for k, (a, b) in enumerate(PARTS):
+        w = b - a
+        lead[0] = 16 * b <= CHUNKS[0][1]
+        sums(6 + k % 2, 256 * (k % 2), R("wb", 0, 256, 16), a, w, lambda u: B(4 + k % 2, w * u, w * u + w))
         cp(R("wk", 4 * a, 4 * a + 2 * w), B(4 + k % 2, 0, 2 * w))
         places(R("slp", a, a + w), 4 * a, w)
         cp(R("ixo", a, a + w), R("slp", a, a + w))
-        scatter(R("tab", 0, HT), R("ixo", a, a + w), R("xf", 16 * a, 16 * (a + w)), 0 if k else 1570)
+        scatter(R("tab", 0, HT), R("ixo", a, a + w), R("xf", 16 * a, 16 * (a + w)))
 
     def centred(j, a, b, src):
         w = b - a
-        o = 1024 + 8 * a + 4 * w * j
-        cp(R("wk", o, o + 2 * w), src)
-        ts(R("wk", o + 2 * w, o + 4 * w), R("wk", o, o + 2 * w), 4095, ALU.bitwise_and)
-        ts(X("us", 256 * j + a, 256 * j + b, T.us[:, 2 * j:2 * j + 2, a:b], 2 * w), R("wk", o + 2 * w, o + 4 * w), -2048.0, ALU.add)
+        o = 512 * j + 2 * a
+        ts(R("rd", o, o + 2 * w), src, 4 * ROUND, ALU.add, 4 * ROUND, ALU.subtract)
+        tt(X("us", 256 * j + a, 256 * j + b, T.us[:, 2 * j:2 * j + 2, a:b], 2 * w), src, R("rd", o, o + 2 * w), ALU.subtract)
 
     for h, (a, b) in enumerate(HALVES):
         w = b - a
-        sums(2 + h, 512 + 512 * h, 16, 48, a, w, lambda j: B(h, w * j, w * j + w))
-        centred(0, a, b, B(h, 0, 2 * w))
+        sums(2 + h, 512 + 512 * h, R("wm"), a, w, lambda j: B(3 - h, w * j, w * j + w))
+        centred(0, a, b, B(3 - h, 0, 2 * w))
 
     def U(j, a, b):
         return X("us", 256 * (j // 2) + a, 256 * (j // 2) + b, T.us[:, j, a:b], b - a)
@@ -380,18 +448,16 @@ def rank_program(g, core, T, topo):
     ts(R("xab", 512, 544), ind(R("xb"), R("po", 0, 2)), -1.0, ALU.mult)
     cp(R("xab", 544, 576), ind(R("xb"), R("po", 16, 18)))
     group([(B(4, 0, 1), idn, C("xab", 512)), (B(4, 0, 1), up2, C("xab", 544))])
-    cp(C("dg", 0), B(4, 0, 1))
-    lin(R("xab", 0, 256), ind(R("xb"), R("po", 0, 16)), -1.0)
-    lin(R("xab", 256, 512), ind(R("xb"), R("po", 16, 32)))
-    group([(B(6, 0, 256), idn, R("xab", 0, 256)), (B(6, 0, 256), up2, R("xab", 256, 512))])
-    lin(R("dd", 0, 256), B(6, 0, 256))
-    ms(R("dd", 256, 272), NONE)
     ts(C("ce", 6), r32, -1.0 / 32, ALU.mult, 3.0, ALU.add)
-    ts(R("m4"), R("rm", 0, 4), C("ce", 6), ALU.is_equal)
-    ms(R("elv"), 11.0)
+    ts(R("m4"), R("rm", 0, 16), C("ce", 6), ALU.is_equal)
+    ts(R("dm"), R("m4"), B(4, 0, 1), ALU.mult)
+    ts(R("kc"), R("ri", 0, 12), 7.5, ALU.is_lt, KB + 127.0, ALU.mult)
+    ts(R("kc"), R("kc"), -127.0, ALU.add)
+    ms(R("elv"), 12.0)
+    ms(R("mo"), -1.0)
     ts(R("idh"), R("rm", 0, 128), me, ALU.is_equal)
     ts(R("m4k"), R("rm", 0, 128), me, ALU.is_equal, -4096.0, ALU.mult)
-    ts(R("cid"), R("rm", 0, 128), me, ALU.is_equal, 35.0 * 2048, ALU.mult)
+    ts(R("cid"), R("rm", 0, 128), me, ALU.is_equal, 65536.0, ALU.mult)
 
     ts(C("tci", 4), pm, -1.0, ALU.add, 1.0 / 3, ALU.mult)
     cp(C("ce", 2), C("tci", 4))
@@ -404,9 +470,14 @@ def rank_program(g, core, T, topo):
         ts(R("pw", 48 * j, 48 * j + 48), R("rm", 0, 48), C("ce", to), ALU.is_equal, C("ce", 8), ALU.mult)
     ts(R("big"), R("rm", 0, 128), me, ALU.is_equal, BIG, ALU.mult)
 
-    def pack(banks, src, a, j):
+    def pack(banks, src, a, j, less=(None, None)):
+        done = []
         for h in range(2):
-            group([(B(banks[h], k, 384, 8), R(src, a + 8 * h + k, a + 2048, 16), R("pw", 48 * j, 48 * j + 48)) for k in range(8)], True)
+            if less[h]:
+                group([(B(banks[h], 0, 384), R("nid"), less[h])], stop=False)
+            done.append(group([(B(banks[h], k, 384, 8), R(src, a + 8 * h + k, a + 2048, 16), R("pw", 48 * j, 48 * j + 48)) for k in range(8)],
+                              not less[h], False))
+        return done
 
     def words(name, j, h, a=0, b=48):
         return X(name, 2 * j + h, 2 * j + h + 1, T[name][:, 48 * j + a:48 * j + b, 8 * h:8 * h + 8], 8 * (b - a))
@@ -414,50 +485,51 @@ def rank_program(g, core, T, topo):
     for j in range(2):
         pack((2, 3), "xb", 2048 * j, 0)
         for h in range(2):
-            lin(words("pk", j, h, 0, 40), B(2 + h, 0, 320), 1.0, -127 * ONE)
-            lin(words("pk", j, h, 40, 48), B(2 + h, 320, 384), 1.0, -127.0)
+            lin(words("pk", j, h, 0, 40), B(2 + h, 0, 320), 1.0, -127 * ONE, "v")
+            lin(words("pk", j, h, 40, 48), B(2 + h, 320, 384), 1.0, -127.0, "v")
 
-    for e in range(n):
-        ms(R("q", 256 * e, 256 * e + 16), 0.0)
+    iota(R("zr"), [[0, 2048]], 0, 0, [R("xf")])
     ts(R("bow"), R("rb"), gp, ALU.is_equal, 1024.0, ALU.mult)
-    ts(R("tie"), R("ri", 0, 4), 1.0 / 256, ALU.mult)
-    ts(R("i16"), R("ri", 0, 16), 16.0, ALU.mult, pm, ALU.add)
-    ts(C("ce", 18), pm, 256.0, ALU.mult, float(HT), ALU.add)
-    lin(R("xo"), R("ri"), 1.0, C("ce", 18))
+    ts(R("tie"), R("ri", 0, 4), 1.0 / 256, ALU.mult, -1.5 / 256, ALU.add)
+    ts(R("i16"), R("ri", 24, 40), 16.0, ALU.mult, pm, ALU.add)
+    iota(R("xo"), [[16, 256]], HT, 1, [R("xf")])
     ts(R("pt", 32, 64), R("pt", 0, 32), 15, ALU.bitwise_and)
-    ts(R("pt", 64, 96), R("pt", 0, 32), 4, ALU.arith_shift_right)
     ts(R("em"), R("rm", 0, 16), pm, ALU.is_equal)
     cp(R("ph"), R("pt", 32, 64))
-    cp(R("pl"), R("pt", 64, 96))
-    ts(R("bon", 0, 128), R("rg"), g16, ALU.is_equal, -512.0, ALU.mult)
-    ts(R("bon", 128, 256), R("rg"), gup, ALU.is_equal, -512.0, ALU.mult)
-    lin(R("mk"), ind(R("em"), R("ph")))
-    ts(C("ce", 19), r32, 0.5, ALU.mult, pm, ALU.add)
-    ts(R("ce", 13, 15), R("ri", 0, 2), gp, ALU.is_equal)
-    ts(R("cg", 8, 10), R("ri", 0, 2), gp, ALU.is_equal, 3.0, ALU.mult)
-    ts(R("fsl"), R("rm", 0, 64), C("ce", 19), ALU.is_equal)
-    ts(R("hn"), R("rm", 0, 128), me, ALU.is_equal, -32.0 * BIG, ALU.mult)
 
-    def turn(bank, names):
-        for r in range(n):
-            for j in range(4):
-                a = 64 * r + 16 * j
-                group([(B(bank, a, a + 16), X(nm, 0, 4, T[nm][:, :, j:256:4], 128), R("fsl", 16 * r, 16 * r + 16)) for nm in names])
+    def spare(t):
+        if t == 0:
+            ts(R("pt", 64, 96), R("pt", 0, 32), 4, ALU.arith_shift_right)
+            cp(R("pl"), R("pt", 64, 96))
+            ts(R("bon", 0, 128), R("rg"), g16, ALU.is_equal, -512.0, ALU.mult)
+            ts(R("bon", 128, 256), R("rg"), gup, ALU.is_equal, -512.0, ALU.mult)
+            ms(R("dd", 256, 272), NONE)
+        if t == 1:
+            ts(R("ce", 13, 15), R("ri", 0, 32, 16), me, ALU.add, g16, ALU.add)
+            for j in range(2):
+                ts(R("fsl", 256 * j, 256 * j + 256), R("ri"), C("ce", 13 + j), ALU.is_equal)
+            ts(R("hn"), R("rm", 0, 128), me, ALU.is_equal, -2.0 ** 60, ALU.mult)
+
+    lin(R("nid"), R("idf"), -1.0)
+
+    def turn(bank, marks):
+        group([(B(bank, 0, 256), R(nm, c + j, c + 256, 2), R("fsl", 256 * j, 256 * j + 256)) for nm, c in marks for j in range(2)])
 
     tab = R("tab", 0, HT)
 
-    def shifted(bank, ds, k0):
-        for e, d in enumerate(ds):
-            a = k0 // 2 + 256 * e
-            lin(R("ndb", a, a + 256), R("elv", 0, 256), 0.0, C("dmf", d))
+    def shifted(bank, ds, k0, qs):
+        for d in ds:
+            lin(R("ndb", 128 * d, 128 * d + 128), R("mo"), C("qf", 8 + d), -127.0, qs)
         for u in range(2):
             for e, d in enumerate(ds):
                 a = k0 + 512 * u + 256 * e
-                ts(R("kk", a, a + 256), U(u, 0, 256), 2.0 ** -12, ALU.mult, C("qf", 4 * u + d), ALU.add)
+                ts(R("kk", a, a + 256), U(u, 0, 256), 2.0 ** -12, ALU.mult,
+                   B(7, 4 * u + d, 4 * u + d + 1) if t and not k0 else C("qf", 4 * u + d), ALU.add)
             group([(B(bank + u), R("cid"), R("elv"))]
-                  + [(B(bank + u, 256 * e, 256 * e + 256), R("idh"), U(u, 0, 256)) for e in range(2)]
-                  + [(B(bank + u), R("we", 128 * u, 128 * u + 128), R("ndb", k0 // 2, k0 // 2 + 512)),
-                     (B(bank + u), R("m4k"), R("kk", k0 + 512 * u, k0 + 512 * u + 512))])
+                  + [(B(bank + u, 256 * e, 256 * e + 256), R("idh"), U(u, 0, 256)) for e in range(2)], stop=False)
+            group([(B(bank + u, 128 * e, 128 * e + 128), R("wb", 128 * u, 128 * u + 128), R("ndb", 128 * ds[e // 2], 128 * ds[e // 2] + 128))
+                   for e in range(4)]
+                  + [(B(bank + u), R("m4k"), R("kk", k0 + 512 * u, k0 + 512 * u + 512))], start=False)
 
     def placed(bank, a, w, o, out="ix", qs="va"):
         lin(R("pa1", o, o + w), B(bank, a, a + w), 1.0, 0.0, qs)
@@ -467,27 +539,29 @@ def rank_program(g, core, T, topo):
         cp(R(out, o, o + w), R("wk", 2 * o, 2 * o + w))
 
     ring = {"ga": 0, "ps": 0, "na": 0}
+    checked = []
 
     def take(name, size):
         a = ring[name] % size
         ring[name] = a + 1
         return a
 
-    def look(offs, c0, bias, shift, lo, bank, first, banks, who, at=0):
+    def look(offs, c0, bias, shift, lo, bank, first, banks, who, check, at=0):
         a, o = 2048 * take("ga", NG // 2), take("na", NN)
-        js = (take("ps", banks), take("ps", banks))
-        for i in range(2):
-            q = who[(c0 + lo) // 64 + i]
-            by = R(offs, c0 + lo + 64 * i, c0 + lo + 64 * i + 64)
-            if offs == "ixr" and q == "v":
-                by = (by[0], R(offs)[1]) + by[2:]
-            lin(R("ga", a + 1024 * i, a + 1024 * i + 1024), ind(tab, by), 1.0, bias, q)
-        pack(js, "ga", a, shift)
-        for h in range(2):
-            tt(words("na", o, h), B(js[h], 0, 384), words("pk", lo // 128, h), ALU.not_equal)
+        js = (banks[take("ps", len(banks))], banks[take("ps", len(banks))])
+        cut, check = who[(c0 + lo) // 128], check[(c0 + lo) // 64:]
+        for q, i, e in (("a", 0, cut), ("v", cut, 128)):
+            by = R(offs, c0 + lo + i, c0 + lo + e)
+            if q == "v" and (offs == "ixr" or t == 0):
+                by = (by[0], R(offs)[1] + [("pk", 0, 4), ("us", 0, 512)]) + by[2:]
+            lin(R("ga", a + 16 * i, a + 16 * e), ind(tab, by), 1.0, bias, q, checked[-LAG] if q == "v" and len(checked) >= LAG else ())
+        packed = pack(js, "ga", a, shift, [words("pk", lo // 128, h) if check[h] == "a" else None for h in range(2)])
+        checked.append([tt(words("na", o, h), B(js[h], 0, 384), words("pk", lo // 128, h), ALU.not_equal) if check[h] == "v"
+                        else size(words("na", o, h), B(js[h], 0, 384)) for h in range(2)])
         out = B(bank, at + lo, at + lo + 128)
-        group([(out, l, R(nm, c + lo, c + lo + 128)) for l, nm, c in first]
-              + [(out, X("na", 2 * o, 2 * o + 2, T.na[:, 48 * o + 8 * w:48 * o + 8 * w + 8, :], 128), R("big")) for w in range(6)])
+        return packed, lambda after: group(
+            [(out, l, R(nm, c + lo, c + lo + 128)) for l, nm, c in first]
+            + [(out, X("na", 2 * o, 2 * o + 2, T.na[:, 48 * o + 8 * w:48 * o + 8 * w + 8, :], 128), R("big")) for w in range(6)], after=after)
 
     for t in range(RO):
         last = t == RO - 1
@@ -495,34 +569,28 @@ def rank_program(g, core, T, topo):
             first = []
         else:
             c0 = 256 * (t - 1)
-            ts(R("cov", c0, c0 + 256), R("ixo"), float(HT), ALU.is_lt)
+            for a, b in HALVES:
+                ts(R("cov", c0 + a, c0 + b), R("xo", a, b), float(HT), ALU.is_lt)
             first = [(idn, "cov", c0)]
             tt(R("pg"), ind(R("cov", c0, c0 + 256), R("pl")), R("mk"), ALU.mult)
-            group([(B(6, 0, 256), idn, R("kr")), (B(6, 0, 256), R("bon", 0, 128), R("pg", 0, 256)),
-                   (B(6, 0, 256), R("bon", 128, 256), R("pg", 256, 512))])
+            group([(B(6, 0, 256), idn, R("kr"))], stop=False)
+            group([(B(6, 0, 256), R("bon", 0, 128), R("pg", 0, 256)), (B(6, 0, 256), R("bon", 128, 256), R("pg", 256, 512))], start=False)
             red(C("nm", 0), B(6, 0, 256), ALU.max, True)
             ts(C("ko", 0), C("nm", 0), 0.0, ALU.min, 256.0, ALU.add)
-            cp(R("dg"), ind(R("dd"), C("ko", 0)))
-        ts(R("dm"), R("m4"), C("dg", 0), ALU.mult)
-        ts(R("dmf"), R("m4"), C("dg", 0), ALU.mult, -1.0, ALU.mult)
-        for j, l in enumerate((R("we", 0, 128), R("we", 128, 256), R("eq"))):
-            group([(B(7, 4 * j, 4 * j + 4), l, R("dm"))])
-        ts(R("qf", 0, 8), B(7, 0, 8), -2.0 ** -12, ALU.mult, KB, ALU.add)
-        ts(R("qf", 8, 12), B(7, 8, 12), -127.0, ALU.add)
-        ts(R("q", 0, 1024, 256), B(7, 8, 12), -1.0, ALU.mult, -127.0, ALU.add)
-        ts(R("q", 1, 1024, 256), B(7, 0, 4), 2.0 ** -12, ALU.mult, KB, ALU.add)
-        ts(R("q", 2, 1024, 256), B(7, 4, 8), 2.0 ** -12, ALU.mult, KB, ALU.add)
-        cp(R("q", 3, 1024, 256), R("dm"))
+            tt(R("dm"), ind(R("dd"), C("ko", 0)), R("m4"), ALU.mult)
+        group([(B(7, 0, 12), R("idf"), R("kc"))], stop=False)
+        group([(B(7, 4 * j, 4 * j + 4), l, R("dm", 0, 4)) for j, l in enumerate((R("we", 0, 128), R("we", 128, 256), R("eq")))], start=False)
+        cp(R("qf", 0, 12), B(7, 0, 12))
         for hh in range(2):
-            shifted(PB[hh], (2 * hh, 2 * hh + 1), 1024 * hh)
+            shifted(PB[hh], (2 * hh, 2 * hh + 1), 1024 * hh, EV[t])
         for hh in range(2):
             for a, w in (((0, 256), (256, 256)) if (t, hh) in SINGLY else ((0, 512),)):
-                placed(PB[hh], a, w, 512 * hh + a)
-        if t > 0:
-            for j in range(2):
-                lin(X("y%d" % t, j, j + 1, T["y%d" % t][:, j, :], 256), R("cov", c0, c0 + 256), C("ce", 13 + j))
+                placed(PB[hh], a, w, 512 * hh + a, "ix", EV[t])
+        ts(R("pa1", 0, 1024, 256), R("qf", 8, 12), -1.0, ALU.mult, -254.0, ALU.add)
+        for u in range(2):
+            ts(R("pa1", 1 + u, 1024, 256), R("qf", 4 * u, 4 * u + 4), -1.0, ALU.mult, 2 * KB, ALU.add)
         if last:
-            turn(6, ("y1", "y2"))
+            turn(6, [("cov", 0), ("cov", 256)])
             lin(R("zf"), B(6, 0, 256))
         ring["ps"] = 0
         if t == 0:
@@ -531,76 +599,92 @@ def rank_program(g, core, T, topo):
             centred(1, 0, 256, B(7))
 
         def fit(d):
-            relu(R("ft", 256 * d, 256 * d + 256), B(6 + d // 2, 256 * (d % 2), 256 * (d % 2) + 256), -2.0, 1.0, C("cl", 4 * t + d))
+            relu(R("ft", 256 * d, 256 * d + 256), B(6 + d % 2, 256 * (d // 2), 256 * (d // 2) + 256), -2.0, 1.0, C("cl", 4 * t + d))
 
+        add = None
         for d in range(n):
-            for lo in (0, 128):
+            for lo, _ in HALVES:
+                packed, later = look("ix", 256 * d, C("qf", 8 + d), 1, lo, 6 + d % 2, first, RING, FORTH[t], CHECK, 256 * (d // 2))
                 if (d, lo) == (3, 128):
-                    fit(2)
-                look("ix", 256 * d, C("qf", 8 + d), 1, lo, 6 + d // 2, first, 6, FORTH, 256 * (d % 2))
-            if d == 1:
-                fit(0)
-            if d % 2:
-                fit(d)
-        cl = R("cl", 4 * t, 4 * t + 4)
+                    fit(1)
+                if add:
+                    add(packed)
+                add = later
+        fit(0)
+        fit(2)
+        group([(B(6, 0, 4), R("bow"), R("tie"))], stop=False)
+        if t == 0:
+            lin(R("xab", 0, 256), ind(R("xb"), R("po", 0, 16)), -1.0, 0.0, "a", packed)
+            lin(R("xab", 256, 512), ind(R("xb"), R("po", 16, 32)), 1.0, 0.0, "a", packed)
+            lin(R("mk"), ind(R("em"), R("ph")), 1.0, 0.0, "a", packed)
+        behind[:] = checked[-1]
+        spare(t)
+        behind[:] = []
+        add(())
+        fit(3)
+        for a, b in HALVES:
+            for u in range(2):
+                group([(B(2 - a // 64 + u, 0, b - a), R("cid"), R("elv", 0, b - a)), (B(2 - a // 64 + u, 0, b - a), R("idh"), U(2 + u, a, b))], stop=False)
         top, base = C("mx", t), C("mx", 4 + t)
-        group([(B(6, 0, 4), R("bow"), R("tie")), (B(6, 0, 4), R("bow"), cl)])
-        group([(B(6, 4, 8), R("bow"), cl)])
+        group([(B(6, 0, 4), R("bow"), R("cl", 4 * t, 4 * t + 4))], start=False)
         red(top, B(6, 0, 4), ALU.max)
-        red(base, B(6, 4, 8), ALU.max)
+        ts(base, top, ROUND, ALU.add, ROUND, ALU.subtract)
         ts(R("so"), R("i16"), base, ALU.subtract, top, ALU.add)
-        cp(R("qw"), ind(R("q"), C("so", 0)))
-        relu(C("yt", 0), base, -1.0, 1.0)
-        lin(C("yt", 1), base, 1.0 / 1024, 0.0, "a")
-        lin(C("yt", 2), base, 1.0 / 256, 3.0, "a")
+        cp(R("qw"), ind(R("pa1"), C("so", 0)))
+        lin(R("ndb", 0, 128), R("mo"), C("qw", 0), -127.0, "a")
+        for a, b in HALVES:
+            w, bank = b - a, 2 - a // 64
+            for u in range(2):
+                ts(R("kk", 256 * u + a, 256 * u + b), U(2 + u, a, b), 2.0 ** -12, ALU.mult, C("qw", 1 + u), ALU.add)
+                group([(B(bank + u, 0, w), R("wb", 128 * u, 128 * u + 128), R("ndb", 0, w)),
+                       (B(bank + u, 0, w), R("m4k"), R("kk", 256 * u + a, 256 * u + b))], start=False)
+            placed(bank, 0, w, a, "ixr", "a")
+        now = (base[0], base[1] + R("pa1", 128, 256)[1]) + base[2:]
+        relu(C("yt", 0), now, -1.0, 1.0)
+        lin(C("yt", 1), now, 1.0 / 1024, 0.0, "a")
+        lin(C("yt", 2), now, 1.0 / 256, 1.5, "a")
         lin(C("yt", 3), top, -1.0 / 256, C("yt", 2), "a")
         lin(C("yws", 8 * rank + t), C("yt", 0), -1.0, C("yt", 3), "a")
         lin(C("yws", 8 * rank + t + 3), C("yt", 0), -1.0, C("yt", 1), "a")
-        for a, b in RESTS:
-            w, bank = b - a, 2 * (a // 128)
-            lin(R("ndb", a, b), R("elv", 0, w), 0.0, C("qw", 3), "a")
-            for u in range(2):
-                ts(R("kk", 256 * u + a, 256 * u + b), U(2 + u, a, b), 2.0 ** -12, ALU.mult, C("qw", 1 + u), ALU.add)
-                group([(B(bank + u, 0, w), R("cid"), R("elv", 0, w)), (B(bank + u, 0, w), R("idh"), U(2 + u, a, b)),
-                       (B(bank + u, 0, w), R("we", 128 * u, 128 * u + 128), R("ndb", a, b)),
-                       (B(bank + u, 0, w), R("m4k"), R("kk", 256 * u + a, 256 * u + b))])
-            placed(bank, 0, w, a, "ixr", "a")
         if last:
-            lin(R("fw"), ind(R("ft"), R("so")))
+            lin(R("fw"), ind(R("ft"), R("so")), 1.0, 0.0, "a")
             first = [(R("hn"), "fw", 0), (R("hn"), "cov", c0)]
             wins = R("yws", 8 * rank, 8 * rank + 6)
             lands([R("yws", 8 * r, 8 * r + 6) for r in others], "yw", ke * (n - 1),
                   send([(wins, off, "yw", [(T.cores[r], wins) for r in others])]))
         else:
-            lin(R("fw"), ind(R("ft"), R("so")), -BIG, BIG)
+            lin(R("fw"), ind(R("ft"), R("so")), -BIG, BIG, "a")
             first = [(R("idf"), "slp", 0)]
-            group([(B(7, 0, 256), R("idf"), R("slp")), (B(7, 0, 256), idn, R("fw"))])
+            if t == 0:
+                group([(B(6, 0, 256), idn, R("xab", 0, 256)), (B(6, 0, 256), up2, R("xab", 256, 512))])
+                lin(R("dd", 0, 256), B(6, 0, 256))
+            group([(B(7, 0, 256), R("idf"), R("slp"))], stop=False)
+            group([(B(7, 0, 256), idn, R("fw"))], start=False)
             tt(R("km"), B(7, 0, 256), R("xo"), ALU.min)
         ring["ps"] = 0
-        for lo in (0, 128):
-            look("ixr", 0, C("qw", 0), 2, lo, 4 + lo // 128, first, 4, WHO)
+        for lo, _ in HALVES:
+            look("ixr", 0, C("qw", 0), 2, lo, 4 + lo // 128, first, (2, 3, 0, 1), WHO[t], CHECKR[t])[1](())
         if not last:
-            for a in (0, 128):
-                tt(R("xo", a, a + 128), B(4 + a // 128, a, a + 128), R("km", a, a + 128), ALU.min)
-                cp(R("ixo", a, a + 128), R("xo", a, a + 128))
-                scatter(R("tab"), R("ixo", a, a + 128), R("zr"))
+            for a, b in HALVES:
+                tt(R("xo", a, b), B(4 + a // 128, a, b), R("km", a, b), ALU.min)
+                cp(R("ixo", a, b), R("xo", a, b))
+                scatter(R("tab"), R("ixo", a, b), R("zr"))
 
-    for hh in range(2):
-        for j in range(2):
-            a = 128 * hh
-            ts(X("y3", 2 * hh + j, 2 * hh + j + 1, T.y3[:, j, a:a + 128], 128), B(4 + hh, a, a + 128), 0.5, ALU.is_lt, C("cg", 8 + j), ALU.mult)
-    turn(6, ("y3",))
+    for a, b in HALVES:
+        ts(R("y3", a, b), B(4 + a // 128, a, b), 0.5, ALU.is_lt, 3.0, ALU.mult)
+    turn(6, [("y3", 0)])
     tt(R("yo"), B(6, 0, 256), R("zf"), ALU.subtract)
-    halves = [thirds[0], thirds[1] | thirds[2], off]
+    lead[0] = True
     for js in ((0, 1), (2,)):
-        back = send([(R("yo", 64 * others[j], 64 * others[j] + 64), halves[j], "yc%d" % rank,
+        back = send([(R("yo", 64 * others[j], 64 * others[j] + 64), masks[j], "yc%d" % rank,
                       [(T.cores[others[j]], R("yl", 64 * rank, 64 * rank + 64))]) for j in js])
     for r in range(n):
-        dma("s", hbm(T.yw[2 * r:2 * r + 2, :]), X("yws", 8 * r, 8 * r + 6, T.yws[0:32:16, 8 * r:8 * r + 6], 6), "st", 128)
-    dma("s", hbm(T.yc[2 * rank:2 * rank + 2, :]), R("yo", 64 * rank, 64 * rank + 64), "st", 128)
-    for j, r in enumerate(others):
-        lands([R("yl", 64 * r, 64 * r + 64)], "yc%d" % r, count(halves[2 - j]), back)
-        dma("sa"[j % 2], hbm(T.yc[2 * r:2 * r + 2, :]), R("yl", 64 * r, 64 * r + 64), "st", 128)
+        dma("s", hbm(T.yw[2 * r:2 * r + 2, :]), X("yws", 8 * r, 8 * r + 6, T.yws[0:32:16, 8 * r:8 * r + 6], 6), "st", 192)
+    for j, r in enumerate([rank] + others):
+        if j:
+            lands([R("yl", 64 * r, 64 * r + 64)], "yc%d" % r, count(masks[3 - j]), back)
+        for h in range(2):
+            dma("sa"[h], hbm(T.yc[2 * r + h:2 * r + h + 1, :]), R("yl" if j else "yo", 64 * r + 32 * h, 64 * r + 32 * h + 32), "st", 192)
 
     cnt = {"v": 0, "a": 0, "p": 0, "g": 0}
     seen = {k: {} for k in Q}
@@ -635,4 +719,4 @@ def rank_program(g, core, T, topo):
     for q in cnt:
         wait("s", "c" + q, cnt[q])
     g.sync.wait_ge(T.sem.sent, sent[0])
-    g.sync.wait_ge(T.sem.st, 128)
+    g.sync.wait_ge(T.sem.st, 192)

from concourse.bass import DstId, RemoteDMATransfer
from concourse.mybir import AluOpType as ALU, AxisListType as AX, ActivationFunctionType as AF

V, H, RO = 4096, 16384, 3
HT = H + V
BIG = 32768.0
ONE = 65793.0
NONE = -512.0
KB = 191.5 + 2.0 ** -13
ROUND = 1.5 * 2.0 ** 33
CHUNKS = ((0, 1024), (1024, 2560), (2560, 4096))
DIRECT = 1
SEQ = (1, 0, 2)
PARTS = ((0, 32), (32, 64), (64, 128), (128, 256))
HALVES = ((0, 128), (128, 256))
SLOW = 4
CA = (512, 1024, 2048, 2048, 2048, 2048, 2048)
CG = (1, 2, 1)
EV = ("va", "v", "v")
CB = 1024
EVEN = [80, 80, 80, 80, 84, 84, 92]
FORTH = [[96, 96] + EVEN[1:], [64] + EVEN, [64] + EVEN]
WHO = [[64, 96], [64, 96], [64, 64]]
CHECK = "v" * 16
CHECKR = ("vvvv", "vvvv", "avav")
LAG = 2
RING = (0, 1, 4, 5, 2, 3)
SINGLY = ((0, 0), (1, 0), (2, 0))
PB = (0, 4)
PASSES = 4
NG, NN = 8, 3
GATHER, SCATTER, PE, WAKE, ISSUE, FLIGHT, LOCAL = 1.56, 3.8, 0.5, 150, 600, 2400, 2200

f32, bf, i32, u16, f16 = "float32", "bfloat16", "int32", "uint16", "float16"
S_ = {
    "tab": (HT + V + 112, f32), "xi": (V, i32), "xs": (V, bf), "xb": (V, bf), "xf": (V, f32), "zr": (2048, f32),
    "ga": (NG * 1024, bf), "kk": (2048, bf), "ndb": (512, bf), "elv": (512, bf), "m4k": (128, bf), "cid": (128, bf),
    "idh": (128, f16), "idf": (128, f32), "nid": (128, f32), "hn": (128, bf), "idw": (224, bf), "sel": (224, f16),
    "fsl": (512, bf), "y3": (256, bf), "rd": (1024, bf), "mo": (128, bf),
    "pw": (144, bf), "big": (128, bf), "neg": (128, bf), "ut": (1536, f32), "xo": (256, f32), "km": (256, f32), "slp": (256, f32),
    "pa1": (1024, f32), "ix": (1024, u16), "ixr": (256, u16), "ixo": (256, u16), "so": (16, u16),
    "wi": (40, i32), "pay": (160, f16), "wf": (8, f32), "pt": (96, i32), "po": (32, u16), "ph": (32, u16), "pl": (32, u16),
    "ri": (256, f32), "rm": (384, bf), "rg": (128, bf), "r32": (128, bf), "rb": (128, bf),
    "i1": (4, i32), "j1": (8, i32), "cf": (8, f32), "cg": (16, f32), "ce": (24, f32), "tci": (8, i32),
    "wm": (32, bf), "wb": (256, bf), "we": (256, bf), "lay": (896, bf), "eq": (128, bf), "bon": (256, bf), "bow": (128, f32),
    "em": (16, bf), "mk": (512, bf), "kr": (256, bf), "i16": (16, f32), "tie": (4, f32), "m4": (16, bf), "kc": (12, f32),
    "xab": (576, bf), "dd": (272, bf), "pg": (512, bf), "nm": (2, f32), "ko": (2, u16), "dm": (16, bf),
    "qf": (16, f32), "qw": (16, f32), "cl": (12, f32), "mx": (8, f32),
    "ft": (1024, bf), "fw": (256, bf), "cov": (512, bf), "zf": (256, f32), "yo": (256, f32), "yl": (256, f32),
    "yt": (4, f32), "yws": (32, f32),
}
SCRATCH = {k: ("sbuf", [128, v[0]], v[1]) for k, v in S_.items()}
SCRATCH["us"] = ("sbuf", [128, 4, 256], f16)
SCRATCH["pk"] = ("sbuf", [128, 96, 16], f32)
SCRATCH["na"] = ("sbuf", [128, 48 * NN, 16], bf)
for k_, (a_, b_) in list(enumerate(CHUNKS))[DIRECT:]:
    SCRATCH["st%d" % k_] = ("dram", [4, 128, (b_ - a_) // 4], bf)
    SCRATCH["dl%d" % k_] = ("dram", [4, 128, (b_ - a_) // 4], bf)
SCRATCH["psA"] = ("psum", [128, 2048], f32)
SCRATCH["psB"] = ("psum", [128, 2048], f32)

SEMAPHORES = (["cv", "ca", "cp", "cg", "sent", "ldw", "st", "pay", "yw"]
              + [s + str(k) for s in ("sg", "ld", "la", "ow", "re", "yc") for k in range(4)])


def count(mask):
    return bin(mask).count("1")


def dst(c, topo):
    rid, pid, _ = topo.addr(c)
    return DstId(rid=rid, pnc=pid)


def shares(core, to, topo):
    eng = [e for e in topo.engines(core, to[0]) if all(e in topo.engines(core, c) for c in to)]
    h = len(eng) // 4
    return sum(1 << e for e in eng), [sum(1 << e for e in part) for part in (eng[:2 * h], eng[2 * h:3 * h], eng[3 * h:])]


def meets(log, reads, writes, engine):
    return [tok for regs, w in ((reads, False), (writes, True)) for name, lo, hi in regs for a, b, ew, tok, q in log.get(name, [])
            if a < hi and lo < b and (w or ew or (name.startswith("ps") and q != engine))]


def enter(log, reads, writes, tok, engine):
    for name, lo, hi in writes:
        log[name] = [e for e in log.get(name, []) if not (lo <= e[0] and e[1] <= hi)] + [(lo, hi, True, tok, engine)]
    for name, lo, hi in reads:
        log.setdefault(name, []).append((lo, hi, False, tok, engine))


def arrange(calls):
    log, deps = {}, []
    for i, c in enumerate(calls):
        key = "".join(c["cost"])
        deps.append(set(meets(log, c["reads"], c["writes"], key if len(key) == 1 else i)) | set(c["after"]))
        enter(log, c["reads"], c["writes"], i, key if len(key) == 1 else i)
    way = [0.0] * len(calls)
    users = [[] for _ in calls]
    for i in reversed(range(len(calls))):
        way[i] = min(calls[i]["cost"].values()) + calls[i]["late"] + WAKE + max([way[j] for j in users[i]] + [0.0])
        for d in deps[i]:
            users[d].append(i)

    def lay(before, after, rank, back):
        busy = {q: [] for q in "vapgsx"}
        left = [len(d) for d in before]
        since = [calls[i]["late"] if back else 0.0 for i in range(len(calls))]
        ready = {i for i in range(len(calls)) if not left[i]}
        at = [None] * len(calls)
        while ready:
            i = max(ready, key=lambda x: (rank[x], x if back else -x))
            ready.remove(i)
            best = None
            for q, cost in calls[i]["cost"].items():
                t, k = since[i], 0
                for k, (a, b) in enumerate(busy[q] + [(1e18, 1e18)]):
                    if t + cost <= a:
                        break
                    t = max(t, b)
                if best is None or t + cost < best[0]:
                    best = (t + cost, t, q, k)
            end, t, q, k = best
            if q != "x":
                busy[q].insert(k, (t, end))
            at[i] = (t, i, q, end)
            for j in after[i]:
                lag = calls[j if back else i]["late"] + (0 if q == "p" and "p" in calls[j]["cost"] else WAKE)
                since[j] = max(since[j], end + lag)
                left[j] -= 1
                if not left[j]:
                    ready.add(j)
        return at

    plan = None
    for _ in range(PASSES):
        at = lay(deps, users, [1e9 - i if c["lead"] else way[i] for i, c in enumerate(calls)], False)
        span = max(x[3] + calls[x[1]]["late"] for x in at)
        if plan is None or span < plan[0]:
            plan = (span, at)
        way = [x[3] for x in lay(users, deps, [x[3] + calls[x[1]]["late"] for x in at], True)]
    return [(i, q) for _, i, q, _ in sorted(plan[1])]


def rank_program(g, core, T, topo):
    rank = T.rank_of(core)
    if rank is None:
        return
    n = len(T.cores)
    others = [(rank + j) % n for j in range(1, n)]
    off, thirds = shares(core, [T.cores[r] for r in others], topo)
    masks = [thirds[0], thirds[1] | thirds[2], off]
    ke = count(off)
    Q = {"v": g.vector, "a": g.scalar, "p": g.tensor, "g": g, "s": g.sync}
    calls = []
    sent = [0]
    line, behind = [], []
    lead = [True]

    def R(name, a=0, b=None, s=1, m=128):
        name = "xi" if name == "wk" else name
        t = T[name]
        b = t.shape[1] if b is None else b
        lo, hi = (a // 512 * 512, (b + 511) // 512 * 512) if name.startswith("ps") else (a, b)
        return (t[0:m, a:b:s] if s != 1 else t[0:m, a:b], [(name, lo, hi)], (b - a + s - 1) // s, SCRATCH[name][2], False)

    def C(name, a):
        return R(name, a, a + 1)

    def B(bank, a=0, b=512, s=1, m=128):
        return R("ps" + "AB"[bank // 4], 512 * (bank % 4) + a, 512 * (bank % 4) + b, s, m)

    def X(name, a, b, view, m):
        return (view, [(name, a, b)], m, SCRATCH[name][2], False)

    def D(k, r=None, name="dl"):
        t = T[name + str(k)]
        return (t[:], [(t.name, 0, n)], 0, bf, False) if r is None else (t[r], [(t.name, r, r + 1)], 0, bf, False)

    def hbm(view):
        return (view, [], 0, i32, False)

    def ind(win, offs):
        return (win[0].indirect(offs[0]), win[1] + offs[1], 16 * offs[2], win[3], True)

    def call(cost, make, outs, ins, late=0, after=(), sem=None):
        if lead[0] and "g" in cost:
            after = tuple(after) + tuple(line)
            line[:] = [len(calls)]
        after = tuple(after) + tuple(behind)
        calls.append({"lead": lead[0], "cost": cost, "make": make, "late": late, "after": after, "sem": sem,
                      "reads": sorted({r for x in ins if isinstance(x, tuple) for r in x[1]}),
                      "writes": sorted({r for x in outs for r in x[1]})})
        return len(calls) - 1

    def ap(x):
        return x[0] if isinstance(x, tuple) else x

    def cyc(out, a, k=1.0):
        if a[4]:
            return 60 + GATHER * a[2]
        return 60 + max(64, a[2] * (0.5 if out[3] in (bf, f16, u16) and a[3] in (bf, f16, u16) and k == 1.0 else k))

    def cp(out, a):
        call({"v": cyc(out, a)}, lambda q: g.vector.tensor_copy(out[0], a[0]), [out], [a])

    def tt(out, a, b, o):
        two = not (a[1][0][0].startswith("ps") or b[1][0][0].startswith("ps"))
        return call({"v": cyc(out, a, 2.0 if two else 1.001)}, lambda q: g.vector.tensor_tensor(out[0], a[0], b[0], o), [out], [a, b])

    def ts(out, a, s1, o1, s2=None, o2=None):
        if o2 is None:
            call({"v": cyc(out, a)}, lambda q: g.vector.tensor_scalar(out[0], a[0], ap(s1), None, o1), [out], [a, s1])
        else:
            call({"v": cyc(out, a)}, lambda q: g.vector.tensor_scalar(out[0], a[0], ap(s1), ap(s2), o1, o2), [out], [a, s1, s2])

    def lin(out, a, scale=1.0, bias=0.0, qs="va", after=()):
        def make(q):
            if q == "a":
                return g.scalar.activation(out[0], a[0], AF.Identity, ap(bias), ap(scale))
            return g.vector.tensor_scalar(out[0], a[0], ap(scale), ap(bias), ALU.mult, ALU.add)
        cost = {"v": cyc(out, a), "a": 80 + (GATHER if a[4] else 1) * a[2]}
        call({q: cost[q] for q in qs}, make, [out], [a, scale, bias], 0, after)

    def relu(out, a, scale, bias, acc=None):
        def make(q):
            if acc is None:
                return g.scalar.activation(out[0], a[0], AF.Relu, bias, scale)
            return g.scalar.activation(out[0], a[0], AF.Relu, bias, scale, accum_out=acc[0])
        call({"a": 100 + a[2]}, make, [out] + ([] if acc is None else [acc]), [a])

    def size(out, a):
        return call({"a": 80 + a[2]}, lambda q: g.scalar.activation(out[0], a[0], AF.Abs, 0.0, 1.0), [out], [a])

    def ms(out, val):
        call({"v": cyc(out, out)}, lambda q: g.vector.memset(out[0], val), [out], [])

    def red(out, a, o, neg=False):
        call({"v": cyc(out, a)}, lambda q: g.vector.tensor_reduce(out[0], a[0], AX.X, o, negate=neg), [out], [a])

    def scatter(win, offs, src):
        call({"a": 80 + SCATTER * src[2]}, lambda q: g.scalar.activation(win[0].indirect(offs[0]), src[0], AF.Silu), [win], [offs, src])

    def group(steps, apart=False, start=True, stop=True, after=()):
        def make(q):
            for i, (out, l, r) in enumerate(steps):
                last = g.tensor.matmul(out[0], l[0], r[0], apart or (start and i == 0), apart or (stop and i == len(steps) - 1))
            return last
        return call({"p": sum(12 + PE * max(64, r[2]) * (4 if r[3] == f32 else 1) for _, _, r in steps)}, make,
                    [s[0] for s in steps], [x for s in steps for x in s[1:]], 0, after)

    def iota(out, pat, base, cm, once=()):
        def make(q):
            if out[3] == i32:
                return g.iota(out[0], pat, base, cm)
            return g.iota(out[0], pat, base, cm, allow_small_or_imprecise_dtypes=True)
        call({"g": 160 + 2 * out[2]}, make, [out], list(once))

    def widen(out, a):
        call({"g": 200 + 2 * a[2]}, lambda q: g.affine_select(out[0], a[0], [[0, a[2]]], ALU.is_ge, 0.0, 0, 0), [out], [a])

    def dma(q, out, src, sem, total, late=LOCAL, hold=120):
        return call({q: hold}, lambda q: Q[q].dma_start(out[0], src[0]), [out], [src], late, (), (sem, total))

    def send(parts, late=0):
        def make(q):
            g.remote_dma_fused([RemoteDMATransfer(dst_ids=[dst(c, topo) for c, _ in to], dma_engine_mask=m,
                                                  remote_sem=T.sem[sem], srcs=[src[0]], dsts=[d[0] for _, d in to])
                                for src, m, sem, to in parts], local_sem=T.sem.sent)
        sent[0] += sum(count(p[1]) for p in parts)
        i = call({"g": ISSUE}, make, [], [p[0] for p in parts], 0, (), "far")
        return call({"x": FLIGHT + late}, None, [], [], 0, (i,), "far")

    def lands(regs, sem, total, twin):
        call({"x": 1}, None, regs, [], -WAKE, (twin,), (sem, total))

    for a, b, src in ((0, 16, T.pa), (16, 17, T.w1), (17, 18, T.w2), (18, 34, T.pb)):
        dma("s", R("wi", a, b), hbm(src[:]), "ldw", 64)
    for k in SEQ:
        a, b = CHUNKS[k]
        w = (b - a) // 4
        if k >= DIRECT:
            dma("s", R("xi", a, b), hbm(T.x[:, a:b]), "ld%d" % k, 16, LOCAL, 2 * w)
            continue
        for j, r in enumerate(others + [rank]):
            dma("s", R("xi", a + w * j, a + w * j + w), hbm(T.x[32 * r:32 * r + 32, a:b]), "ld%d" % k, 64, LOCAL, w // 2)

    cleared = [0]

    def clear(q, w):
        out = R("tab", cleared[0], cleared[0] + w)
        cleared[0] += w
        if q == "v":
            ms(out, 0.0)
        elif q == "a":
            call({"a": 80 + w + (1570 if cleared[0] == 512 + w else 0)},
                 lambda q: g.scalar.activation(out[0], T.tab[:, 0:w], AF.Silu), [out], [R("tab", 0, w)])
        else:
            iota(out, [[0, w]], 0, 0)

    clear("v", 512)
    for w in CA:
        clear("a", w)

    mine = 40 * rank
    ts(R("pay", mine, mine + 34), R("wi", 0, 34), -2048.0, ALU.add)
    cp(R("pay", mine + 16, mine + 18), R("wi", 16, 18))
    slot = R("pay", mine, mine + 34)
    iota(R("i1"), [[32, 4]], 0, 1)
    iota(R("ri"), [[1, 256]], 0, 0)
    iota(R("kr"), [[-1, 256]], 256, 0)
    iota(R("rm"), [[0, 3], [1, 128]], 0, 0)
    iota(R("rg"), [[16, 8], [0, 16]], 0, 0)
    iota(R("r32"), [[0, 4], [1, 32]], 0, 0)
    iota(R("rb"), [[0, 4], [1, 2], [0, 16]], 0, 0)
    lands([R("pay", 40 * r, 40 * r + 34) for r in others], "pay", ke * (n - 1),
          send([(slot, off, "pay", [(T.cores[r], slot) for r in others])], 1500))

    ts(R("j1", 0, 4), R("i1"), 112, ALU.bitwise_and)
    ts(C("j1", 4), C("i1", 0), 15, ALU.bitwise_and)
    ts(C("j1", 5), C("i1", 0), 31, ALU.bitwise_and)
    ts(C("j1", 6), C("i1", 0), 96, ALU.bitwise_and)
    ts(C("j1", 7), C("i1", 0), 4, ALU.arith_shift_right, 1, ALU.bitwise_and)
    cp(R("cf"), R("j1"))
    g16, gup, pm, p31, r32, gp = C("cf", 0), C("cf", 1), C("cf", 4), C("cf", 5), C("cf", 6), C("cf", 7)
    me = C("cg", 4)
    ts(me, g16, pm, ALU.add)
    ts(C("ce", 0), p31, 96.0, ALU.add)
    ts(C("ce", 1), r32, 32.0 * rank, ALU.is_equal)
    ts(R("sel"), R("ri", 0, 224), C("ce", 0), ALU.is_equal, C("ce", 1), ALU.mult)
    ts(R("idf"), R("rm", 0, 128), me, ALU.is_equal)
    ms(R("neg"), -128.0)

    for lo, a, b, step in ((20, 16, 34, 0), (0, 0, 18, 1), (18, 16, 18, -1)):
        group([(B(7, lo, lo + b - a), R("sel", 96 - 32 * r, 224 - 32 * r), R("pay", 40 * ((r + step) % n) + a, 40 * ((r + step) % n) + b))
               for r in range(n)])
    cp(R("wf", 0, 6), B(7, 16, 22))
    ts(R("pt", 0, 16), B(7, 22, 38), 2048.0, ALU.add)
    ts(R("pt", 16, 32), B(7, 0, 16), 2048.0, ALU.add)
    for u in range(2):
        ts(R("wb", 128 * u, 128 * u + 128), R("rg"), g16, ALU.is_equal, C("wf", 4 + u), ALU.mult)
    lead[0] = False
    for u in range(2):
        for kind, (to, w) in enumerate(((1, 0), (3, 2))):
            a = 16 * kind + 8 * u
            ts(R("wm", a, a + 8), R("rm", 0, 128, 16), C("cf", to), ALU.is_equal, C("wf", w + u), ALU.mult)
    ts(R("eq"), R("r32"), p31, ALU.is_equal)
    group([(B(7, 0, 256), R("eq"), R("wb"))])
    lin(R("we"), B(7, 0, 256), -2.0 ** -12)

    lead[0] = True
    for k in SEQ:
        a, b = CHUNKS[k]
        ts(R("xs", a, b), R("xi", a, b), 128.0, ALU.add)
        if k >= DIRECT:
            dma("s", D(k, None, "st"), R("xs", a, b), "sg%d" % k, 16, LOCAL + (b - a) // 4)
            dma("s", D(k, rank), (T.xs[32 * rank:32 * rank + 32, a:b],) + R("xs", a, b)[1:], "ow%d" % k, 16)
    for k, (a, b) in enumerate(CHUNKS):
        w = (b - a) // 4
        if k < DIRECT:
            for js in ((0, 1), (2,)):
                twin = send([(R("xs", a + w * j, a + w * j + w), masks[j], "la%d" % k,
                              [(T.cores[others[j]], R("ga", a + w * rank, a + w * rank + w))]) for j in js], SLOW * w)
            lands([R("ga", a + w * r, a + w * r + w) for r in others], "la%d" % k, 2 * ke, twin)
        else:
            lands([D(k, r) for r in others], "la%d" % k, ke,
                  send([(D(k, r, "st"), thirds[(j + k) % 3], "la%d" % k, [(T.cores[r], D(k, rank))]) for j, r in enumerate(others)], SLOW * w))
            dma("s", R("xb", a, b), D(k), "re%d" % k, 16, LOCAL + 2 * w)
        for _ in range(CG[k]):
            clear("g", 512)

    ts(C("tci", 5), C("i1", 0), 3, ALU.bitwise_and)
    cp(C("ce", 20), C("tci", 5))
    ts(C("ce", 21), C("ce", 20), me, ALU.subtract, 0.25, ALU.mult)
    ts(C("ce", 22), C("ce", 21), 160.0, ALU.add)
    ts(R("cg", 10, 14), R("ri", 0, 4), C("ce", 20), ALU.is_equal)
    for j in range(4):
        ts(R("lay", 224 * j, 224 * j + 224), R("kr", 0, 224), C("ce", 22), ALU.is_equal, C("cg", 10 + j), ALU.mult)
    for _ in range((HT - sum(CA) - CB) // 512 - 1 - sum(CG)):
        clear("v", 512)

    def unfold(k):
        a, b = CHUNKS[k]
        w = (b - a) // 4
        step = 512 // w * w if k < DIRECT else 512
        for lo in range(a, b, step):
            hi = min(b, lo + step)
            if k < DIRECT:
                bank = lo // step % 2
                for c in range(lo, hi, w):
                    j = (c - a) // w
                    group([(B(bank, c - lo, c - lo + w), R("lay", 224 * j + 96 - 32 * r, 224 * j + 224 - 32 * r),
                            R("xs", b - w, b) if r == rank else R("ga", a + w * r, a + w * r + w)) for r in [rank] + others])
                lin(R("xb", lo, hi), B(bank, 0, hi - lo), 1.0, 0.0, "a")
            widen(R("xf", lo, hi), R("xb", lo, hi))

    def sums(bank, o, by, c0, m, out):
        w = 16 * by[2]
        group([(B(bank, k, w, 16, m), R("xb", 16 * c0 + k, 16 * (c0 + m), 16), by) for k in range(16)], True)
        lin(R("ut", o, o + w, 1, m), B(bank, 0, w, 1, m))
        turned(o, m, out, range(2))

    def turned(o, m, out, js):
        for j in js:
            group([(out(j), R("wb", 128 * (j % 2), 128 * (j % 2) + 128), R("neg", 0, m)),
                   (out(j), R("ut", o + 128 * j, o + 128 * j + 128, 1, m), R("idf", 0, m, 1, m))])

    def places(out, o, w):
        ts(R("wk", o + 2 * w, o + 4 * w), R("wk", o, o + 2 * w), 4095, ALU.bitwise_and)
        tt(R("wk", o, o + w), R("wk", o + 2 * w, o + 3 * w), R("wk", o + 3 * w, o + 4 * w), ALU.mult)
        ts(R("wk", o + w, o + 2 * w), R("wk", o, o + w), 5, ALU.arith_shift_right, H - 1, ALU.bitwise_and)
        tt(out, R("wk", o + w, o + 2 * w), R("wk", o + 3 * w, o + 4 * w), ALU.add)

    for k in range(len(CHUNKS)):
        lead[0] = k == 0
        unfold(k)
        if k == 0:
            behind[:] = [len(calls) - 2]
            clear("a", CB)
            behind[:] = []
    for k, (a, b) in enumerate(PARTS):
        w = b - a
        lead[0] = 16 * b <= CHUNKS[0][1]
        sums(6 + k % 2, 256 * (k % 2), R("wb", 0, 256, 16), a, w, lambda u: B(4 + k % 2, w * u, w * u + w))
        cp(R("wk", 4 * a, 4 * a + 2 * w), B(4 + k % 2, 0, 2 * w))
        places(R("slp", a, a + w), 4 * a, w)
        cp(R("ixo", a, a + w), R("slp", a, a + w))
        scatter(R("tab", 0, HT), R("ixo", a, a + w), R("xf", 16 * a, 16 * (a + w)))

    def centred(j, a, b, src):
        w = b - a
        o = 512 * j + 2 * a
        ts(R("rd", o, o + 2 * w), src, 4 * ROUND, ALU.add, 4 * ROUND, ALU.subtract)
        tt(X("us", 256 * j + a, 256 * j + b, T.us[:, 2 * j:2 * j + 2, a:b], 2 * w), src, R("rd", o, o + 2 * w), ALU.subtract)

    for h, (a, b) in enumerate(HALVES):
        w = b - a
        sums(2 + h, 512 + 512 * h, R("wm"), a, w, lambda j: B(3 - h, w * j, w * j + w))
        centred(0, a, b, B(3 - h, 0, 2 * w))

    def U(j, a, b):
        return X("us", 256 * (j // 2) + a, 256 * (j // 2) + b, T.us[:, j, a:b], b - a)

    ts(R("idw"), R("rm", 0, 224), me, ALU.is_equal)
    idn, up2 = R("idw", 0, 128), R("idw", 96, 224)
    cp(R("po"), R("pt", 0, 32))
    ts(R("xab", 512, 544), ind(R("xb"), R("po", 0, 2)), -1.0, ALU.mult)
    cp(R("xab", 544, 576), ind(R("xb"), R("po", 16, 18)))
    group([(B(4, 0, 1), idn, C("xab", 512)), (B(4, 0, 1), up2, C("xab", 544))])
    ts(C("ce", 6), r32, -1.0 / 32, ALU.mult, 3.0, ALU.add)
    ts(R("m4"), R("rm", 0, 16), C("ce", 6), ALU.is_equal)
    ts(R("dm"), R("m4"), B(4, 0, 1), ALU.mult)
    ts(R("kc"), R("ri", 0, 12), 7.5, ALU.is_lt, KB + 127.0, ALU.mult)
    ts(R("kc"), R("kc"), -127.0, ALU.add)
    ms(R("elv"), 12.0)
    ms(R("mo"), -1.0)
    ts(R("idh"), R("rm", 0, 128), me, ALU.is_equal)
    ts(R("m4k"), R("rm", 0, 128), me, ALU.is_equal, -4096.0, ALU.mult)
    ts(R("cid"), R("rm", 0, 128), me, ALU.is_equal, 65536.0, ALU.mult)

    ts(C("tci", 4), pm, -1.0, ALU.add, 1.0 / 3, ALU.mult)
    cp(C("ce", 2), C("tci", 4))
    ts(C("ce", 3), C("ce", 2), -3.0, ALU.mult, pm, ALU.add)
    ts(C("ce", 4), C("ce", 3), 32512.5, ALU.mult, -32257.5, ALU.add)
    ts(C("ce", 8), C("ce", 4), C("ce", 3), ALU.mult, 1.0, ALU.add)
    ts(C("ce", 5), C("ce", 2), 8.0, ALU.mult)
    ts(R("ce", 9, 13), R("cf", 0, 4), 1.0 / 16, ALU.mult, C("ce", 5), ALU.add)
    for j, to in enumerate((9, 12, 10)):
        ts(R("pw", 48 * j, 48 * j + 48), R("rm", 0, 48), C("ce", to), ALU.is_equal, C("ce", 8), ALU.mult)
    ts(R("big"), R("rm", 0, 128), me, ALU.is_equal, BIG, ALU.mult)

    def pack(banks, src, a, j, less=(None, None)):
        done = []
        for h in range(2):
            if less[h]:
                group([(B(banks[h], 0, 384), R("nid"), less[h])], stop=False)
            done.append(group([(B(banks[h], k, 384, 8), R(src, a + 8 * h + k, a + 2048, 16), R("pw", 48 * j, 48 * j + 48)) for k in range(8)],
                              not less[h], False))
        return done

    def words(name, j, h, a=0, b=48):
        return X(name, 2 * j + h, 2 * j + h + 1, T[name][:, 48 * j + a:48 * j + b, 8 * h:8 * h + 8], 8 * (b - a))

    for j in range(2):
        pack((2, 3), "xb", 2048 * j, 0)
        for h in range(2):
            lin(words("pk", j, h, 0, 40), B(2 + h, 0, 320), 1.0, -127 * ONE, "v")
            lin(words("pk", j, h, 40, 48), B(2 + h, 320, 384), 1.0, -127.0, "v")

    iota(R("zr"), [[0, 2048]], 0, 0, [R("xf")])
    ts(R("bow"), R("rb"), gp, ALU.is_equal, 1024.0, ALU.mult)
    ts(R("tie"), R("ri", 0, 4), 1.0 / 256, ALU.mult, -1.5 / 256, ALU.add)
    ts(R("i16"), R("ri", 24, 40), 16.0, ALU.mult, pm, ALU.add)
    iota(R("xo"), [[16, 256]], HT, 1, [R("xf")])
    ts(R("pt", 32, 64), R("pt", 0, 32), 15, ALU.bitwise_and)
    ts(R("em"), R("rm", 0, 16), pm, ALU.is_equal)
    cp(R("ph"), R("pt", 32, 64))

    def spare(t):
        if t == 0:
            ts(R("pt", 64, 96), R("pt", 0, 32), 4, ALU.arith_shift_right)
            cp(R("pl"), R("pt", 64, 96))
            ts(R("bon", 0, 128), R("rg"), g16, ALU.is_equal, -512.0, ALU.mult)
            ts(R("bon", 128, 256), R("rg"), gup, ALU.is_equal, -512.0, ALU.mult)
            ms(R("dd", 256, 272), NONE)
        if t == 1:
            ts(R("ce", 13, 15), R("ri", 0, 32, 16), me, ALU.add, g16, ALU.add)
            for j in range(2):
                ts(R("fsl", 256 * j, 256 * j + 256), R("ri"), C("ce", 13 + j), ALU.is_equal)
            ts(R("hn"), R("rm", 0, 128), me, ALU.is_equal, -2.0 ** 60, ALU.mult)

    lin(R("nid"), R("idf"), -1.0)

    def turn(bank, marks):
        group([(B(bank, 0, 256), R(nm, c + j, c + 256, 2), R("fsl", 256 * j, 256 * j + 256)) for nm, c in marks for j in range(2)])

    tab = R("tab", 0, HT)

    def shifted(bank, ds, k0, qs):
        for d in ds:
            lin(R("ndb", 128 * d, 128 * d + 128), R("mo"), C("qf", 8 + d), -127.0, qs)
        for u in range(2):
            for e, d in enumerate(ds):
                a = k0 + 512 * u + 256 * e
                ts(R("kk", a, a + 256), U(u, 0, 256), 2.0 ** -12, ALU.mult,
                   B(7, 4 * u + d, 4 * u + d + 1) if t and not k0 else C("qf", 4 * u + d), ALU.add)
            group([(B(bank + u), R("cid"), R("elv"))]
                  + [(B(bank + u, 256 * e, 256 * e + 256), R("idh"), U(u, 0, 256)) for e in range(2)], stop=False)
            group([(B(bank + u, 128 * e, 128 * e + 128), R("wb", 128 * u, 128 * u + 128), R("ndb", 128 * ds[e // 2], 128 * ds[e // 2] + 128))
                   for e in range(4)]
                  + [(B(bank + u), R("m4k"), R("kk", k0 + 512 * u, k0 + 512 * u + 512))], start=False)

    def placed(bank, a, w, o, out="ix", qs="va"):
        lin(R("pa1", o, o + w), B(bank, a, a + w), 1.0, 0.0, qs)
        tt(R("wk", 2 * o, 2 * o + w), R("pa1", o, o + w), B(bank + 1, a, a + w), ALU.mult)
        ts(R("wk", 2 * o + w, 2 * o + 2 * w), R("wk", 2 * o, 2 * o + w), 5, ALU.arith_shift_right, H - 1, ALU.bitwise_and)
        tt(R("wk", 2 * o, 2 * o + w), R("wk", 2 * o + w, 2 * o + 2 * w), B(bank + 1, a, a + w), ALU.add)
        cp(R(out, o, o + w), R("wk", 2 * o, 2 * o + w))

    ring = {"ga": 0, "ps": 0, "na": 0}
    checked = []

    def take(name, size):
        a = ring[name] % size
        ring[name] = a + 1
        return a

    def look(offs, c0, bias, shift, lo, bank, first, banks, who, check, at=0):
        a, o = 2048 * take("ga", NG // 2), take("na", NN)
        js = (banks[take("ps", len(banks))], banks[take("ps", len(banks))])
        cut, check = who[(c0 + lo) // 128], check[(c0 + lo) // 64:]
        for q, i, e in (("a", 0, cut), ("v", cut, 128)):
            by = R(offs, c0 + lo + i, c0 + lo + e)
            if q == "v" and (offs == "ixr" or t == 0):
                by = (by[0], R(offs)[1] + [("pk", 0, 4), ("us", 0, 512)]) + by[2:]
            lin(R("ga", a + 16 * i, a + 16 * e), ind(tab, by), 1.0, bias, q, checked[-LAG] if q == "v" and len(checked) >= LAG else ())
        packed = pack(js, "ga", a, shift, [words("pk", lo // 128, h) if check[h] == "a" else None for h in range(2)])
        checked.append([tt(words("na", o, h), B(js[h], 0, 384), words("pk", lo // 128, h), ALU.not_equal) if check[h] == "v"
                        else size(words("na", o, h), B(js[h], 0, 384)) for h in range(2)])
        out = B(bank, at + lo, at + lo + 128)
        return packed, lambda after: group(
            [(out, l, R(nm, c + lo, c + lo + 128)) for l, nm, c in first]
            + [(out, X("na", 2 * o, 2 * o + 2, T.na[:, 48 * o + 8 * w:48 * o + 8 * w + 8, :], 128), R("big")) for w in range(6)], after=after)

    for t in range(RO):
        last = t == RO - 1
        if t == 0:
            first = []
        else:
            c0 = 256 * (t - 1)
            for a, b in HALVES:
                ts(R("cov", c0 + a, c0 + b), R("xo", a, b), float(HT), ALU.is_lt)
            first = [(idn, "cov", c0)]
            tt(R("pg"), ind(R("cov", c0, c0 + 256), R("pl")), R("mk"), ALU.mult)
            group([(B(6, 0, 256), idn, R("kr"))], stop=False)
            group([(B(6, 0, 256), R("bon", 0, 128), R("pg", 0, 256)), (B(6, 0, 256), R("bon", 128, 256), R("pg", 256, 512))], start=False)
            red(C("nm", 0), B(6, 0, 256), ALU.max, True)
            ts(C("ko", 0), C("nm", 0), 0.0, ALU.min, 256.0, ALU.add)
            tt(R("dm"), ind(R("dd"), C("ko", 0)), R("m4"), ALU.mult)
        group([(B(7, 0, 12), R("idf"), R("kc"))], stop=False)
        group([(B(7, 4 * j, 4 * j + 4), l, R("dm", 0, 4)) for j, l in enumerate((R("we", 0, 128), R("we", 128, 256), R("eq")))], start=False)
        cp(R("qf", 0, 12), B(7, 0, 12))
        for hh in range(2):
            shifted(PB[hh], (2 * hh, 2 * hh + 1), 1024 * hh, EV[t])
        for hh in range(2):
            for a, w in (((0, 256), (256, 256)) if (t, hh) in SINGLY else ((0, 512),)):
                placed(PB[hh], a, w, 512 * hh + a, "ix", EV[t])
        ts(R("pa1", 0, 1024, 256), R("qf", 8, 12), -1.0, ALU.mult, -254.0, ALU.add)
        for u in range(2):
            ts(R("pa1", 1 + u, 1024, 256), R("qf", 4 * u, 4 * u + 4), -1.0, ALU.mult, 2 * KB, ALU.add)
        if last:
            turn(6, [("cov", 0), ("cov", 256)])
            lin(R("zf"), B(6, 0, 256))
        ring["ps"] = 0
        if t == 0:
            for h in range(2):
                turned(512 + 512 * h, 128, lambda j: B(7, 256 * j + 128 * h - 512, 256 * j + 128 * h - 384), (2, 3))
            centred(1, 0, 256, B(7))

        def fit(d):
            relu(R("ft", 256 * d, 256 * d + 256), B(6 + d % 2, 256 * (d // 2), 256 * (d // 2) + 256), -2.0, 1.0, C("cl", 4 * t + d))

        add = None
        for d in range(n):
            for lo, _ in HALVES:
                packed, later = look("ix", 256 * d, C("qf", 8 + d), 1, lo, 6 + d % 2, first, RING, FORTH[t], CHECK, 256 * (d // 2))
                if (d, lo) == (3, 128):
                    fit(1)
                if add:
                    add(packed)
                add = later
        fit(0)
        fit(2)
        group([(B(6, 0, 4), R("bow"), R("tie"))], stop=False)
        if t == 0:
            lin(R("xab", 0, 256), ind(R("xb"), R("po", 0, 16)), -1.0, 0.0, "a", packed)
            lin(R("xab", 256, 512), ind(R("xb"), R("po", 16, 32)), 1.0, 0.0, "a", packed)
            lin(R("mk"), ind(R("em"), R("ph")), 1.0, 0.0, "a", packed)
        behind[:] = checked[-1]
        spare(t)
        behind[:] = []
        add(())
        fit(3)
        for a, b in HALVES:
            for u in range(2):
                group([(B(2 - a // 64 + u, 0, b - a), R("cid"), R("elv", 0, b - a)), (B(2 - a // 64 + u, 0, b - a), R("idh"), U(2 + u, a, b))], stop=False)
        top, base = C("mx", t), C("mx", 4 + t)
        group([(B(6, 0, 4), R("bow"), R("cl", 4 * t, 4 * t + 4))], start=False)
        red(top, B(6, 0, 4), ALU.max)
        ts(base, top, ROUND, ALU.add, ROUND, ALU.subtract)
        ts(R("so"), R("i16"), base, ALU.subtract, top, ALU.add)
        cp(R("qw"), ind(R("pa1"), C("so", 0)))
        lin(R("ndb", 0, 128), R("mo"), C("qw", 0), -127.0, "a")
        for a, b in HALVES:
            w, bank = b - a, 2 - a // 64
            for u in range(2):
                ts(R("kk", 256 * u + a, 256 * u + b), U(2 + u, a, b), 2.0 ** -12, ALU.mult, C("qw", 1 + u), ALU.add)
                group([(B(bank + u, 0, w), R("wb", 128 * u, 128 * u + 128), R("ndb", 0, w)),
                       (B(bank + u, 0, w), R("m4k"), R("kk", 256 * u + a, 256 * u + b))], start=False)
            placed(bank, 0, w, a, "ixr", "a")
        now = (base[0], base[1] + R("pa1", 128, 256)[1]) + base[2:]
        relu(C("yt", 0), now, -1.0, 1.0)
        lin(C("yt", 1), now, 1.0 / 1024, 0.0, "a")
        lin(C("yt", 2), now, 1.0 / 256, 1.5, "a")
        lin(C("yt", 3), top, -1.0 / 256, C("yt", 2), "a")
        lin(C("yws", 8 * rank + t), C("yt", 0), -1.0, C("yt", 3), "a")
        lin(C("yws", 8 * rank + t + 3), C("yt", 0), -1.0, C("yt", 1), "a")
        if last:
            lin(R("fw"), ind(R("ft"), R("so")), 1.0, 0.0, "a")
            first = [(R("hn"), "fw", 0), (R("hn"), "cov", c0)]
            wins = R("yws", 8 * rank, 8 * rank + 6)
            lands([R("yws", 8 * r, 8 * r + 6) for r in others], "yw", ke * (n - 1),
                  send([(wins, off, "yw", [(T.cores[r], wins) for r in others])]))
        else:
            lin(R("fw"), ind(R("ft"), R("so")), -BIG, BIG, "a")
            first = [(R("idf"), "slp", 0)]
            if t == 0:
                group([(B(6, 0, 256), idn, R("xab", 0, 256)), (B(6, 0, 256), up2, R("xab", 256, 512))])
                lin(R("dd", 0, 256), B(6, 0, 256))
            group([(B(7, 0, 256), R("idf"), R("slp"))], stop=False)
            group([(B(7, 0, 256), idn, R("fw"))], start=False)
            tt(R("km"), B(7, 0, 256), R("xo"), ALU.min)
        ring["ps"] = 0
        for lo, _ in HALVES:
            look("ixr", 0, C("qw", 0), 2, lo, 4 + lo // 128, first, (2, 3, 0, 1), WHO[t], CHECKR[t])[1](())
        if not last:
            for a, b in HALVES:
                tt(R("xo", a, b), B(4 + a // 128, a, b), R("km", a, b), ALU.min)
                cp(R("ixo", a, b), R("xo", a, b))
                scatter(R("tab"), R("ixo", a, b), R("zr"))

    for a, b in HALVES:
        ts(R("y3", a, b), B(4 + a // 128, a, b), 0.5, ALU.is_lt, 3.0, ALU.mult)
    turn(6, [("y3", 0)])
    tt(R("yo"), B(6, 0, 256), R("zf"), ALU.subtract)
    lead[0] = True
    for js in ((0, 1), (2,)):
        back = send([(R("yo", 64 * others[j], 64 * others[j] + 64), masks[j], "yc%d" % rank,
                      [(T.cores[others[j]], R("yl", 64 * rank, 64 * rank + 64))]) for j in js])
    for r in range(n):
        dma("s", hbm(T.yw[2 * r:2 * r + 2, :]), X("yws", 8 * r, 8 * r + 6, T.yws[0:32:16, 8 * r:8 * r + 6], 6), "st", 192)
    for j, r in enumerate([rank] + others):
        if j:
            lands([R("yl", 64 * r, 64 * r + 64)], "yc%d" % r, count(masks[3 - j]), back)
        for h in range(2):
            dma("sa"[h], hbm(T.yc[2 * r + h:2 * r + h + 1, :]), R("yl" if j else "yo", 64 * r + 32 * h, 64 * r + 32 * h + 32), "st", 192)

    cnt = {"v": 0, "a": 0, "p": 0, "g": 0}
    seen = {k: {} for k in Q}
    log = {}

    def wait(q, sem, val):
        if seen[q].get(sem, 0) < val:
            Q[q].wait_ge(T.sem[sem], val)
            seen[q][sem] = val

    for i, q in arrange(calls):
        c = calls[i]
        if q != "x":
            need = {}
            for sem, val in meets(log, c["reads"], c["writes"], q):
                if not (q == "p" and sem == "cp"):
                    need[sem] = max(need.get(sem, 0), val)
            for sem, val in need.items():
                wait(q, sem, val)
            made = c["make"](q)
        if c["sem"] == "far":
            continue
        if c["sem"] is None:
            cnt[q] += 1
            tok = ("c" + q, cnt[q])
            made.then_inc(T.sem[tok[0]], 1)
        else:
            tok = c["sem"]
            if q != "x":
                made.then_inc(T.sem[tok[0]], 16)
        enter(log, c["reads"], c["writes"], tok, q)
    for q in cnt:
        wait("s", "c" + q, cnt[q])
    g.sync.wait_ge(T.sem.sent, sent[0])
    g.sync.wait_ge(T.sem.st, 192)
